import numpy as np, ml_dtypes
CORES = [2,3,42,43,82,83,122,123]
N = 8
BF = ml_dtypes.bfloat16
M, L, CAP, VI, ST = 3072, 256, 128, 4, 3
W = M + (VI - 1) * L
def weights(rng):
    w = rng.integers(0, 64, (N, 8, 16)); o = np.argsort(rng.random((N, 8, 16)), axis=-1)
    a = o[..., :1] == np.arange(16); b = o[..., 1:2] == np.arange(16)
    return np.where(a, 1, np.where(b, 16, w)), a[:, :, None], b[:, :, None]
def aim(v, w, a, b, t):
    v = np.where(a | b, 0, v); need = (t - np.sum(v * w[:, :, None], axis=-1)) & 63
    return v + a * (need & 15)[..., None] + b * (need >> 4)[..., None]
def shake(rng, v, k, top):
    return np.clip(v + np.floor((2 * k + 1) * rng.random(v.shape)).astype(np.int64) - k, 0, top)
def homes(rng, e):
    t = (64 * rng.random((N, 8, M)) ** e).astype(np.int64)
    t = (t * (2 * rng.integers(0, 32, (N, 8, 1)) + 1) + rng.integers(0, 64, (N, 8, 1))) & 63
    t[:, :, 1:65] = np.arange(64); return t
def points(rng, w, a, b, top):
    tree = homes(rng, rng.choice(np.array([1.0, 1.5, 2.0, 3.0]), (N, 8, 1)))
    mid = rng.integers(0, top + 1, (N, 8, 64, 16)); k = rng.integers(0, 9, (N, 8, M, 1)); k[:, :, 1:65] = 0
    v = shake(rng, np.take_along_axis(mid, tree[..., None], 2), k, top)
    far = rng.random((N, 8, M, 1)) < 0.3; far[:, :, 1:65] = False
    return tree, aim(np.where(far, rng.integers(0, top + 1, v.shape), v), w, a, b, tree)
def grow(v, tree):
    x = v.astype(np.int32); c = np.zeros(N * 8 * M * 16, np.int64)
    R, g, n = np.nonzero(np.broadcast_to(np.arange(M) > 64, (N, 8, M))); at = tree[R, g, n] + 1
    for _ in range(24):
        if len(n) == 0: break
        band = np.add.reduce(np.abs(x[R, g, n] - x[R, g, at]), axis=-1) >> 4
        key = ((R * 8 + g) * M + at) * 16 + band
        u, i = np.unique(key, return_index=True); c[u] = n[i]
        more = np.ones(len(n), bool); more[i] = False
        R, g, n, at = R[more], g[more], n[more], c[key[more]]
    return c.reshape(N, 8, M, 16)
def queries(rng, v, tree, w, a, b):
    o = rng.integers(1, M, (N, 8, VI * L)); k = rng.integers(0, 7, (N, 8, VI * L, 1))
    s = shake(rng, np.take_along_axis(v, o[..., None], 2), k, 15)
    s = np.where(rng.random((N, 8, VI * L, 1)) < 0.25, rng.integers(0, 16, s.shape), s)
    return aim(s, w, a, b, np.take_along_axis(tree, o, 2))
def radii(rng):
    z = (N, 8, VI * L)
    return np.where(rng.random(z) < 0.7, rng.integers(100, 256, z), rng.integers(0, 100, z))
def full(v):
    return np.ascontiguousarray(v.transpose(0, 1, 3, 2)).reshape(N, 128, -1)
def pack(v, c, s, w, r0, th):
    return {"pt": full(v).astype(np.float32).astype(BF), "ch": full(c).astype(np.int32), "q": full(s).astype(np.float32).astype(BF),
            "w": np.ascontiguousarray(w.reshape(N, 128, 1)).astype(np.int32), "r0": r0.astype(np.int32), "th": np.repeat(th, 16, axis=1)[..., None].astype(np.int32)}
def setup_inputs(rng):
    w, a, b = weights(rng); tree, v = points(rng, w, a, b, 15)
    return pack(v, grow(v, tree), queries(rng, v, tree, w, a, b), w, radii(rng), rng.integers(20, 60, (N, 8)))
def setup_inputs_room(rng):
    w, a, b = weights(rng); tree, v = points(rng, w, a, b, 10); z = (N, 8, VI * L)
    n = rng.choice(np.array([0, 1, CAP - 1, CAP, CAP + 1, L]), (N, 8)); n[0] = (CAP, CAP + 1, L, CAP - 1, 1, 0, CAP, CAP + 1); n[:, 2] = L
    n = np.concatenate([n[:, :, None], np.full((N, 8, VI - 1), L // 2)], axis=2)
    hot = (np.argsort(rng.random((N, 8, VI, L)), axis=-1) < n[..., None]).reshape(z)
    s = np.where(hot[..., None], rng.integers(12, 16, z + (16,)), queries(rng, v, tree, w, a, b))
    r0 = np.where(hot, rng.choice(np.array([20, 21, 255, 255, 255]), z), rng.integers(0, 20, z))
    return pack(v, grow(v, tree), s, w, r0, np.full((N, 8), 20))
def setup_inputs_knots(rng):
    w, a, b = weights(rng); v = rng.integers(0, 16, (N, 8, M, 16)); v[:, 1::2] = v[:, 1::2][:, :, rng.integers(0, 37, M)]
    dens = rng.choice(np.array([1.0, 0.6, 0.2]), (N, 8, 1, 1)); dens[:, 0] = 1.0; dens[:, 1] = 0.2; dens[:, 2] = 0.3
    c = np.where(rng.random((N, 8, M, 16)) < dens, rng.integers(1, M, (N, 8, M, 16)), 0)
    c[:, 3] = rng.choice(np.array([0, 1, 64, 65, M - 1]), (N, M, 16))
    c[:, 5] = np.where(rng.random((N, M, 16)) < 0.5, np.arange(M)[:, None], c[:, 5])
    x = rng.integers(1, M, (N, M, 2)); e = np.arange(16) - rng.integers(1, 6, (N, M, 1)); j = rng.choice(np.array([-1, 3, 4]), (N, M, 1))
    some = rng.random((N, M, 1)) < 0.4; some[:, 1:65] = True
    c[:, 6] = some * np.where((e >= 0) & (e < 3), x[:, :, :1], np.where(e == j, x[:, :, 1:], 0)); c[:, :, 0] = 0
    return pack(v, c, queries(rng, v, rng.integers(0, 64, (N, 8, M)), w, a, b), w, radii(rng), rng.integers(20, 80, (N, 8)))
def setup_inputs_ties(rng):
    w = rng.integers(0, 64, (N, 8, 16)); v = 4 * rng.integers(0, 4, (N, 8, M, 16)); tree = homes(rng, 1.0); z = (N, 8, VI * L)
    s = np.take_along_axis(v, rng.integers(1, M, z)[..., None], 2); s = np.where(rng.random(s.shape) < 0.3, 4 * rng.integers(0, 4, s.shape), s)
    s = np.where(rng.random(s.shape) < 0.01, 15, s); s[:, ::2, 1::2] = s[:, ::2, ::2]
    r0 = np.where(rng.random(z) < 0.4, 16 * rng.integers(3, 9, z) + rng.choice(np.array([-1, 1]), z), 4 * rng.integers(10, 40, z))
    return pack(v, grow(v, tree), s, w, r0, 4 * rng.integers(8, 15, (N, 8)))
def setup_inputs_ends(rng):
    w, a, b = weights(rng); tree, v = points(rng, w, a, b, 15); n = np.arange(L)
    v[:, 4, 65:65 + L] = rng.integers(0, 16, (N, L, 16)); tree[:, 4, 65:65 + L] = n & 63; v = aim(v, w, a, b, tree)
    s = queries(rng, v, tree, w, a, b); s[:, 4, :L] = v[:, 4, 65:65 + L]
    w[:, 1] = 0; w[:, 2] = 63; v[:, :, 1] = 0; v[:, :, 64] = 15; v[:, :, M - 1] = 15; v[:, 3, 1:65] = 0
    c = grow(v, tree); c[:, :, 1, 15] = M - 1; c[:, 3] = 0; c[:, 4, 65:] = 0; c[:, 4, 1 + (n & 63), 4 * (n >> 6) + 2] = 65 + n
    R = np.arange(N); z = 1 + ((15 * np.sum(w[:, 7], axis=-1)) & 63)
    v[R, 7, z] = 0; v[:, 7, 65] = 0; v[:, 7, 66] = 15
    c[R, 7, z] = 0; c[R, 7, z, 9] = 65; c[:, 7, 65] = 0; c[:, 7, 65, 4] = 66
    s[:, 1, ::3] = 15; s[:, 3, ::2] = 15; s[:, 3, 1::4] = rng.integers(14, 16, s[:, 3, 1::4].shape); s[:, 7, ::4] = 15
    s[:, :, 0] = 15; s[:, :, L - 1] = 0
    r0 = rng.choice(np.array([0, 1, 15, 16, 17, 120, 254, 255]), (N, 8, VI * L)); high = np.array([240, 241, 255])
    r0[:, 3, ::2] = rng.choice(high, r0[:, 3, ::2].shape); r0[:, 3, 1::4] = rng.choice(np.array([191, 192, 239, 240, 241, 255]), r0[:, 3, 1::4].shape)
    r0[:, 4, :L] = 255; r0[:, 7, ::4] = rng.choice(high, r0[:, 7, ::4].shape); r0[:, :, 0] = 255; r0[:, :, L - 1] = 255
    th = rng.choice(np.array([0, 1, 16, 30, 240]), (N, 8)); th[:, 0] = 0; th[:, 3] = np.array([0, 240, 241, 255])[R & 3]; th[:, 4] = 0; th[:, 5] = 255; th[:, 6] = 240
    return pack(v, c, s, w, r0, th)
def setup_inputs_spread(rng):
    w = rng.integers(0, 64, (N, 8, 16)); e = rng.choice(np.array([0.25, 0.5, 1.0, 2.0, 4.0]), (N, 8, 1, 16))
    v = (16 * rng.random((N, 8, M, 16)) ** e).astype(np.int64); s = (16 * rng.random((N, 8, VI * L, 16)) ** e).astype(np.int64)
    c = grow(v, homes(rng, 4.0)); c = np.where(rng.random(c.shape) < 0.1, rng.integers(0, M, c.shape), c); c[:, :, 0] = 0
    th = np.exp2(7 * rng.random((N, 8))).astype(np.int64); th[:, 0] = 8
    return pack(np.clip(v, 0, 15), c, np.clip(s, 0, 15), w, rng.integers(0, 256, (N, 8, VI * L)), th)
def check_inputs(d):
    bad = []
    for k in ("pt", "q"):
        x = np.asarray(d[k]).astype(np.float32)
        if not (np.all(x >= 0) and np.all(x <= 15) and np.all(x == np.floor(x))): bad.append("whole numbers from 0 to 15 in " + k)
    for k, hi in (("ch", M - 1), ("w", 63), ("r0", 255), ("th", 255)):
        if np.min(d[k]) < 0 or np.max(d[k]) > hi: bad.append("range of " + k)
    if np.any(np.asarray(d["ch"])[:, :, 0] != 0): bad.append("column 0 of ch")
    x = np.asarray(d["th"]).reshape(-1, 16)
    if np.any(x != x[:, :1]): bad.append("one threshold a group")
    return bad
def dist(u, v):
    return np.add.reduce(np.abs(u - v), axis=-1)
def inside(D, rho):
    i = np.arange(16); return (16 * i <= (D + rho)[..., None]) & (16 * i + 15 >= (D - rho)[..., None])
def at(k, i):
    return np.take_along_axis(k, i[..., None], -1)[..., 0]
def reference(pt, ch, q, w, r0, th):
    X = np.zeros((N, 8, W, 16), np.int32); X[:, :, :M] = pt.astype(np.float32).astype(np.int32).reshape(N, 8, 16, M).transpose(0, 1, 3, 2)
    C = np.zeros((N, 8, W, 16), np.int32); C[:, :, :M] = ch.reshape(N, 8, 16, M).transpose(0, 1, 3, 2)
    Q = np.ascontiguousarray(q.astype(np.float32).astype(np.int32).reshape(N, 8, 16, VI * L).transpose(0, 1, 3, 2))
    wt = w.astype(np.int32).reshape(N, 8, 1, 16); lim = th.reshape(N, 8, 16)[:, :, :1]
    a, b, ln = np.ogrid[0:N, 0:8, 0:L]; far_off = 1000
    yr, yb, yp, held = [], [], [], None
    for t in range(VI):
        v = np.array(Q[:, :, t * L:(t + 1) * L]); rho = np.array(r0[:, :, t * L:(t + 1) * L]).astype(np.int32); best = np.zeros((N, 8, L), np.int32)
        if held is not None:
            hv, hr, hb, sent, place = held; h = np.nonzero(sent); to = ((h[0] + 1) % N, h[1], place[h])
            v[to] = hv[h]; rho[to] = hr[h]; best[to] = hb[h]
        kid = np.zeros((N, 8, ST + 1, L, 16), np.int32); far = np.zeros((N, 8, ST + 1, L, 16), np.int32); own = np.zeros((N, 8, ST + 1, L), np.int32)
        lev = np.zeros((N, 8, L), np.int64); push = np.ones((N, 8, L), bool)
        m = 1 + (np.add.reduce(wt * v, axis=-1) & 63); D = dist(X[a, b, m], v)
        for s in range(ST + 1):
            if s > 0:
                k = kid[a, b, lev, ln]; f = far[a, b, lev, ln]; ok = (k > 0) & inside(own[a, b, lev, ln], rho)
                i = np.argmin(np.where(ok, f, far_off), axis=-1); push = np.any(ok, axis=-1)
                m = np.where(push, at(k, i), 0); D = np.where(push, at(f, i), far_off)
                h = np.nonzero(push); kid[h[0], h[1], lev[h], h[2], i[h]] = 0
                lev = np.where(push, lev + 1, np.maximum(lev - 1, 0))
            P = np.where(inside(D, rho) & push[..., None], C[a, b, m], 0)
            F = dist(X[a[..., None], b[..., None], P], v[:, :, :, None])
            h = np.nonzero(push); e = (h[0], h[1], lev[h], h[2])
            kid[e] = P[h]; far[e] = F[h]; own[e] = D[h]
            key = np.concatenate([D[..., None], np.where(P > 0, F, far_off)], axis=-1); node = np.concatenate([m[..., None], P], axis=-1)
            i = np.argmin(key, axis=-1); least = at(key, i); better = least < rho
            best = np.where(better, 4096 * a + at(node, i), best); rho = np.where(better, least, rho)
        yr.append(rho); yb.append(best)
        if t == VI - 1: break
        goes = rho >= lim; here = (best > 0) & (best >> 12 == a); node = np.where(here, best & 4095, 0); row = rho >> 4
        can = goes & here & (C[a, b, node, row] == 0)
        earlier = np.arange(L)[None, :] < np.arange(L)[:, None]
        win = can & ~np.any((node[:, :, :, None] == node[:, :, None, :]) & can[:, :, None, :] & earlier, axis=-1)
        X[:, :, M + t * L:M + (t + 1) * L] = v; h = np.nonzero(win); C[h[0], h[1], node[h], row[h]] = M + t * L + h[2]
        yp.append(np.where(win, node, 0))
        place = np.add.accumulate(goes.astype(np.int64), axis=2) - 1
        held = (v, rho, best, goes & (place < CAP), place)
    return {"yr": np.concatenate(yr, axis=2).astype(np.float32), "yb": np.concatenate(yb, axis=2).astype(np.float32), "yp": np.concatenate(yp, axis=2).astype(np.float32)}

@@ -1,0 +1,741 @@
+from concourse.mybir import AluOpType, AxisListType, ActivationFunctionType
+
+OP = AluOpType
+AF = ActivationFunctionType
+M0, LN, VI, W = 3072, 256, 4, 3840
+C0 = 491520
+BIG = 16777216
+FR = 1.0 / BIG
+TR = 256
+CHUNKS = ((32, "S"), (32, "V"), (32, "V"), (32, "V"))
+
+AR = {"af": ("float32", 15800), "ab": ("bfloat16", 35000), "ai": ("int32", 3600), "au": ("uint16", 1200)}
+SCRATCH = {k: ("sbuf", [128, n], d) for k, (d, n) in AR.items()}
+SCRATCH["ptab"] = ("sbuf", [128, W], "bfloat16")
+SCRATCH["ctab"] = ("sbuf", [128, TR + W], "float32")
+SCRATCH["cint"] = ("sbuf", [128, M0], "int32")
+SCRATCH["qsb"] = ("sbuf", [128, VI * LN], "bfloat16")
+for _h in range(2):
+    for _b in ("key", "dif", "msc", "lst"):
+        SCRATCH["%s%d" % (_b, _h)] = ("psum", [128, 512], "float32")
+NY = 40
+SEMAPHORES = ["sV", "sS", "sP", "sG"] + ["y%d" % k for k in range(NY)] + ["pq1", "pq2", "pq3", "pr1", "pr2", "pr3", "aq1", "aq2", "aq3", "ar1", "ar2", "ar3"] + ["l%d" % k for k in range(12)]
+CYC = 0.83
+GX = 1.55
+A_SPREAD = "G"
+LEAD = 0.0
+LOOK = 70.0
+LATER = 2500.0
+HOP = 90.0
+
+
+def rank_program(g, core, T, topo):
+    rank = T.rank_of(core)
+    if rank is None:
+        return
+    N = len(T.cores)
+    ops = []
+    acc = {}
+    fill = {k: 0 for k in AR}
+    names = {}
+    bonus = [0.0]
+    psum = {k for k in SCRATCH if SCRATCH[k][0] == "psum"}
+
+    def al(name, n, kind):
+        n2 = (n + 15) // 16 * 16
+        b = fill[kind]
+        fill[kind] = b + n2
+        if fill[kind] > AR[kind][1]:
+            raise ValueError("arena %s" % kind)
+        names[name] = (kind, b, n)
+        return name
+
+    def v(name, lo=0, hi=None, st=1, p=128):
+        if name in names:
+            k, b, n = names[name]
+        else:
+            k, b, n = name, 0, SCRATCH[name][1][1]
+        if hi is None:
+            hi = n
+        return (k, b + lo, b + hi, st, p)
+
+    def ap(x):
+        if len(x) == 2:
+            return ap(x[0]).indirect(ap(x[1]))
+        k, lo, hi, st, p = x
+        t = T[k]
+        if st == 1:
+            return t[0:p, lo:hi]
+        return t[0:p, lo:hi:st]
+
+    def width(x):
+        if len(x) == 2:
+            return 16 * (x[1][2] - x[1][1])
+        return len(range(x[1], x[2], x[3]))
+
+    def is2(x):
+        return len(x) == 5 and (x[0] in ("ab", "au", "ptab", "qsb"))
+
+    def overlap(a, b):
+        if a[1] >= b[2] or b[1] >= a[2]:
+            return False
+        if a[3] == b[3] and a[3] > 1 and (a[1] - b[1]) % a[3]:
+            return False
+        return True
+
+    def covers(a, b):
+        return (a[3] == 1 and a[1] <= b[1] and a[2] >= b[2]) or a[1:4] == b[1:4]
+
+    def add(eng, emit, reads, writes, busy, lat=0.0, sem=None, extra=()):
+        i = len(ops)
+        deps = {}
+
+        def dep(j, kind):
+            if j == i:
+                return
+            need = not (eng == "P" and ops[j]["eng"] == "P")
+            deps[j] = deps.get(j, False) or need
+        flat = []
+        for x in reads:
+            flat += list(x) if len(x) == 2 else [x]
+        wr = []
+        for x in writes:
+            if len(x) == 2:
+                wr.append(x[0])
+                flat.append(x[1])
+            else:
+                wr.append(x)
+
+        def norm(x):
+            return (x[0], 0, 512, 1, 128) if x[0] in psum else x
+        flat = [norm(x) for x in flat]
+        wr = [norm(x) for x in wr]
+        for x in flat:
+            for (j, y, w) in acc.get(x[0], []):
+                if w and overlap(x, y):
+                    dep(j, "RAW")
+                elif not w and x[0] in psum and ops[j]["eng"] != eng:
+                    dep(j, "RR")
+        for x in wr:
+            for (j, y, w) in acc.get(x[0], []):
+                if overlap(x, y):
+                    dep(j, "WAW" if w else "WAR")
+        for x in flat:
+            acc.setdefault(x[0], []).append((i, x, False))
+        for x in wr:
+            acc[x[0]] = [e for e in acc.get(x[0], []) if e[0] == i or not covers(x, e[1])]
+            acc[x[0]].append((i, x, True))
+        ops.append({"eng": eng, "emit": emit, "deps": deps, "busy": busy, "lat": lat, "sem": sem, "tdeps": list(extra), "bonus": bonus[0]})
+        return i
+
+    def vdur(out, ins, two=False):
+        n = width(out)
+        for x in ins:
+            if len(x) == 2:
+                return 50 + GX * CYC * n
+        if len(out) == 2:
+            return 50 + 3.5 * CYC * width(out)
+        c = 1.0
+        if two and all(x[0] not in psum for x in ins):
+            c = 2.0
+        elif not two and is2(out) and all(is2(x) for x in ins):
+            c = 0.5
+        return 25 + CYC * max(64, c * n)
+
+    def cp(out, a):
+        add("V", lambda: g.vector.tensor_copy(ap(out), ap(a)), [a], [out], vdur(out, [a]))
+
+    def tt(out, a, b, op):
+        add("V", lambda: g.vector.tensor_tensor(ap(out), ap(a), ap(b), op), [a, b], [out], vdur(out, [a, b], True))
+
+    def ts(out, a, s1, op0, s2=None, op1=None):
+        rd = [a] + ([s1] if isinstance(s1, tuple) else [])
+
+        def emit():
+            s = ap(s1) if isinstance(s1, tuple) else s1
+            if op1 is None:
+                return g.vector.tensor_scalar(ap(out), ap(a), s, None, op0)
+            return g.vector.tensor_scalar(ap(out), ap(a), s, s2, op0, op1)
+        add("V", emit, rd, [out], vdur(out, [a]))
+
+    def scan(out, d0, d1, init, op0, op1):
+        add("V", lambda: g.vector.tensor_tensor_scan(ap(out), ap(d0), ap(d1), init, op0, op1), [d0, d1], [out], 25 + CYC * width(out))
+
+    def red(out, a):
+        add("V", lambda: g.vector.tensor_reduce(ap(out), ap(a), axis=AxisListType.X, op=OP.min, apply_absolute_value=True), [a], [out], 25 + CYC * width(a))
+
+    def ms(out, c):
+        add("V", lambda: g.vector.memset(ap(out), c), [], [out], 25 + CYC * max(64, width(out) * (0.5 if is2(out) else 1)))
+
+    def act(out, a, func, bias=None, scale=None, accum=None):
+        rd = [a] + ([bias] if isinstance(bias, tuple) else [])
+
+        def emit():
+            kw = {}
+            if bias is not None:
+                kw["bias"] = ap(bias) if isinstance(bias, tuple) else bias
+            if scale is not None:
+                kw["scale"] = scale
+            if accum is not None:
+                kw["accum_out"] = ap(accum)
+            return g.scalar.activation(ap(out), ap(a), func, **kw)
+        d = 65 + CYC * width(out) * (GX if len(a) == 2 else 1)
+        add("S", emit, rd, [out] + ([] if accum is None else [accum]), d + (0 if accum is None else 25))
+
+    def mm(out, parts, start=True, stop=True, outs=None):
+        n = len(parts)
+        dur = 0.0
+        rd = []
+        for (a, b) in parts:
+            rd += [a, b]
+            f = 4 if a[0] == "af" else 1
+            dur += 0.72 * f * max(min(64, width(a)), width(b))
+
+        def emit():
+            ins = None
+            for k, (a, b) in enumerate(parts):
+                o = out if outs is None else outs[k]
+                ins = g.tensor.matmul(ap(o), ap(a), ap(b), start and k == 0, stop and k == n - 1)
+            return ins
+        add("P", emit, rd, [out], dur + 30)
+
+    def iota(out, pat, base, cm, fl=False):
+        add("G", lambda: g.iota(ap(out), pat, base, cm, allow_small_or_imprecise_dtypes=True) if fl else g.iota(ap(out), pat, base, cm), [], [out], 130 + 2 * CYC * width(out))
+
+    def asel(out, a, pat, cop, fillv, base, cm):
+        add("G", lambda: g.affine_select(ap(out), ap(a), pat, cop, fillv, base, cm), [a], [out], 170 + 2 * CYC * width(out))
+
+    ysem = [0]
+
+    def dma(out_fn, in_fn, reads, writes, lat):
+        s = "y%d" % ysem[0]
+        ysem[0] += 1
+        return add("Y", lambda: g.sync.dma_start(out_fn(), in_fn()), reads, writes, 60.0, lat, (s, 16))
+
+    lsem = [0]
+    right, left = T.cores[(rank + 1) % N], T.cores[(rank - 1) % N]
+
+    def engs(a, b):
+        return topo.engines(a, b)[:8]
+
+    def send(out, a, dst, rsem):
+        s = "l%d" % lsem[0]
+        lsem[0] += 1
+        es = engs(core, dst)
+        mk = sum(1 << e for e in es)
+        rid, pid = topo.addr(dst)[:2]
+        return add("G", lambda: (g.remote_dma(ap(out), ap(a), T.sem[rsem], T.sem[s], pid, rid, mk), None)[1], [a], [], 900.0, 0.0, (s, len(es)))
+
+    def arrive(out, src, rsem, after, lat):
+        n = len(engs(src, core))
+        return add("R", None, [], [out], 0.0, lat, (rsem, n), [after])
+
+    F, B, I, U = "af", "ab", "ai", "au"
+    al("wi", 1, I)
+    al("thi", 1, I)
+    al("r0i", 1024, I)
+    dma(lambda: ap(v("wi")), lambda: T.w[:], [], [v("wi")], 2000)
+    dma(lambda: ap(v("qsb")), lambda: T.q[:], [], [v("qsb")], 3000)
+    dma(lambda: ap(v("r0i", p=8)), lambda: T.r0[:], [], [v("r0i")], 3200)
+    dma(lambda: ap(v("thi")), lambda: T.th[:], [], [v("thi")], 3300)
+    dma(lambda: ap(v("ptab", 0, M0)), lambda: T.pt[:], [], [v("ptab", 0, M0)], 5500)
+    for k in range(3):
+        dma(lambda k=k: ap(v("cint", 1024 * k, 1024 * k + 1024)), lambda k=k: T.ch[:, 1024 * k:1024 * k + 1024], [], [v("cint", 1024 * k, 1024 * k + 1024)], 7000 + 1500 * k)
+    ms(v("ptab", M0, W), 0.0)
+    ms(v("ctab", TR + M0, TR + W), 0.0)
+
+    for nm, n, k in [("onesb", 128, B), ("onesf", 128, F), ("Ib", 128, B), ("If", 128, F), ("nI", 128, B), ("tri", 128, B),
+                     ("TriD", 128, B), ("t8k", 128, B), ("tri8", 128, B), ("dgl", 128, B), ("Blk", 128, B), ("maskL", 128, F), ("rhsC", 8, F), ("BS", 8, B),
+                     ("iT", 128, F), ("addR", 128, F), ("mulR", 128, F), ("maxR", 128, F), ("trs", 16, F), ("trw", 16, F), ("zk", 128, B), ("zk0", 128, F), ("zk1", 128, F),
+                     ("RS", 8, F), ("RB1", 8, F), ("RTb", 8, B), ("sel", 128, F), ("rowc", 1, F), ("pf", 1, F), ("wf", 1, F), ("thf", 1, F), ("thr", 128, B),
+                     ("thv", 8, F), ("WS", 8, B), ("WB", 143, B), ("r0f", 1024, F), ("r0row", 1024, F), ("selg", 2048, B), ("nsel", 1024, B),
+                     ("i1", 128, I), ("i2", 128, I), ("i3", 8, I), ("i4", 8, I), ("i5", 128, I), ("i6", 128, I), ("i8", 1, I), ("i9", 1, I),
+                     ("zs", 2048, B), ("sg1", 2048, B), ("ns1", 1024, B), ("ic", 128, I), ("id", 128, F), ("il", 80, I), ("lists", 80, U)]:
+        al(nm, n, k)
+    for t in range(3):
+        for h in range(2):
+            al("Ik%d%d" % (t, h), 128, B)
+    ms(v("onesb"), 1.0)
+    ms(v("onesf"), 1.0)
+    asel(v("If"), v("onesf"), [[-1, 128]], OP.is_equal, 0.0, 0, 1)
+    cp(v("Ib"), v("If"))
+    ts(v("nI"), v("Ib"), -1.0, OP.mult)
+    cp(v("wf"), v("wi"))
+    iota(v("i3"), [[-16, 8]], 0, 1)
+    ts(v("i4"), v("i3"), 4, OP.arith_shift_right)
+    ts(v("rhsC"), v("i4"), 0.0, OP.is_equal)
+    ts(v("WS"), v("rhsC"), v("wf"), OP.mult)
+    ms(v("WB"), 0.0)
+    cp(v("WB", 15, 128, 16), v("WS"))
+    ts(v("BS"), v("rhsC"), 1.0 / 256, OP.mult)
+    ts(v("RS"), v("i3"), 0.0, OP.is_equal, 1.0 / 256, OP.mult)
+    ts(v("RTb"), v("i3"), 0.0, OP.is_equal)
+    ts(v("RB1"), v("i3"), 1.0, OP.is_equal)
+    iota(v("il", 0, 8), [[1, 8]], 0, 0)
+    iota(v("il", 8, 16), [[16, 8]], 15, 0)
+    for k in range(6):
+        iota(v("il", 16 + 8 * k, 24 + 8 * k), [[7, 8]], 1 + k, 0)
+    cp(v("lists", 0, 64), v("il", 0, 64))
+
+    def lst(k):
+        return v("lists", 8 * k, 8 * k + 8)
+    iota(v("i1"), [[-1, 128]], 256, 1)
+    ts(v("i2"), v("i1"), 15, OP.bitwise_and)
+    ts(v("maskL"), v("i2"), 0.0, OP.is_equal)
+    iota(v("i5"), [[-16, 8], [0, 16]], 0, 1)
+    ts(v("i6"), v("i5"), 4, OP.arith_shift_right)
+    ts(v("Blk"), v("i6"), 0.0, OP.is_equal)
+    iota(v("iT"), [[0, 8], [1, 16]], 0, 0, True)
+    ts(v("addR"), v("iT"), 0.0, OP.is_equal, 4.0, OP.mult)
+    ts(v("maxR"), v("iT"), 0.0, OP.is_equal)
+    ts(v("mulR"), v("iT"), 0.0, OP.is_gt)
+    ts(v("zk0"), v("iT"), -16.0, OP.mult)
+    asel(v("zk1", p=2), v("zk0", p=2), [[0, 128]], OP.is_ge, -7.5, 0, -1)
+    cp(v("zk", p=2), v("zk1", p=2))
+    iota(v("i8"), [[0, 1]], 0, 1)
+    cp(v("pf"), v("i8"))
+    ts(v("i9"), v("i8"), 15, OP.bitwise_and)
+    ts(v("rowc"), v("i9"), 4096.0 * FR, OP.mult, C0 * FR, OP.add)
+    iota(v("ic", p=16), [[1, 128]], 0, -16)
+    ts(v("sel", p=16), v("ic", p=16), 0.0, OP.is_equal)
+    ts(v("id", p=16), v("ic", p=16), -127.0, OP.is_equal)
+    tt(v("sel", p=16), v("sel", p=16), v("id", p=16), OP.add)
+    cp(v("r0f", p=8), v("r0i", p=8))
+    for k in range(2):
+        mm(v("dif%d" % k), [(v("sel", p=8), v("r0f", 512 * k, 512 * k + 512, p=8))])
+        act(v("r0row", 512 * k, 512 * k + 512), v("dif%d" % k), AF.Copy)
+    for t in range(1, 4):
+        al("hq%d" % t, 512, B)
+        al("hr%d" % t, 512, F)
+        al("lq%d" % t, 128, B)
+        al("lr%d" % t, 128, F)
+    for t in range(1, 4):
+        j = send(v("hq%d" % t, 0, 128), v("qsb", 256 * t, 256 * t + 128), left, "pq%d" % t)
+        arrive(v("hq%d" % t, 0, 128), right, "pq%d" % t, j, 6000.0)
+        j = send(v("hr%d" % t, 0, 128), v("r0row", 256 * t, 256 * t + 128), left, "pr%d" % t)
+        arrive(v("hr%d" % t, 0, 128), right, "pr%d" % t, j, 6000.0)
+    ms(v("ptab", 0, 1), 31.0)
+    for k in range(3):
+        cp(v("ctab", TR + 1024 * k, TR + 1024 * k + 1024), v("cint", 1024 * k, 1024 * k + 1024))
+    asel(v("tri"), v("onesb"), [[1, 128]], OP.is_gt, 0.0, 0, -1)
+    ts(v("TriD"), v("Ib"), -1024.0, OP.mult)
+    tt(v("TriD"), v("TriD"), v("tri"), OP.add)
+    ms(v("t8k"), 8192.0)
+    asel(v("tri8"), v("t8k"), [[1, 128]], OP.is_ge, 0.0, 0, -1)
+    ts(v("dgl"), v("Ib"), v("pf"), OP.mult)
+    for t in range(3):
+        for h in range(2):
+            ts(v("Ik%d%d" % (t, h)), v("Ib"), float(M0 + 256 * t + 128 * h), OP.mult)
+    iota(v("trs"), [[128, 2], [0, 8]], 256 - 1024, 1, True)
+    iota(v("trw"), [[128, 2], [0, 8]], 0, 1, True)
+    cp(v("thf"), v("thi"))
+    ts(v("thr"), v("onesf"), v("thf"), OP.mult)
+    mm(v("lst0", 0, 8), [(v("thr"), v("RTb"))])
+    ts(v("thv"), v("lst0", 0, 8), 1.0 / 256, OP.mult, C0 * FR, OP.add)
+    ms(v("zs", p=16), 0.0)
+    asel(v("sg1", p=16), v("zs", p=16), [[-1, 8], [0, 256]], OP.not_equal, 1.0, 0, 1)
+    asel(v("selg", p=16), v("sg1", p=16), [[-1, 8], [0, 256]], OP.not_equal, 1.0, -8, 1)
+    asel(v("ns1", p=16), v("zs", 0, 1024, p=16), [[-1, 8], [0, 128]], OP.not_equal, -1.0, 0, 1)
+    asel(v("nsel", p=16), v("ns1", p=16), [[-1, 8], [0, 128]], OP.not_equal, -1.0, -8, 1)
+
+    for h in range(2):
+        for nm, n, k in [("P16", 128, U), ("mo", 8, U), ("kS", 128, F), ("gm", 128, B), ("adm", 128, B), ("pen", 128, B), ("df", 2048, B),
+                         ("ad", 2048, B), ("sc1", 128, F), ("ins", 128, B), ("t1", 8, I), ("mI", 8, I), ("E", 128, F), ("li", 8, I), ("li2", 8, I),
+                         ("rm", 8, I), ("rm2", 8, I), ("rm3", 8, F), ("kd", 8, F), ("bi", 8, F), ("np2", 8, F), ("sl0", 8, F), ("sel3", 8, F),
+                         ("a3", 128, B), ("b3", 128, B), ("s3", 128, F),
+                         ("tI", 56, I), ("H", 56, I), ("L", 56, I), ("upd", 56, F), ("nu", 56, F), ("pk", 56, F), ("nsc", 56, F), ("O", 16, F), ("Og", 128, F),
+                         ("nz", 8, F), ("bz", 8, F), ("bb", 8, F), ("cd", 8, F), ("slt", 8, F), ("sl16", 8, U), ("rbs", 128, F), ("bI", 56, I), ("oh", 128, B),
+                         ("nb16", 8, U), ("Kb", 128, F), ("pr", 128, F), ("osc", 128, F), ("vals", 128, F), ("nF", 8, I), ("dgi", 16, I), ("z", 8, F), ("nc", 8, F),
+                         ("DG", 16, B), ("dm", 8, F), ("sq0", 256, F), ("sq1", 256, F), ("sq2", 256, F), ("sq3", 256, F), ("sr", 256, B),
+                         ("nd", 8, F), ("wn", 8, F), ("wg", 128, F), ("z2", 8, F), ("ncs", 8, F), ("z3", 8, F), ("off", 8, F), ("of16", 8, U)]:
+            al(nm + str(h), n, k)
+        for s in range(4):
+            al("As%d%d" % (s, h), 128, F)
+        for s in range(3):
+            al("v2%d%d" % (s, h), 128, F)
+            al("sc2%d%d" % (s, h), 128, F)
+        for k in range(2):
+            al("NB%d%d" % (k, h), 56, F)
+            ms(v("NB%d%d" % (k, h)), 1.5)
+        ms(v("nsc%d" % h), 0.0)
+    al("FAR", 16, B)
+    al("Ud", 256, B)
+    al("q16a", 2048, B)
+    for t in range(4):
+        al("q16b%d" % t, 2048, B)
+
+    def qv(t, h):
+        if h == 0 and t > 0:
+            return ("lq%d" % t, 0)
+        return ("qsb", 256 * t + 128 * h)
+
+    def q16(t, h):
+        return "q16a" if h == 0 else "q16b%d" % t
+
+    def spread(t, h, how):
+        nm, o = qv(t, h)
+        for i in range(16):
+            out, a = v(q16(t, h), i, 2048, 16), v(nm, o, o + 128)
+            if how == "G":
+                asel(out, a, [[0, 128]], OP.is_ge, 0.0, 1, 0)
+            elif how == "V" or i % 3 < 2:
+                cp(out, a)
+            else:
+                act(out, a, AF.Copy)
+
+    def tolist(h, win, offs, dst, plus=None):
+        E = v("E%d" % h)
+        tt(E, (win, offs), v("maskL"), OP.mult)
+        o = v("lst%d" % h, 0, 8)
+        mm(o, [(E, v("rhsC"))])
+        if plus is None:
+            cp(dst, o)
+        else:
+            ts(dst, o, float(plus), OP.add)
+
+    def begin(t, h):
+        nm, o = qv(t, h)
+        hs = str(h)
+        NB = "NB%d%d" % (t % 2, h)
+        if t < 3:
+            act(v("ptab", M0 + 256 * t + 128 * h, M0 + 256 * t + 128 * h + 128), v(nm, o, o + 128), AF.Copy)
+        l8 = v("lst" + hs, 0, 8)
+        mm(l8, [(v("WB", 15 - l, 143 - l), v(nm, o + l, o + 128, 16)) for l in range(16)])
+        cp(v("li" + hs), l8)
+        ts(v("li2" + hs), v("li" + hs), 63, OP.bitwise_and)
+        ts(v("mo" + hs), v("li2" + hs), 1.0, OP.add)
+        m8 = v("msc" + hs, 0, 8)
+        mm(m8, [(v(nm, o, o + 128), v("WS"))])
+        cp(v("rm" + hs), m8)
+        ts(v("rm2" + hs), v("rm" + hs), 63, OP.bitwise_and)
+        ts(v("rm3" + hs), v("rm2" + hs), FR, OP.mult, (1 + C0) * FR, OP.add)
+        if h == 0 and t > 0:
+            rv = v("lr%d" % t)
+        else:
+            rv = v("r0row", 256 * t + 128 * h, 256 * t + 128 * h + 128)
+        mm(m8, [(rv, v("RS"))])
+        ts(v(NB, 1, 56, 7), m8, C0 * FR, OP.add)
+        if h == 0 and t > 0:
+            mm(m8, [(rv, v("RB1"))])
+            cp(v("bi" + hs), m8)
+
+    def push(t, h, s):
+        hs = str(h)
+        NB = "NB%d%d" % (t % 2, h)
+        nm, o = qv(t, h)
+        W1 = M0 + 256 * t
+        mo = v("mo" + hs)
+        ch, pt = v("ctab", TR, TR + W1), v("ptab", 0, W1)
+        key = v("key" + hs, 0, 128)
+        cp(v("P16" + hs), (ch, mo))
+        act(v("gm" + hs), (pt, mo), AF.Copy)
+        mz = v("msc" + hs, 0, 128)
+        mm(mz, [(v("Ib"), v("gm" + hs)), (v("nI"), v(nm, o, o + 128))])
+        act(v("adm" + hs), mz, AF.Abs)
+        act(v("kS" + hs), (ch, mo), AF.Identity, bias=v("rowc"), scale=FR)
+        As = v("As%d%d" % (s, h))
+        if s == 0:
+            m2 = v("msc" + hs, 256, 264)
+            mm(m2, [(v("adm" + hs), v("BS"))])
+            tt(v("kd" + hs), m2, v("rm3" + hs), OP.add)
+            tt(v(NB, 2, 56, 7), v("kd" + hs), v(NB, 1, 56, 7), OP.min)
+        m3 = v("msc" + hs, 128, 256)
+        mm(m3, [(v("adm" + hs), v("Blk")), (v("onesb", p=2), v("zk", p=2))])
+        act(As, m3, AF.Abs, scale=1.0 / 256)
+        prev = 1 if s == 0 else s + 2
+        tt(v("pen" + hs), (v(NB), lst(1 + prev)), As, OP.is_lt)
+        mm(key, [(v("kS" + hs), v("If")), (v("Ib"), v("pen" + hs))], True, False)
+        l0 = 0
+        save = bonus[0]
+        for n_l, who in CHUNKS:
+            P = v("P16" + hs, l0, l0 + n_l)
+            a, b = 16 * l0, 16 * (l0 + n_l)
+            l0 += n_l
+            df, ad, qq = v("df" + hs, a, b), v("ad" + hs, a, b), v(q16(t, h), a, b)
+            bonus[0] = save - LATER
+            if who == "S":
+                act(df, (pt, P), AF.Copy)
+                d = v("dif" + hs, 0, b - a)
+                mm(d, [(v("Ib"), df), (v("nI"), qq)])
+                act(ad, d, AF.Abs)
+            else:
+                tt(df, (pt, P), qq, OP.subtract)
+                act(ad, df, AF.Abs)
+        bonus[0] = save
+        mm(key, [(v("ad" + hs, i, 2048, 16), v("BS")) for i in range(16)], False, True, [v("key" + hs, i, 128, 16) for i in range(16)])
+        sc1 = "sc1" + hs
+        scan(v(sc1), v("addR"), key, 4.0, OP.add, OP.min)
+        k15 = v(sc1, 15, 128, 16)
+        if s < 3:
+            v2, sc2 = v("v2%d%d" % (s, h)), "sc2%d%d" % (s, h)
+            if s == 0:
+                tt(v(NB, 3, 56, 7), v(NB, 2, 56, 7), k15, OP.min)
+                tt(v("ins" + hs), (v(NB), lst(4)), As, OP.is_lt)
+            else:
+                tt(v("ins" + hs), (v(sc1), lst(1)), As, OP.is_lt)
+            tt(v2, key, v("ins" + hs), OP.max)
+            scan(v(sc2), v("maxR"), v2, 1.0, OP.max, OP.min)
+            src = v(sc2, 15, 128, 16)
+            if s == 2:
+                tt(v("sel3" + hs), src, v("sl0" + hs), OP.min)
+                src = v("sel3" + hs)
+            ts(v("t1" + hs), src, float(BIG), OP.mult, -float(C0), OP.add)
+            ts(v("mI" + hs), v("t1" + hs), 4095, OP.bitwise_and)
+            tolist(h, v("mI" + hs), lst(0), mo)
+        if s > 0:
+            tt(v(NB, s + 3, 56, 7), v(NB, s + 2, 56, 7), k15, OP.min)
+        if s == 1:
+            v20, s20 = v("v20" + hs), v("sc20" + hs)
+            tt(v("a3" + hs), (s20, lst(1)), v20, OP.is_ge)
+            tt(v("b3" + hs), (v(NB), lst(5)), v("As0" + hs), OP.is_lt)
+            m4 = v("msc" + hs, 384, 512)
+            mm(m4, [(v("If"), v20), (v("Ib"), v("a3" + hs)), (v("Ib"), v("b3" + hs))])
+            scan(v("s3" + hs), v("maxR"), m4, 1.0, OP.max, OP.min)
+            ts(v("np2" + hs), v("sc21" + hs, 15, 128, 16), 1.0, OP.is_lt)
+            tt(v("sl0" + hs), v("np2" + hs), v("s3" + hs, 15, 128, 16), OP.max)
+
+    def finish(t, h):
+        hs = str(h)
+        NB = "NB%d%d" % (t % 2, h)
+        if t < 3:
+            tt(v("FAR", 8 * h, 8 * h + 8), v(NB, 6, 56, 7), v("thv"), OP.is_ge)
+        ts(v("tI" + hs), v(NB), float(BIG), OP.mult, -float(C0), OP.add)
+        ts(v("H" + hs), v("tI" + hs), 16, OP.arith_shift_right)
+        ts(v("L" + hs), v("tI" + hs), 4095, OP.bitwise_and)
+        tt(v("upd" + hs, 1, 56), v("H" + hs, 1, 56), v("H" + hs, 0, 55), OP.is_lt)
+        tt(v("nu" + hs, 1, 56), v("H" + hs, 1, 56), v("H" + hs, 0, 55), OP.is_ge)
+        tt(v("pk" + hs, 1, 56), v("upd" + hs, 1, 56), v("L" + hs, 1, 56), OP.mult)
+        scan(v("nsc" + hs, 1, 56), v("nu" + hs, 1, 56), v("pk" + hs, 1, 56), 0.0, OP.mult, OP.add)
+
+    def node(h):
+        return v("nsc%d" % h, 6, 56, 7)
+
+    def codes(t, h):
+        hs = str(h)
+        cp(v("O" + hs, 0, 8), v("H" + hs, 6, 56, 7))
+        ts(v("nz" + hs), node(h), 0.0, OP.is_gt, float(4096 * rank), OP.mult)
+        if h == 0 and t > 0:
+            tt(v("cd" + hs), node(h), v("nz" + hs), OP.add)
+            ts(v("bz" + hs), node(h), 0.0, OP.is_equal)
+            tt(v("bb" + hs), v("bz" + hs), v("bi" + hs), OP.mult)
+            tt(v("O" + hs, 8, 16), v("cd" + hs), v("bb" + hs), OP.add)
+        else:
+            tt(v("O" + hs, 8, 16), node(h), v("nz" + hs), OP.add)
+        mm(v("lst" + hs, 0, 128, p=16), [(v("O" + hs), v("If"))])
+        act(v("Og" + hs, p=16), v("lst" + hs, 0, 128, p=16), AF.Copy)
+        k, b, n = names["Og" + hs]
+        c = 256 * t + 128 * h
+        dma(lambda: T.yr[:, c:c + 128], lambda: T[k][0:8, b:b + 128], [v("Og" + hs)], [], 2000)
+        dma(lambda: T.yb[:, c:c + 128], lambda: T[k][8:16, b:b + 128], [v("Og" + hs)], [], 2000)
+
+    def slots(t, h):
+        hs = str(h)
+        o = v("lst" + hs, 0, 8)
+        parts = [(v("TriD"), v("FAR", 8 * h, 8 * h + 8))]
+        if h == 1:
+            parts.append((v("onesb"), v("FAR", 0, 8)))
+        mm(o, parts)
+        tt(v("slt" + hs), o, v("trs", 8 * h, 8 * h + 8), OP.min)
+        tolist(h, v("slt" + hs), lst(0), v("sl16" + hs), 1024)
+        nm, qo = qv(t, h)
+        cp((v("hq%d" % (t + 1)), v("sl16" + hs)), v(nm, qo, qo + 128))
+
+    def radii(t, h):
+        hs = str(h)
+        m = v("msc" + hs, 0, 128)
+        mm(m, [(v("sel", p=16), v("Og" + hs, p=16))])
+        act(v("rbs" + hs), m, AF.Copy)
+        cp((v("hr%d" % (t + 1)), v("sl16" + hs)), v("rbs" + hs))
+
+    def grow1(t, h):
+        hs = str(h)
+        tolist(h, v("nsc" + hs), lst(7), v("nb16" + hs))
+        act(v("Kb" + hs), (v("ctab", TR, TR + M0 + 256 * t), v("nb16" + hs)), AF.Copy)
+        ts(v("bI" + hs), v("tI" + hs), 20, OP.arith_shift_right)
+        oh = v("oh" + hs)
+        tt(oh, (v("bI" + hs), lst(7)), v("iT"), OP.is_equal)
+        m = v("msc" + hs, 0, 128)
+        mm(m, [(v("Kb" + hs), v("If"))])
+        tt(v("pr" + hs), m, oh, OP.mult)
+        scan(v("osc" + hs), v("mulR"), v("pr" + hs), 0.0, OP.mult, OP.add)
+        tt(v("nF" + hs), node(h), v("FAR", 8 * h, 8 * h + 8), OP.mult)
+        ts(v("dgi" + hs, 0, 8), v("nF" + hs), 4032, OP.bitwise_and)
+        ts(v("dgi" + hs, 8, 16), v("nF" + hs), 63, OP.bitwise_and)
+        ts(v("z" + hs), v("osc" + hs, 15, 128, 16), 0.0, OP.is_equal)
+        tt(v("DG" + hs, 0, 8), v("z" + hs), v("dgi" + hs, 0, 8), OP.mult)
+        tt(v("DG" + hs, 8, 16), v("z" + hs), v("dgi" + hs, 8, 16), OP.mult)
+        tt(v("nc" + hs), v("z" + hs), v("nF" + hs), OP.mult)
+        mm(v("lst" + hs, 0, 128, p=16), [(v("DG" + hs), v("Ib"))])
+        act(v("Ud", 128 * h, 128 * h + 128, p=16), v("lst" + hs, 0, 128, p=16), AF.Copy)
+        ts(v("z2" + hs), v("nc" + hs), 0.0, OP.is_gt, float(TR), OP.mult)
+        tt(v("ncs" + hs), v("z2" + hs), v("nc" + hs), OP.add)
+        d = v("msc" + hs, 0, 128)
+        mm(d, [(oh, v("dgl")), (oh, v("Ik%d%d" % (t, h))), (v("If"), v("Kb" + hs))])
+        act(v("vals" + hs), d, AF.Copy)
+
+    def grow2(t, h):
+        hs = str(h)
+        w = 128 * (h + 1)
+        per = 512 // w
+        for b in range(8 // per):
+            vec = 2 * b < 8 // per
+            bank = ("dif0", "dif1", "key0", "key1")[b if h == 1 else 2 * b]
+            gs = range(per * b, per * b + per)
+            for k, gg in enumerate(gs):
+                x = v(bank, w * k, w * k + w)
+                y = v(bank, w * k + w - 128, w * k + w)
+                neg = (v("nsel", 128 * gg, 128 * gg + 128, p=16), v("Ud", 0, w, p=16))
+                own = (v("Ud", 128 * h, 128 * h + 128, p=16), v("selg", 256 * gg, 256 * gg + w, p=16))
+                if vec:
+                    mm(x, [own, neg, (v("Ib"), v("tri8"))], True, True, [x, x, y])
+                else:
+                    mm(x, [neg, (v("Ib"), v("tri8"))], True, True, [x, y])
+            for k, gg in enumerate(gs):
+                x = v(bank, w * k, w * k + w)
+                if vec:
+                    red(v("dm" + hs, gg, gg + 1), x)
+                else:
+                    act(v("sq%d" % (gg % 4) + hs, 0, w), x, AF.Square, bias=v("nc" + hs, gg, gg + 1))
+            for gg in gs:
+                if not vec:
+                    act(v("sr" + hs, 0, w), v("sq%d" % (gg % 4) + hs, 0, w), AF.Relu, bias=1.0, scale=-1.0, accum=v("dm" + hs, gg, gg + 1))
+        ts(v("nd" + hs, 0, 4), v("dm" + hs, 0, 4), 0.5, OP.is_gt)
+        ts(v("nd" + hs, 4, 8), v("dm" + hs, 4, 8), 0.5, OP.is_lt)
+        tt(v("z3" + hs), v("nd" + hs), v("ncs" + hs), OP.mult)
+        tt(v("off" + hs), v("z3" + hs), v("trw", 8 * h, 8 * h + 8), OP.max)
+        tolist(h, v("off" + hs), lst(0), v("of16" + hs))
+        cp((v("ctab"), v("of16" + hs)), v("vals" + hs))
+        tt(v("wn" + hs), v("nd" + hs), v("nc" + hs), OP.mult)
+        mm(v("lst" + hs, 0, 128, p=8), [(v("wn" + hs), v("If"))])
+        act(v("wg" + hs, p=8), v("lst" + hs, 0, 128, p=8), AF.Copy)
+        c = 256 * t + 128 * h
+        dma(lambda: T.yp[:, c:c + 128], lambda: ap(v("wg" + hs, p=8)), [v("wg" + hs)], [], 2000)
+
+    for h in range(2):
+        spread(0, h, "VS")
+    for t in range(1, 4):
+        spread(t, 1, "G")
+    begin(0, 0)
+    begin(0, 1)
+    for t in range(VI):
+        order = (0, 1) if t == 0 else (1, 0)
+        for s in range(4):
+            for h in order:
+                bonus[0] = LEAD * (1 - h)
+                push(t, h, s)
+        bonus[0] = 0.0
+        for h in order:
+            finish(t, h)
+        if t < 3:
+            for h in (0, 1):
+                slots(t, h)
+            jq = send(v("lq%d" % (t + 1)), v("hq%d" % (t + 1), 0, 128), right, "aq%d" % (t + 1))
+            arrive(v("lq%d" % (t + 1)), left, "aq%d" % (t + 1), jq, 3000.0)
+        for h in order:
+            codes(t, h)
+        if t < 3:
+            for h in order:
+                grow1(t, h)
+            for h in (0, 1):
+                radii(t, h)
+            jr = send(v("lr%d" % (t + 1)), v("hr%d" % (t + 1), 0, 128), right, "ar%d" % (t + 1))
+            arrive(v("lr%d" % (t + 1)), left, "ar%d" % (t + 1), jr, 3000.0)
+            for h in order:
+                grow2(t, h)
+            begin(t + 1, 1)
+            spread(t + 1, 0, A_SPREAD)
+            begin(t + 1, 0)
+
+    n = len(ops)
+    succ = [[] for _ in range(n)]
+    cnt = [0] * n
+    for i, o in enumerate(ops):
+        ps = set(o["deps"]) | set(o["tdeps"])
+        cnt[i] = len(ps)
+        for j in ps:
+            succ[j].append(i)
+    pri = [0.0] * n
+    for i in range(n - 1, -1, -1):
+        o = ops[i]
+        pri[i] = o["busy"] + o["lat"] + max([pri[k] + HOP for k in succ[i]] + [0.0])
+    free = {e: 0.0 for e in "VSPGYR"}
+    ready = {e: [] for e in free}
+    est = [0.0] * n
+    for i in range(n):
+        if cnt[i] == 0:
+            ready[ops[i]["eng"]].append(i)
+    sched = []
+    left_n = n
+    while left_n:
+        bt, be = None, None
+        for e in free:
+            if ready[e]:
+                t0 = max(free[e], min(est[i] for i in ready[e]))
+                if bt is None or t0 < bt:
+                    bt, be = t0, e
+        cand = [i for i in ready[be] if est[i] <= bt + LOOK]
+        i = max(cand, key=lambda k: (pri[k] + ops[k]["bonus"], -k))
+        ready[be].remove(i)
+        o = ops[i]
+        sched.append(i)
+        left_n -= 1
+        bt = max(bt, est[i])
+        end = bt + o["busy"]
+        if be != "R":
+            free[be] = end
+        for k in succ[i]:
+            need = ops[k]["deps"].get(i, True)
+            a = (end + o["lat"] + HOP) if need else end
+            est[k] = max(est[k], a)
+            cnt[k] -= 1
+            if cnt[k] == 0:
+                ready[ops[k]["eng"]].append(k)
+
+    queue = {"V": g.vector, "S": g.scalar, "P": g.tensor, "G": g, "Y": g.sync}
+    count = {"V": 0, "S": 0, "P": 0, "G": 0}
+    known = {e: {} for e in queue}
+    done = [None] * n
+    clock = [None] * n
+    totals = {}
+    for i in sched:
+        o = ops[i]
+        e = o["eng"]
+        if e == "R":
+            done[i] = (o["sem"][0], o["sem"][1])
+            totals[done[i][0]] = done[i][1]
+            clock[i] = {done[i][0]: done[i][1]}
+            continue
+        kn = known[e]
+        want = {}
+        for j, need in o["deps"].items():
+            if need:
+                s, val = done[j]
+                if kn.get(s, 0) < val and want.get(s, (0, 0))[0] < val:
+                    want[s] = (val, j)
+        for s in list(want):
+            val = want[s][0]
+            if any(s2 != s and clock[want[s2][1]].get(s, 0) >= val for s2 in want):
+                del want[s]
+        for s, (val, j) in want.items():
+            queue[e].wait_ge(T.sem[s], val)
+            for s2, v2 in clock[j].items():
+                if kn.get(s2, 0) < v2:
+                    kn[s2] = v2
+        ins = o["emit"]()
+        if o["sem"] is None:
+            count[e] += 1
+            s, val = "s" + e, count[e]
+            ins.then_inc(T.sem[s], 1)
+        else:
+            s, val = o["sem"][0], o["sem"][1]
+            if e == "Y":
+                ins.then_inc(T.sem[s], 16)
+        done[i] = (s, val)
+        totals[s] = max(totals.get(s, 0), val)
+        c = dict(kn)
+        c[s] = val
+        clock[i] = c
+    kn = known["G"]
+    for s in totals:
+        if kn.get(s, 0) < totals[s]:
+            g.wait_ge(T.sem[s], totals[s])

@@ -3,30 +3,38 @@ from concourse.mybir import AluOpType, AxisListType, ActivationFunctionType
 OP = AluOpType
 AF = ActivationFunctionType
 M0, LN, VI, W = 3072, 256, 4, 3840
-C0 = 491520
-BIG = 16777216
-FR = 1.0 / BIG
-TR = 256
-CHUNKS = ((32, "S"), (32, "V"), (32, "V"), (32, "V"))
+U = 131072.0
+NONE = 16777216.0
+PEN = 268435456.0
+OFF = 135.7 * U
+KK = 4096.0
+STRIP = ~(31 << 12)
+BASE = 1.75
+PW = 168
+CFG = {
+    "chunks": (((32, "S"), (32, "V"), (32, "V"), (32, "V")), ((32, "S"), (32, "S"), (32, "V"), (32, "V"))),
+    "kgroups": ((0, 128),),
+    "p16": "V",
+    "pen": "S",
+    "spread0": "VSGVSGVSGVSGVSGV",
+    "eq": ("VVVVVVSS", "VVVVVVSS", "VVVVSSSS"),
+    "engines": 8,
+    "look": 70.0, "later": 2500.0, "hop": 90.0, "lead": 0.0,
+}
 
-AR = {"af": ("float32", 15800), "ab": ("bfloat16", 35000), "ai": ("int32", 3600), "au": ("uint16", 1200)}
+AR = {"af": ("float32", 14000), "ab": ("bfloat16", 44000), "ai": ("int32", 2600), "au": ("uint16", 1200)}
 SCRATCH = {k: ("sbuf", [128, n], d) for k, (d, n) in AR.items()}
 SCRATCH["ptab"] = ("sbuf", [128, W], "bfloat16")
-SCRATCH["ctab"] = ("sbuf", [128, TR + W], "float32")
+SCRATCH["ctab"] = ("sbuf", [128, W], "float32")
 SCRATCH["cint"] = ("sbuf", [128, M0], "int32")
 SCRATCH["qsb"] = ("sbuf", [128, VI * LN], "bfloat16")
 for _h in range(2):
     for _b in ("key", "dif", "msc", "lst"):
         SCRATCH["%s%d" % (_b, _h)] = ("psum", [128, 512], "float32")
 NY = 40
-SEMAPHORES = ["sV", "sS", "sP", "sG"] + ["y%d" % k for k in range(NY)] + ["pq1", "pq2", "pq3", "pr1", "pr2", "pr3", "aq1", "aq2", "aq3", "ar1", "ar2", "ar3"] + ["l%d" % k for k in range(12)]
+SEMAPHORES = ["sV", "sS", "sP", "sG"] + ["y%d" % k for k in range(NY)] + ["a1", "a2", "a3", "l1", "l2", "l3"]
 CYC = 0.83
 GX = 1.55
-A_SPREAD = "G"
-LEAD = 0.0
-LOOK = 70.0
-LATER = 2500.0
-HOP = 90.0
 
 
 def rank_program(g, core, T, topo):
@@ -34,6 +42,7 @@ def rank_program(g, core, T, topo):
     if rank is None:
         return
     N = len(T.cores)
+    HOP, LOOK, LATER = CFG["hop"], CFG["look"], CFG["later"]
     ops = []
     acc = {}
     fill = {k: 0 for k in AR}
@@ -63,10 +72,11 @@ def rank_program(g, core, T, topo):
         if len(x) == 2:
             return ap(x[0]).indirect(ap(x[1]))
         k, lo, hi, st, p = x
+        p0, p1 = p if isinstance(p, tuple) else (0, p)
         t = T[k]
         if st == 1:
-            return t[0:p, lo:hi]
-        return t[0:p, lo:hi:st]
+            return t[p0:p1, lo:hi]
+        return t[p0:p1, lo:hi:st]
 
     def width(x):
         if len(x) == 2:
@@ -90,7 +100,7 @@ def rank_program(g, core, T, topo):
         i = len(ops)
         deps = {}
 
-        def dep(j, kind):
+        def dep(j):
             if j == i:
                 return
             need = not (eng == "P" and ops[j]["eng"] == "P")
@@ -113,13 +123,13 @@ def rank_program(g, core, T, topo):
         for x in flat:
             for (j, y, w) in acc.get(x[0], []):
                 if w and overlap(x, y):
-                    dep(j, "RAW")
+                    dep(j)
                 elif not w and x[0] in psum and ops[j]["eng"] != eng:
-                    dep(j, "RR")
+                    dep(j)
         for x in wr:
             for (j, y, w) in acc.get(x[0], []):
                 if overlap(x, y):
-                    dep(j, "WAW" if w else "WAR")
+                    dep(j)
         for x in flat:
             acc.setdefault(x[0], []).append((i, x, False))
         for x in wr:
@@ -149,38 +159,32 @@ def rank_program(g, core, T, topo):
         add("V", lambda: g.vector.tensor_tensor(ap(out), ap(a), ap(b), op), [a, b], [out], vdur(out, [a, b], True))
 
     def ts(out, a, s1, op0, s2=None, op1=None):
-        rd = [a] + ([s1] if isinstance(s1, tuple) else [])
+        rd = [a] + [s for s in (s1, s2) if isinstance(s, tuple)]
 
         def emit():
             s = ap(s1) if isinstance(s1, tuple) else s1
             if op1 is None:
                 return g.vector.tensor_scalar(ap(out), ap(a), s, None, op0)
-            return g.vector.tensor_scalar(ap(out), ap(a), s, s2, op0, op1)
+            return g.vector.tensor_scalar(ap(out), ap(a), s, ap(s2) if isinstance(s2, tuple) else s2, op0, op1)
         add("V", emit, rd, [out], vdur(out, [a]))
 
     def scan(out, d0, d1, init, op0, op1):
         add("V", lambda: g.vector.tensor_tensor_scan(ap(out), ap(d0), ap(d1), init, op0, op1), [d0, d1], [out], 25 + CYC * width(out))
 
-    def red(out, a):
-        add("V", lambda: g.vector.tensor_reduce(ap(out), ap(a), axis=AxisListType.X, op=OP.min, apply_absolute_value=True), [a], [out], 25 + CYC * width(a))
-
     def ms(out, c):
         add("V", lambda: g.vector.memset(ap(out), c), [], [out], 25 + CYC * max(64, width(out) * (0.5 if is2(out) else 1)))
 
-    def act(out, a, func, bias=None, scale=None, accum=None):
-        rd = [a] + ([bias] if isinstance(bias, tuple) else [])
+    def act(out, a, func, bias=None, scale=None):
+        rd = [a] + [s for s in (bias, scale) if isinstance(s, tuple)]
 
         def emit():
             kw = {}
             if bias is not None:
                 kw["bias"] = ap(bias) if isinstance(bias, tuple) else bias
             if scale is not None:
-                kw["scale"] = scale
-            if accum is not None:
-                kw["accum_out"] = ap(accum)
+                kw["scale"] = ap(scale) if isinstance(scale, tuple) else scale
             return g.scalar.activation(ap(out), ap(a), func, **kw)
-        d = 65 + CYC * width(out) * (GX if len(a) == 2 else 1)
-        add("S", emit, rd, [out] + ([] if accum is None else [accum]), d + (0 if accum is None else 25))
+        add("S", emit, rd, [out], 65 + CYC * width(out) * (GX if len(a) == 2 else 1))
 
     def mm(out, parts, start=True, stop=True, outs=None):
         n = len(parts)
@@ -189,7 +193,7 @@ def rank_program(g, core, T, topo):
         for (a, b) in parts:
             rd += [a, b]
             f = 4 if a[0] == "af" else 1
-            dur += 0.72 * f * max(min(64, width(a)), width(b))
+            dur += 0.72 * f * max(min(64, width(a)), width(b)) + 5
 
         def emit():
             ins = None
@@ -197,7 +201,7 @@ def rank_program(g, core, T, topo):
                 o = out if outs is None else outs[k]
                 ins = g.tensor.matmul(ap(o), ap(a), ap(b), start and k == 0, stop and k == n - 1)
             return ins
-        add("P", emit, rd, [out], dur + 30)
+        add("P", emit, rd, [out], dur, 30.0)
 
     def iota(out, pat, base, cm, fl=False):
         add("G", lambda: g.iota(ap(out), pat, base, cm, allow_small_or_imprecise_dtypes=True) if fl else g.iota(ap(out), pat, base, cm), [], [out], 130 + 2 * CYC * width(out))
@@ -206,163 +210,185 @@ def rank_program(g, core, T, topo):
         add("G", lambda: g.affine_select(ap(out), ap(a), pat, cop, fillv, base, cm), [a], [out], 170 + 2 * CYC * width(out))
 
     ysem = [0]
+    ylast = []
 
     def dma(out_fn, in_fn, reads, writes, lat):
         s = "y%d" % ysem[0]
         ysem[0] += 1
-        return add("Y", lambda: g.sync.dma_start(out_fn(), in_fn()), reads, writes, 60.0, lat, (s, 16))
+        i = add("Y", lambda: g.sync.dma_start(out_fn(), in_fn()), reads, writes, 60.0, lat, (s, 16), ylast[-1:])
+        return i
 
-    lsem = [0]
     right, left = T.cores[(rank + 1) % N], T.cores[(rank - 1) % N]
 
     def engs(a, b):
-        return topo.engines(a, b)[:8]
+        return topo.engines(a, b)[:CFG["engines"]]
 
-    def send(out, a, dst, rsem):
-        s = "l%d" % lsem[0]
-        lsem[0] += 1
+    def send(out, a, dst, rsem, lsem):
         es = engs(core, dst)
         mk = sum(1 << e for e in es)
         rid, pid = topo.addr(dst)[:2]
-        return add("G", lambda: (g.remote_dma(ap(out), ap(a), T.sem[rsem], T.sem[s], pid, rid, mk), None)[1], [a], [], 900.0, 0.0, (s, len(es)))
+        return add("G", lambda: (g.remote_dma(ap(out), ap(a), T.sem[rsem], T.sem[lsem], pid, rid, mk), None)[1], [a], [], 900.0, 0.0, (lsem, len(es)))
 
     def arrive(out, src, rsem, after, lat):
         n = len(engs(src, core))
         return add("R", None, [], [out], 0.0, lat, (rsem, n), [after])
 
-    F, B, I, U = "af", "ab", "ai", "au"
+    F, B, I, S16 = "af", "ab", "ai", "au"
     al("wi", 1, I)
     al("thi", 1, I)
     al("r0i", 1024, I)
-    dma(lambda: ap(v("wi")), lambda: T.w[:], [], [v("wi")], 2000)
-    dma(lambda: ap(v("qsb")), lambda: T.q[:], [], [v("qsb")], 3000)
-    dma(lambda: ap(v("r0i", p=8)), lambda: T.r0[:], [], [v("r0i")], 3200)
-    dma(lambda: ap(v("thi")), lambda: T.th[:], [], [v("thi")], 3300)
-    dma(lambda: ap(v("ptab", 0, M0)), lambda: T.pt[:], [], [v("ptab", 0, M0)], 5500)
+    RT = 128
+    cuts = (RT, 1024, 2048, M0)
+    loads = [(v("wi"), lambda: T.w[:], 2000), (v("qsb"), lambda: T.q[:], 3000), (v("cint", 0, RT), lambda: T.ch[:, 0:RT], 3300),
+             (v("r0i", p=8), lambda: T.r0[:], 3400), (v("ptab", 0, M0), lambda: T.pt[:], 7000), (v("thi"), lambda: T.th[:], 7000)]
     for k in range(3):
-        dma(lambda k=k: ap(v("cint", 1024 * k, 1024 * k + 1024)), lambda k=k: T.ch[:, 1024 * k:1024 * k + 1024], [], [v("cint", 1024 * k, 1024 * k + 1024)], 7000 + 1500 * k)
-    ms(v("ptab", M0, W), 0.0)
-    ms(v("ctab", TR + M0, TR + W), 0.0)
+        loads.append((v("cint", cuts[k], cuts[k + 1]), lambda k=k: T.ch[:, cuts[k]:cuts[k + 1]], 9500 + 2500 * k))
+    for (o, src, lat) in loads:
+        ylast.append(dma(lambda o=o: ap(o), src, [], [o], lat))
+    del ylast[:]
 
-    for nm, n, k in [("onesb", 128, B), ("onesf", 128, F), ("Ib", 128, B), ("If", 128, F), ("nI", 128, B), ("tri", 128, B),
-                     ("TriD", 128, B), ("t8k", 128, B), ("tri8", 128, B), ("dgl", 128, B), ("Blk", 128, B), ("maskL", 128, F), ("rhsC", 8, F), ("BS", 8, B),
-                     ("iT", 128, F), ("addR", 128, F), ("mulR", 128, F), ("maxR", 128, F), ("trs", 16, F), ("trw", 16, F), ("zk", 128, B), ("zk0", 128, F), ("zk1", 128, F),
-                     ("RS", 8, F), ("RB1", 8, F), ("RTb", 8, B), ("sel", 128, F), ("rowc", 1, F), ("pf", 1, F), ("wf", 1, F), ("thf", 1, F), ("thr", 128, B),
-                     ("thv", 8, F), ("WS", 8, B), ("WB", 143, B), ("r0f", 1024, F), ("r0row", 1024, F), ("selg", 2048, B), ("nsel", 1024, B),
-                     ("i1", 128, I), ("i2", 128, I), ("i3", 8, I), ("i4", 8, I), ("i5", 128, I), ("i6", 128, I), ("i8", 1, I), ("i9", 1, I),
-                     ("zs", 2048, B), ("sg1", 2048, B), ("ns1", 1024, B), ("ic", 128, I), ("id", 128, F), ("il", 80, I), ("lists", 80, U)]:
+    for nm, n, k in [("onesb", 128, B), ("onesf", 128, F), ("Ib", 128, B), ("If", 128, F), ("nI", 128, B), ("Ipen", 128, B), ("IU", 128, B), ("I128", 128, B),
+                     ("I256", 128, B), ("n8k", 128, B), ("r8k", 128, B), ("tri", 128, B), ("TriD", 128, B), ("dgl", 128, B), ("Blk", 128, B), ("maskL", 128, F),
+                     ("maskP", 128, F), ("mask3", 384, F), ("rhsC", 8, F), ("BS", 8, B), ("iT", 128, F), ("iT8", 128, F), ("maxR", 128, F), ("zk", 128, B),
+                     ("zk0", 128, F), ("zk1", 128, F), ("rowc", 1, F), ("i9", 1, I), ("XC", 384, B), ("xa", 128, I), ("e0", 128, F), ("e8", 128, F), ("xr", 128, F),
+                     ("xs", 384, F), ("c16", 1, F), ("c17", 1, F), ("c18", 1, F), ("k1", 1, F), ("k2", 1, F), ("k3", 1, F), ("n16", 1, F),
+                     ("RTb", 8, B), ("pf", 1, F), ("wf", 1, F), ("thf", 1, F), ("thr", 128, B), ("thv", 8, F), ("WS", 8, B), ("r0b", 1024, B), ("N0", 64, F), ("N0o", 64, F),
+                     ("i1", 128, I), ("i2", 128, I), ("i3", 8, I), ("i4", 8, I), ("i5", 128, I), ("i6", 128, I), ("i8", 1, I), ("il", 80, I), ("lists", 80, S16),
+                     ("zs", 1024, B), ("sg1", 1024, B), ("SW", 1024, B), ("iob", 128, B), ("fr", PW, B), ("wb", 256, F), ("wr", 256, F), ("wc", 2, F), ("nw", 2, F),
+                     ("Dw0", 128, B), ("Dw1", 128, B), ("FAR", 16, B), ("rm", 24, I), ("rm2", 64, I), ("rm3", 64, F), ("Er", 384, F), ("mor", 64, S16), ("u", 144, B)]:
         al(nm, n, k)
-    for t in range(3):
-        for h in range(2):
-            al("Ik%d%d" % (t, h), 128, B)
     ms(v("onesb"), 1.0)
     ms(v("onesf"), 1.0)
     asel(v("If"), v("onesf"), [[-1, 128]], OP.is_equal, 0.0, 0, 1)
     cp(v("Ib"), v("If"))
-    ts(v("nI"), v("Ib"), -1.0, OP.mult)
+    for nm, c in (("nI", -1.0), ("Ipen", PEN), ("IU", U), ("I128", 128.0), ("I256", 256.0), ("n8k", -8192.0)):
+        ts(v(nm), v("Ib"), c, OP.mult)
+    ms(v("r8k", p=1), 8192.0)
     cp(v("wf"), v("wi"))
     iota(v("i3"), [[-16, 8]], 0, 1)
     ts(v("i4"), v("i3"), 4, OP.arith_shift_right)
     ts(v("rhsC"), v("i4"), 0.0, OP.is_equal)
     ts(v("WS"), v("rhsC"), v("wf"), OP.mult)
-    ms(v("WB"), 0.0)
-    cp(v("WB", 15, 128, 16), v("WS"))
-    ts(v("BS"), v("rhsC"), 1.0 / 256, OP.mult)
-    ts(v("RS"), v("i3"), 0.0, OP.is_equal, 1.0 / 256, OP.mult)
+    ts(v("BS"), v("rhsC"), U, OP.mult)
     ts(v("RTb"), v("i3"), 0.0, OP.is_equal)
-    ts(v("RB1"), v("i3"), 1.0, OP.is_equal)
-    iota(v("il", 0, 8), [[1, 8]], 0, 0)
-    iota(v("il", 8, 16), [[16, 8]], 15, 0)
-    for k in range(6):
-        iota(v("il", 16 + 8 * k, 24 + 8 * k), [[7, 8]], 1 + k, 0)
-    cp(v("lists", 0, 64), v("il", 0, 64))
-
-    def lst(k):
-        return v("lists", 8 * k, 8 * k + 8)
+    iota(v("il", 0, 24), [[1, 24]], 0, 0)
+    iota(v("il", 24, 32), [[16, 8]], 15, 0)
+    iota(v("il", 32, 40), [[1, 8]], PW - 8, 0)
+    iota(v("i8"), [[0, 1]], 0, 1)
+    ts(v("il", 42, 43), v("i8"), 7, OP.bitwise_and)
+    cp(v("il", 43, 44), v("il", 42, 43))
+    ts(v("il", 40, 41), v("il", 42, 43), float(PW - 8), OP.add)
+    cp(v("il", 41, 42), v("il", 42, 43))
+    cp(v("lists", 0, 44), v("il", 0, 44))
+    L0, L15, LNF, LZ = v("lists", 0, 8), v("lists", 24, 32), v("lists", 32, 41), v("lists", 42, 44)
     iota(v("i1"), [[-1, 128]], 256, 1)
     ts(v("i2"), v("i1"), 15, OP.bitwise_and)
     ts(v("maskL"), v("i2"), 0.0, OP.is_equal)
+    for k in range(3):
+        cp(v("mask3", 128 * k, 128 * k + 128), v("maskL"))
+    cp(v("pf"), v("i8"))
+    ts(v("maskP"), v("maskL"), v("pf"), OP.mult)
     iota(v("i5"), [[-16, 8], [0, 16]], 0, 1)
     ts(v("i6"), v("i5"), 4, OP.arith_shift_right)
     ts(v("Blk"), v("i6"), 0.0, OP.is_equal)
     iota(v("iT"), [[0, 8], [1, 16]], 0, 0, True)
-    ts(v("addR"), v("iT"), 0.0, OP.is_equal, 4.0, OP.mult)
-    ts(v("maxR"), v("iT"), 0.0, OP.is_equal)
-    ts(v("mulR"), v("iT"), 0.0, OP.is_gt)
+    ts(v("iT8"), v("iT"), -8.0, OP.add)
+    ts(v("maxR"), v("iT"), 0.0, OP.is_equal, 3 * NONE, OP.mult)
+    ts(v("maxR"), v("maxR"), -2 * NONE, OP.add)
     ts(v("zk0"), v("iT"), -16.0, OP.mult)
     asel(v("zk1", p=2), v("zk0", p=2), [[0, 128]], OP.is_ge, -7.5, 0, -1)
     cp(v("zk", p=2), v("zk1", p=2))
-    iota(v("i8"), [[0, 1]], 0, 1)
-    cp(v("pf"), v("i8"))
     ts(v("i9"), v("i8"), 15, OP.bitwise_and)
-    ts(v("rowc"), v("i9"), 4096.0 * FR, OP.mult, C0 * FR, OP.add)
-    iota(v("ic", p=16), [[1, 128]], 0, -16)
-    ts(v("sel", p=16), v("ic", p=16), 0.0, OP.is_equal)
-    ts(v("id", p=16), v("ic", p=16), -127.0, OP.is_equal)
-    tt(v("sel", p=16), v("sel", p=16), v("id", p=16), OP.add)
-    cp(v("r0f", p=8), v("r0i", p=8))
-    for k in range(2):
-        mm(v("dif%d" % k), [(v("sel", p=8), v("r0f", 512 * k, 512 * k + 512, p=8))])
-        act(v("r0row", 512 * k, 512 * k + 512), v("dif%d" % k), AF.Copy)
-    for t in range(1, 4):
-        al("hq%d" % t, 512, B)
-        al("hr%d" % t, 512, F)
-        al("lq%d" % t, 128, B)
-        al("lr%d" % t, 128, F)
-    for t in range(1, 4):
-        j = send(v("hq%d" % t, 0, 128), v("qsb", 256 * t, 256 * t + 128), left, "pq%d" % t)
-        arrive(v("hq%d" % t, 0, 128), right, "pq%d" % t, j, 6000.0)
-        j = send(v("hr%d" % t, 0, 128), v("r0row", 256 * t, 256 * t + 128), left, "pr%d" % t)
-        arrive(v("hr%d" % t, 0, 128), right, "pr%d" % t, j, 6000.0)
+    ts(v("rowc"), v("i9"), 4096.0, OP.mult, 4096.0 - NONE, OP.add)
+    iota(v("xa", p=32), [[-1, 8], [0, 16]], 0, 1)
+    ts(v("e0", p=32), v("xa", p=32), 0.0, OP.is_equal)
+    ts(v("e8", p=32), v("xa", p=32), 8.0, OP.is_equal)
+    ts(v("c16", p=32), v("pf", p=32), 16.0, OP.is_equal, 16.0, OP.mult)
+    ts(v("n16", p=32), v("c16", p=32), -1.0, OP.mult)
+    ts(v("k1", p=32), v("pf", p=32), 17.0, OP.is_equal, 120.5, OP.mult)
+    ts(v("k2", p=32), v("pf", p=32), 17.0, OP.is_equal, -15.5, OP.mult)
+    ts(v("c17", p=32), v("pf", p=32), 17.0, OP.is_equal, -256.0, OP.mult)
+    ts(v("c18", p=32), v("pf", p=32), 18.0, OP.is_equal, -0.5, OP.mult)
+    tt(v("k3", p=32), v("c17", p=32), v("c18", p=32), OP.add)
+    ts(v("xs", 0, 128, p=32), v("iT", p=32), v("n16", p=32), OP.mult, v("k1", p=32), OP.add)
+    ts(v("xs", 128, 256, p=32), v("iT", p=32), v("n16", p=32), OP.mult, v("k2", p=32), OP.add)
+    ts(v("xs", 256, 384, p=32), v("iT", p=32), v("c16", p=32), OP.mult, v("k3", p=32), OP.add)
+    tt(v("XC", 0, 128, p=32), v("xs", 0, 128, p=32), v("e0", p=32), OP.add)
+    tt(v("xr", p=32), v("e0", p=32), v("e8", p=32), OP.subtract)
+    tt(v("XC", 128, 256, p=32), v("xs", 128, 256, p=32), v("xr", p=32), OP.add)
+    tt(v("xr", p=32), v("e0", p=32), v("e8", p=32), OP.add)
+    tt(v("XC", 256, 384, p=32), v("xs", 256, 384, p=32), v("xr", p=32), OP.subtract)
+    cp(v("r0b", p=8), v("r0i", p=8))
+    mm(v("lst0", 0, 64), [(v("r0b", 128 * j, 128 * j + 128, p=8), v("Ib", 0, 8, p=8)) for j in range(1)], True, True, [v("lst0", 0, 8)])
+    mm(v("lst1", 0, 64), [(v("r0b", 128, 256, p=8), v("Ib", 0, 8, p=8))], True, True, [v("lst1", 0, 8)])
+    for h in range(2):
+        ts(v("N0", 8 * h, 8 * h + 8), v("lst%d" % h, 0, 8), -128.0, OP.add, U, OP.mult)
+        ts(v("N0o", 8 * h, 8 * h + 8), v("N0", 8 * h, 8 * h + 8), OFF, OP.add, KK, OP.mult)
     ms(v("ptab", 0, 1), 31.0)
+    cp(v("ctab", 0, RT), v("cint", 0, RT))
     for k in range(3):
-        cp(v("ctab", TR + 1024 * k, TR + 1024 * k + 1024), v("cint", 1024 * k, 1024 * k + 1024))
-    asel(v("tri"), v("onesb"), [[1, 128]], OP.is_gt, 0.0, 0, -1)
-    ts(v("TriD"), v("Ib"), -1024.0, OP.mult)
-    tt(v("TriD"), v("TriD"), v("tri"), OP.add)
-    ms(v("t8k"), 8192.0)
-    asel(v("tri8"), v("t8k"), [[1, 128]], OP.is_ge, 0.0, 0, -1)
-    ts(v("dgl"), v("Ib"), v("pf"), OP.mult)
-    for t in range(3):
-        for h in range(2):
-            ts(v("Ik%d%d" % (t, h)), v("Ib"), float(M0 + 256 * t + 128 * h), OP.mult)
-    iota(v("trs"), [[128, 2], [0, 8]], 256 - 1024, 1, True)
-    iota(v("trw"), [[128, 2], [0, 8]], 0, 1, True)
-    cp(v("thf"), v("thi"))
-    ts(v("thr"), v("onesf"), v("thf"), OP.mult)
-    mm(v("lst0", 0, 8), [(v("thr"), v("RTb"))])
-    ts(v("thv"), v("lst0", 0, 8), 1.0 / 256, OP.mult, C0 * FR, OP.add)
-    ms(v("zs", p=16), 0.0)
-    asel(v("sg1", p=16), v("zs", p=16), [[-1, 8], [0, 256]], OP.not_equal, 1.0, 0, 1)
-    asel(v("selg", p=16), v("sg1", p=16), [[-1, 8], [0, 256]], OP.not_equal, 1.0, -8, 1)
-    asel(v("ns1", p=16), v("zs", 0, 1024, p=16), [[-1, 8], [0, 128]], OP.not_equal, -1.0, 0, 1)
-    asel(v("nsel", p=16), v("ns1", p=16), [[-1, 8], [0, 128]], OP.not_equal, -1.0, -8, 1)
+        cp(v("ctab", cuts[k], cuts[k + 1]), v("cint", cuts[k], cuts[k + 1]))
+    ms(v("ctab", M0, W), 0.0)
 
     for h in range(2):
-        for nm, n, k in [("P16", 128, U), ("mo", 8, U), ("kS", 128, F), ("gm", 128, B), ("adm", 128, B), ("pen", 128, B), ("df", 2048, B),
-                         ("ad", 2048, B), ("sc1", 128, F), ("ins", 128, B), ("t1", 8, I), ("mI", 8, I), ("E", 128, F), ("li", 8, I), ("li2", 8, I),
-                         ("rm", 8, I), ("rm2", 8, I), ("rm3", 8, F), ("kd", 8, F), ("bi", 8, F), ("np2", 8, F), ("sl0", 8, F), ("sel3", 8, F),
-                         ("a3", 128, B), ("b3", 128, B), ("s3", 128, F),
-                         ("tI", 56, I), ("H", 56, I), ("L", 56, I), ("upd", 56, F), ("nu", 56, F), ("pk", 56, F), ("nsc", 56, F), ("O", 16, F), ("Og", 128, F),
-                         ("nz", 8, F), ("bz", 8, F), ("bb", 8, F), ("cd", 8, F), ("slt", 8, F), ("sl16", 8, U), ("rbs", 128, F), ("bI", 56, I), ("oh", 128, B),
-                         ("nb16", 8, U), ("Kb", 128, F), ("pr", 128, F), ("osc", 128, F), ("vals", 128, F), ("nF", 8, I), ("dgi", 16, I), ("z", 8, F), ("nc", 8, F),
-                         ("DG", 16, B), ("dm", 8, F), ("sq0", 256, F), ("sq1", 256, F), ("sq2", 256, F), ("sq3", 256, F), ("sr", 256, B),
-                         ("nd", 8, F), ("wn", 8, F), ("wg", 128, F), ("z2", 8, F), ("ncs", 8, F), ("z3", 8, F), ("off", 8, F), ("of16", 8, U)]:
-            al(nm + str(h), n, k)
-        for s in range(4):
-            al("As%d%d" % (s, h), 128, F)
-        for s in range(3):
-            al("v2%d%d" % (s, h), 128, F)
-            al("sc2%d%d" % (s, h), 128, F)
-        for k in range(2):
-            al("NB%d%d" % (k, h), 56, F)
-            ms(v("NB%d%d" % (k, h)), 1.5)
-        ms(v("nsc%d" % h), 0.0)
-    al("FAR", 16, B)
-    al("Ud", 256, B)
+        for nm, n, k in [("P16", 128, S16), ("mo", 8, S16), ("kS", 128, F), ("gm", 128, B), ("adm", 128, B), ("pen", 256, B), ("df", 2048, B), ("ad", 2048, B),
+                         ("sc1", 128, F), ("sc2", 128, F), ("ins", 128, B), ("v20", 128, F), ("v21", 128, F), ("op", 8, F), ("s20", 128, F), ("TN", 16, I), ("ST", 16, I), ("DR", 16, B), ("DT", 128, B), ("mI", 8, I), ("E", 128, F),
+                         ("of", 8, F), ("kd", 8, F), ("As0", 128, F), ("As1", 128, F), ("a3", 128, B), ("b3", 128, B), ("s3", 128, F), ("np2", 8, F), ("sl0", 8, F),
+                         ("DI", 32, I), ("PL", PW, B), ("z", 8, F), ("wi3", 32, B), ("ndf", 8, F), ("fl", 8, F), ("dl", 8, F), ("bI", 8, I), ("oh", 128, B), ("nb16", 8, S16),
+                         ("Kb", 128, F), ("osc", 128, F), ("cand", 8, B), ("vals", 128, F), ("Ud", 128, B), ("EQ0", 1024, B), ("EQ1", 1024, B), ("ea", 1024, B),
+                         ("win", 8, F), ("wd", 8, F), ("wn", 8, F), ("of16", 8, S16), ("Og", 256, F), ("wg", 128, F), ("slt", 8, B), ("PM", 1024, B)]:
+            if not (nm == "EQ0" and h == 1):
+                al(nm + str(h), n, k)
+        ms(v("DT%d" % h, p=32), 1.0)
+        ms(v("PL%d" % h, PW - 8, PW), -1.0)
     al("q16a", 2048, B)
     for t in range(4):
         al("q16b%d" % t, 2048, B)
+        if t > 0:
+            for nm, n in (("FT", 144), ("RV", PW), ("SB", PW), ("lq", 128)):
+                al("%s%d" % (nm, t), n, B)
+        if t < 3:
+            for h in range(2):
+                al("Ik%d%d" % (t, h), 128, B)
+
+    def late_constants():
+        asel(v("tri"), v("onesb"), [[1, 128]], OP.is_gt, 0.0, 0, -1)
+        ts(v("TriD"), v("Ib"), -1024.0, OP.mult)
+        tt(v("TriD"), v("TriD"), v("tri"), OP.add)
+        ts(v("dgl"), v("Ib"), v("pf"), OP.mult)
+        for t in range(3):
+            for h in range(2):
+                ts(v("Ik%d%d" % (t, h)), v("Ib"), float(M0 + 256 * t + 128 * h), OP.mult)
+        cp(v("thf"), v("thi"))
+        ts(v("thr"), v("onesf"), v("thf"), OP.mult)
+        mm(v("msc0", 0, 8), [(v("thr"), v("RTb"))])
+        ts(v("thv"), v("msc0", 0, 8), -128.0, OP.add, U, OP.mult)
+        iota(v("zs", p=16), [[0, 1024]], 0, 0, True)
+        asel(v("sg1", p=16), v("zs", p=16), [[-1, 8], [0, 128]], OP.not_equal, 1.0, 0, 1)
+        asel(v("SW", p=16), v("sg1", p=16), [[-1, 8], [0, 128]], OP.not_equal, 256.0, -8, 1)
+        iota(v("iob"), [[1, 128]], 0, 0, True)
+        ms(v("fr", 0, PW - 8, p=1), 0.0)
+        ms(v("fr", PW - 8, PW, p=1), 1.0)
+        ms(v("wb", p=1), 1.0 / BASE)
+        ms(v("wr", p=1), 0.0)
+        scan(v("wr", p=1), v("wb", p=1), v("wr", p=1), BASE ** 120, OP.mult, OP.add)
+        mm(v("msc1", 0, 2), [(v("wr", 0, 128, p=1), v("onesf", 0, 1, p=1))], True, True, [v("msc1", 0, 1)])
+        ts(v("wc", 0, 1), v("msc1", 0, 1), BASE ** 8, OP.mult)
+        mm(v("msc1", 0, 2), [(v("wr", 128, 256, p=1), v("onesf", 0, 1, p=1))], True, True, [v("msc1", 0, 1)])
+        ts(v("wc", 1, 2), v("msc1", 0, 1), BASE ** 8, OP.mult)
+        ts(v("nw"), v("wc"), -1.0, OP.mult)
+        for h in range(2):
+            ts(v("Dw%d" % h), v("Ib"), v("wc", h, h + 1), OP.mult, -2.55, OP.mult)
+        o = v("msc0", 0, 48)
+        mm(o, [(v("onesb", p=1), v("zs", 0, 48, p=1))] + [(v("r0b", 128 * j, 128 * j + 128, p=8), v("Ib", 0, 8, p=8)) for j in range(2, 8)], True, True,
+           [o] + [v("msc0", 8 * j - 16, 8 * j - 8) for j in range(2, 8)])
+        ts(v("N0", 16, 64), o, -128.0, OP.add, U, OP.mult)
+        ts(v("N0o", 16, 64), v("N0", 16, 64), OFF, OP.add, KK, OP.mult)
+        for t in range(1, 4):
+            ms(v("FT%d" % t, 128, 144), 0.0)
+            ts(v("FT%d" % t, 128, 136), v("N0", 16 * t, 16 * t + 8), 1.0 / U, OP.mult)
+            mm(v("msc1", 0, 128), [(v("qsb", 256 * t, 256 * t + 128), v("Ib"))])
+            act(v("FT%d" % t, 0, 128), v("msc1", 0, 128), AF.Copy)
 
     def qv(t, h):
         if h == 0 and t > 0:
@@ -376,78 +402,111 @@ def rank_program(g, core, T, topo):
         nm, o = qv(t, h)
         for i in range(16):
             out, a = v(q16(t, h), i, 2048, 16), v(nm, o, o + 128)
-            if how == "G":
+            e = how[i % len(how)]
+            if e == "G":
                 asel(out, a, [[0, 128]], OP.is_ge, 0.0, 1, 0)
-            elif how == "V" or i % 3 < 2:
+            elif e == "V":
                 cp(out, a)
             else:
                 act(out, a, AF.Copy)
 
-    def tolist(h, win, offs, dst, plus=None):
+    def tolist(h, win, dst, own=None):
         E = v("E%d" % h)
-        tt(E, (win, offs), v("maskL"), OP.mult)
         o = v("lst%d" % h, 0, 8)
-        mm(o, [(E, v("rhsC"))])
-        if plus is None:
+        tt(E, (win, L0), v("maskL"), OP.mult)
+        if own is None:
+            mm(o, [(E, v("rhsC"))])
             cp(dst, o)
         else:
-            ts(dst, o, float(plus), OP.add)
+            mm(o, [(v("maskP"), v("rhsC")), (E, v("rhsC"))])
+            ts(dst, o, float(own), OP.add)
+
+    RS = {(0, 0): 0, (0, 1): 1, (1, 1): 2, (2, 1): 3, (3, 1): 4, (1, 0): 5, (2, 0): 6, (3, 0): 7}
+
+    def roots(which, bank):
+        n, j = len(which), RS[which[0]]
+        o = v(bank, 0, 8 * n)
+        outs = [v(bank, 8 * k, 8 * k + 8) for k in range(n)]
+        zero = [(v("onesb", p=1), v("zs", 0, 8 * n, p=1))] if n > 1 else []
+        qs = [qv(t, h) for (t, h) in which]
+        mm(o, zero + [(v(nm, c, c + 128), v("WS")) for (nm, c) in qs], True, True, [o] * len(zero) + outs)
+        cp(v("rm", 0, 8 * n), o)
+        r2 = v("rm2", 8 * j, 8 * j + 8 * n)
+        ts(r2, v("rm", 0, 8 * n), 63, OP.bitwise_and)
+        tt(v("Er", 0, 128 * n), (r2, v("lists", 0, 8 * n)), v("mask3", 0, 128 * n), OP.mult)
+        mm(o, zero + [(v("Er", 128 * k, 128 * k + 128), v("rhsC")) for k in range(n)], True, True, [o] * len(zero) + outs)
+        ts(v("mor", 8 * j, 8 * j + 8 * n), o, 1.0, OP.add)
+        ts(v("rm3", 8 * j, 8 * j + 8 * n), r2, 1.0 - NONE, OP.add)
+
+    def receive(t):
+        RV, u = "RV%d" % t, v("u")
+        tt(u, (v(RV), LNF), v("FT%d" % t), OP.mult)
+        m = v("msc0", 0, 128)
+        mm(m, [(v(RV, 0, 128), v("Ib")), (v("u", 0, 128), v("Ib"))])
+        act(v("lq%d" % t), m, AF.Copy)
+        o = v("lst0", 0, 8)
+        mm(o, [(v("IU"), v(RV, 128, 136)), (v("IU"), v("u", 128, 136))])
+        cp(v("N0", 16 * t, 16 * t + 8), o)
+        ts(v("N0o", 16 * t, 16 * t + 8), o, OFF, OP.add, KK, OP.mult)
 
     def begin(t, h):
         nm, o = qv(t, h)
         hs = str(h)
-        NB = "NB%d%d" % (t % 2, h)
         if t < 3:
             act(v("ptab", M0 + 256 * t + 128 * h, M0 + 256 * t + 128 * h + 128), v(nm, o, o + 128), AF.Copy)
-        l8 = v("lst" + hs, 0, 8)
-        mm(l8, [(v("WB", 15 - l, 143 - l), v(nm, o + l, o + 128, 16)) for l in range(16)])
-        cp(v("li" + hs), l8)
-        ts(v("li2" + hs), v("li" + hs), 63, OP.bitwise_and)
-        ts(v("mo" + hs), v("li2" + hs), 1.0, OP.add)
-        m8 = v("msc" + hs, 0, 8)
-        mm(m8, [(v(nm, o, o + 128), v("WS"))])
-        cp(v("rm" + hs), m8)
-        ts(v("rm2" + hs), v("rm" + hs), 63, OP.bitwise_and)
-        ts(v("rm3" + hs), v("rm2" + hs), FR, OP.mult, (1 + C0) * FR, OP.add)
-        if h == 0 and t > 0:
-            rv = v("lr%d" % t)
-        else:
-            rv = v("r0row", 256 * t + 128 * h, 256 * t + 128 * h + 128)
-        mm(m8, [(rv, v("RS"))])
-        ts(v(NB, 1, 56, 7), m8, C0 * FR, OP.add)
-        if h == 0 and t > 0:
-            mm(m8, [(rv, v("RB1"))])
-            cp(v("bi" + hs), m8)
+
+    def lanes_of(t, h):
+        nm, o = qv(t, h)
+        m = v("msc%d" % h, 0, 128)
+        mm(m, [(v(nm, o, o + 128), v("Ib"))])
+        act(v("PL%d" % h, 0, 128), m, AF.Copy)
 
     def push(t, h, s):
         hs = str(h)
-        NB = "NB%d%d" % (t % 2, h)
         nm, o = qv(t, h)
         W1 = M0 + 256 * t
-        mo = v("mo" + hs)
-        ch, pt = v("ctab", TR, TR + W1), v("ptab", 0, W1)
-        key = v("key" + hs, 0, 128)
-        cp(v("P16" + hs), (ch, mo))
-        act(v("gm" + hs), (pt, mo), AF.Copy)
-        mz = v("msc" + hs, 0, 128)
-        mm(mz, [(v("Ib"), v("gm" + hs)), (v("nI"), v(nm, o, o + 128))])
-        act(v("adm" + hs), mz, AF.Abs)
-        act(v("kS" + hs), (ch, mo), AF.Identity, bias=v("rowc"), scale=FR)
-        As = v("As%d%d" % (s, h))
+        j = RS[(t, h)]
+        mo = v("mor", 8 * j, 8 * j + 8) if s == 0 else v("mo" + hs)
+        ch, pt = v("ctab", 0, RT if s == 0 else W1), v("ptab", 0, W1)
+        kb, k0 = "key" + hs, 0
+        key = v(kb, k0, k0 + 128)
+        TN, ST = "TN" + hs, "ST" + hs
+        As = v("As%d" % min(s, 1) + hs)
+        kS, P16 = v("kS" + hs), v("P16" + hs)
+        act(kS, (ch, mo), AF.Identity, bias=v("rowc"))
+        if CFG["p16"] == "V":
+            cp(P16, (ch, mo))
+        else:
+            ts(P16, kS, v("rowc"), OP.subtract)
+        n0 = 16 * t + 8 * h
+        pens = [v("pen" + hs, 0, 128)]
         if s == 0:
-            m2 = v("msc" + hs, 256, 264)
+            act(v("gm" + hs), (pt, mo), AF.Copy)
+            mz = v("msc" + hs, 0, 128)
+            mm(mz, [(v("Ib"), v("gm" + hs)), (v("nI"), v(nm, o, o + 128))])
+            act(v("adm" + hs), mz, AF.Abs)
+            m3 = v("msc" + hs, 128, 256)
+            mm(m3, [(v("adm" + hs), v("Blk")), (v("onesb", p=2), v("zk", p=2))])
+            act(As, m3, AF.Abs, scale=U * KK)
+            m2 = v("lst" + hs, 0, 8)
             mm(m2, [(v("adm" + hs), v("BS"))])
-            tt(v("kd" + hs), m2, v("rm3" + hs), OP.add)
-            tt(v(NB, 2, 56, 7), v("kd" + hs), v(NB, 1, 56, 7), OP.min)
-        m3 = v("msc" + hs, 128, 256)
-        mm(m3, [(v("adm" + hs), v("Blk")), (v("onesb", p=2), v("zk", p=2))])
-        act(As, m3, AF.Abs, scale=1.0 / 256)
-        prev = 1 if s == 0 else s + 2
-        tt(v("pen" + hs), (v(NB), lst(1 + prev)), As, OP.is_lt)
-        mm(key, [(v("kS" + hs), v("If")), (v("Ib"), v("pen" + hs))], True, False)
+            tt(v("kd" + hs), m2, v("rm3", 8 * j, 8 * j + 8), OP.add)
+            tt(v(ST, 8, 16), v("kd" + hs), v("N0", n0, n0 + 8), OP.min)
+            tt(pens[0], (v("N0o", n0, n0 + 8), L0), As, OP.is_lt)
+        else:
+            m = v("msc" + hs, 0, 128, p=16)
+            mm(m, [(v("DR" + hs), v("Ib"))])
+            act(v("DT" + hs, p=16), m, AF.Copy, scale=1.0 / U)
+            lo = 0 if s < 3 else 128
+            mm(v("msc" + hs, 128 + lo, 512), [(v("DT" + hs, p=19), v("XC", lo, 384, p=19))])
+            act(v("pen" + hs), v("msc" + hs, 256, 512), AF.Relu)
+            if s < 3:
+                act(As, v("msc" + hs, 128, 256), AF.Abs, scale=U * KK)
+            pens.append(v("pen" + hs, 128, 256))
+        mm(key, [(kS, v("If"))] + [(v("Ipen"), x) for x in pens], True, False)
         l0 = 0
         save = bonus[0]
-        for n_l, who in CHUNKS:
+        for ci, (n_l, who) in enumerate(CFG["chunks"][h]):
             P = v("P16" + hs, l0, l0 + n_l)
             a, b = 16 * l0, 16 * (l0 + n_l)
             l0 += n_l
@@ -456,195 +515,219 @@ def rank_program(g, core, T, topo):
             if who == "S":
                 act(df, (pt, P), AF.Copy)
                 d = v("dif" + hs, 0, b - a)
-                mm(d, [(v("Ib"), df), (v("nI"), qq)])
+                mm(d, [(v("nI"), qq), (v("Ib"), df)])
                 act(ad, d, AF.Abs)
             else:
                 tt(df, (pt, P), qq, OP.subtract)
                 act(ad, df, AF.Abs)
         bonus[0] = save
-        mm(key, [(v("ad" + hs, i, 2048, 16), v("BS")) for i in range(16)], False, True, [v("key" + hs, i, 128, 16) for i in range(16)])
-        sc1 = "sc1" + hs
-        scan(v(sc1), v("addR"), key, 4.0, OP.add, OP.min)
+        for (a, b) in CFG["kgroups"]:
+            mm(key, [(v("ad" + hs, 16 * a + i, 16 * b, 16), v("BS")) for i in range(16)], False, b == 128, [v(kb, k0 + i, k0 + 128, 16, (a, b)) for i in range(16)])
+        sc1, sc2, v2 = "sc1" + hs, ("sc2" if s else "s20") + hs, v("v2%d" % min(s, 1) + hs)
+        scan(v(sc1), v("maxR"), key, NONE, OP.max, OP.min)
         k15 = v(sc1, 15, 128, 16)
+        of = v("of" + hs)
+        if s == 0:
+            tt(v(TN, 8, 16), v(ST, 8, 16), k15, OP.min)
+            ts(of, v(TN, 8, 16), OFF, OP.add, -KK, OP.mult)
+        elif s < 3:
+            ts(of, k15, OFF, OP.add, -KK, OP.mult)
         if s < 3:
-            v2, sc2 = v("v2%d%d" % (s, h)), "sc2%d%d" % (s, h)
-            if s == 0:
-                tt(v(NB, 3, 56, 7), v(NB, 2, 56, 7), k15, OP.min)
-                tt(v("ins" + hs), (v(NB), lst(4)), As, OP.is_lt)
-            else:
-                tt(v("ins" + hs), (v(sc1), lst(1)), As, OP.is_lt)
+            tt(v("ins" + hs), (of, L0), As, OP.add)
             tt(v2, key, v("ins" + hs), OP.max)
-            scan(v(sc2), v("maxR"), v2, 1.0, OP.max, OP.min)
+            scan(v(sc2), v("maxR"), v2, NONE, OP.max, OP.min)
             src = v(sc2, 15, 128, 16)
             if s == 2:
-                tt(v("sel3" + hs), src, v("sl0" + hs), OP.min)
-                src = v("sel3" + hs)
-            ts(v("t1" + hs), src, float(BIG), OP.mult, -float(C0), OP.add)
-            ts(v("mI" + hs), v("t1" + hs), 4095, OP.bitwise_and)
-            tolist(h, v("mI" + hs), lst(0), mo)
+                tt(v(TN, 0, 8), src, v("sl0" + hs), OP.min)
+            else:
+                cp(v(TN, 0, 8), src)
+            ts(v("mI" + hs), v(TN, 0, 8), 4095, OP.bitwise_and)
+            tolist(h, v("mI" + hs), v("mo" + hs))
         if s > 0:
-            tt(v(NB, s + 3, 56, 7), v(NB, s + 2, 56, 7), k15, OP.min)
+            tt(v(TN, 8, 16), v(ST, 8, 16), k15, OP.min)
+        if s < 3:
+            ts(v(ST), v(TN), STRIP, OP.bitwise_and)
+            cp(v("DR" + hs), v(ST))
+        if s == 0:
+            tt(v("a3" + hs), (v(sc2), L15), v2, OP.is_ge)
         if s == 1:
-            v20, s20 = v("v20" + hs), v("sc20" + hs)
-            tt(v("a3" + hs), (s20, lst(1)), v20, OP.is_ge)
-            tt(v("b3" + hs), (v(NB), lst(5)), v("As0" + hs), OP.is_lt)
-            m4 = v("msc" + hs, 384, 512)
-            mm(m4, [(v("If"), v20), (v("Ib"), v("a3" + hs)), (v("Ib"), v("b3" + hs))])
-            scan(v("s3" + hs), v("maxR"), m4, 1.0, OP.max, OP.min)
-            ts(v("np2" + hs), v("sc21" + hs, 15, 128, 16), 1.0, OP.is_lt)
-            tt(v("sl0" + hs), v("np2" + hs), v("s3" + hs, 15, 128, 16), OP.max)
+            ts(v("op" + hs), of, -1.0, OP.mult)
+            tt(v("b3" + hs), (v("op" + hs), L0), v("As0" + hs), OP.is_lt)
+            ts(v("np2" + hs), v(TN, 0, 8), NONE, OP.is_lt, 4 * NONE, OP.mult)
+            k00 = v("lst" + hs, 128, 256)
+            mm(k00, [(v("If"), v("v20" + hs)), (v("Ipen"), v("a3" + hs)), (v("Ipen"), v("b3" + hs))])
+            scan(v("s3" + hs), v("maxR"), k00, NONE, OP.max, OP.min)
+            tt(v("sl0" + hs), v("np2" + hs), v("s3" + hs, 15, 128, 16), OP.add)
 
-    def finish(t, h):
+    def digits(t, h):
         hs = str(h)
-        NB = "NB%d%d" % (t % 2, h)
+        Nn, DI, PL = v("TN" + hs, 8, 16), "DI" + hs, "PL" + hs
+        ts(v(DI, 24, 32), Nn, 4095, OP.bitwise_and)
         if t < 3:
-            tt(v("FAR", 8 * h, 8 * h + 8), v(NB, 6, 56, 7), v("thv"), OP.is_ge)
-        ts(v("tI" + hs), v(NB), float(BIG), OP.mult, -float(C0), OP.add)
-        ts(v("H" + hs), v("tI" + hs), 16, OP.arith_shift_right)
-        ts(v("L" + hs), v("tI" + hs), 4095, OP.bitwise_and)
-        tt(v("upd" + hs, 1, 56), v("H" + hs, 1, 56), v("H" + hs, 0, 55), OP.is_lt)
-        tt(v("nu" + hs, 1, 56), v("H" + hs, 1, 56), v("H" + hs, 0, 55), OP.is_ge)
-        tt(v("pk" + hs, 1, 56), v("upd" + hs, 1, 56), v("L" + hs, 1, 56), OP.mult)
-        scan(v("nsc" + hs, 1, 56), v("nu" + hs, 1, 56), v("pk" + hs, 1, 56), 0.0, OP.mult, OP.add)
+            tolist(h, v(DI, 24, 32), v("nb16" + hs))
+            tt(v("FAR", 8 * h, 8 * h + 8), Nn, v("thv"), OP.is_ge)
+        ts(v(DI, 8, 16), Nn, 255, OP.bitwise_and)
+        ts(v(DI, 16, 24), Nn, 4095, OP.bitwise_and, 8, OP.arith_shift_right)
+        ts(v(DI, 0, 8), Nn, 17, OP.arith_shift_right)
+        cp(v(PL, 128, 152), v(DI, 0, 24))
+        ts(v(PL, 152, 160), v(DI, 24, 32), 0.0, OP.is_gt, float(16 * rank), OP.mult)
 
-    def node(h):
-        return v("nsc%d" % h, 6, 56, 7)
-
-    def codes(t, h):
+    def wishes(t, h):
         hs = str(h)
-        cp(v("O" + hs, 0, 8), v("H" + hs, 6, 56, 7))
-        ts(v("nz" + hs), node(h), 0.0, OP.is_gt, float(4096 * rank), OP.mult)
-        if h == 0 and t > 0:
-            tt(v("cd" + hs), node(h), v("nz" + hs), OP.add)
-            ts(v("bz" + hs), node(h), 0.0, OP.is_equal)
-            tt(v("bb" + hs), v("bz" + hs), v("bi" + hs), OP.mult)
-            tt(v("O" + hs, 8, 16), v("cd" + hs), v("bb" + hs), OP.add)
-        else:
-            tt(v("O" + hs, 8, 16), node(h), v("nz" + hs), OP.add)
-        mm(v("lst" + hs, 0, 128, p=16), [(v("O" + hs), v("If"))])
-        act(v("Og" + hs, p=16), v("lst" + hs, 0, 128, p=16), AF.Copy)
-        k, b, n = names["Og" + hs]
+        DI, PL = "DI" + hs, "PL" + hs
+        act(v("Kb" + hs), (v("ctab", 0, M0 + 256 * t), v("nb16" + hs)), AF.Copy)
+        m = v("msc" + hs, 0, 128, p=16)
+        mm(m, [(v(PL, 136, 152), v("Ib"))])
+        act(v("Ud" + hs, p=16), m, AF.Copy)
+        cp(v("ndf" + hs), v(DI, 24, 32))
+        ts(v("bI" + hs), v("TN" + hs, 8, 16), 21, OP.arith_shift_right)
+        oh = v("oh" + hs)
+        tt(oh, (v("bI" + hs), L0), v("iT8"), OP.is_equal)
+        tt(v("fl" + hs), v("FAR", 8 * h, 8 * h + 8), v("ndf" + hs), OP.min)
+        ts(v("dl" + hs), v("ndf" + hs), v("pf"), OP.subtract, float(M0 + 256 * t + 128 * h), OP.subtract)
+        x = v("msc" + hs, 128, 256)
+        mm(x, [(v("onesb", p=1), v("r8k", p=1)), (v("n8k"), oh), (v("Kb" + hs), v("If"))])
+        scan(v("osc" + hs), v("maxR"), x, NONE, OP.max, OP.min)
+        tt(v("cand" + hs), v("osc" + hs, 15, 128, 16), v("fl" + hs), OP.is_lt)
+        for k, bank in enumerate(("key" + hs, "dif" + hs)):
+            for gg in range(4 * k, 4 * k + 4):
+                c = 128 * (gg % 4)
+                mm(v(bank, c, c + 128), [(v("SW", 128 * gg, 128 * gg + 128, p=16), v("Ud" + hs, p=16))])
+        d = v("msc" + hs, 256, 384)
+        mm(d, [(oh, v("dgl")), (oh, v("Ik%d%d" % (t, h))), (v("If"), v("Kb" + hs))])
+        act(v("vals" + hs), d, AF.Copy)
+
+    def equal(a, b, how):
+        dst = "EQ%d%d" % (0 if a == b == 0 else 1, a)
+        run = [gg for gg in range(8) if how[gg] == "S"]
+        for gg in range(8):
+            src = v(("key", "dif")[gg // 4] + str(b), 128 * (gg % 4), 128 * (gg % 4) + 128)
+            col = v("ndf%d" % a, gg, gg + 1)
+            if how[gg] == "V":
+                ts(v(dst, 128 * gg, 128 * gg + 128), src, col, OP.is_equal, v("wc", a, a + 1), OP.mult)
+            else:
+                act(v("ea%d" % b, 128 * gg, 128 * gg + 128), src, AF.Abs, bias=col, scale=-1.0)
+        if run:
+            lo, hi = 128 * run[0], 128 * run[-1] + 128
+            act(v(dst, lo, hi), v("ea%d" % b, lo, hi), AF.Relu, bias=v("wc", a, a + 1), scale=v("nw", a, a + 1))
+
+    def count(a, b, first, last):
+        dst = "EQ%d%d" % (0 if a == b == 0 else 1, a)
+        o = v("lst%d" % b, 0, 8)
+        head = [(v("Dw%d" % b), v("cand%d" % b))] if first else []
+        mm(o, head + [(v(dst, 128 * gg, 128 * gg + 128), v("cand%d" % a, gg, gg + 1)) for gg in range(8)], first, last,
+           [o] * len(head) + [v("lst%d" % b, gg, gg + 1) for gg in range(8)])
+
+    def grow(t, h):
+        hs = str(h)
+        ts(v("win" + hs), v("lst" + hs, 0, 8), 0.0, OP.is_lt)
+        tt(v("wd" + hs), v("win" + hs), v("dl" + hs), OP.mult)
+        tolist(h, v("wd" + hs), v("of16" + hs), M0 + 256 * t + 128 * h)
+        cp((v("ctab", 0, M0 + 256 * t + 256), v("of16" + hs)), v("vals" + hs))
+
+    def parents(t, h):
+        hs = str(h)
+        tt(v("wn" + hs), v("win" + hs), v("ndf" + hs), OP.mult)
+        m = v("msc" + hs, 0, 128, p=8)
+        mm(m, [(v("wn" + hs), v("If"))])
+        act(v("wg" + hs, p=8), m, AF.Copy)
         c = 256 * t + 128 * h
-        dma(lambda: T.yr[:, c:c + 128], lambda: T[k][0:8, b:b + 128], [v("Og" + hs)], [], 2000)
-        dma(lambda: T.yb[:, c:c + 128], lambda: T[k][8:16, b:b + 128], [v("Og" + hs)], [], 2000)
+        dma(lambda: T.yp[:, c:c + 128], lambda: ap(v("wg" + hs, p=8)), [v("wg" + hs)], [], 2000)
 
-    def slots(t, h):
+    def carried(t):
+        ts(v("z0"), v("DI0", 24, 32), 0.0, OP.is_equal)
+        tt(v("wi30"), (v("z0"), LZ), v("RV%d" % t, 136, 168), OP.mult)
+        tt(v("PL0", 136, 160), v("PL0", 136, 160), v("wi30", 0, 24), OP.add)
+
+    def outputs(t, h):
         hs = str(h)
-        o = v("lst" + hs, 0, 8)
+        PL = "PL" + hs
+        a, b = v("msc" + hs, 0, 128, p=8), v("msc" + hs, 128, 256, p=8)
+        mm(a, [(v("onesb", 0, 8), v("I128")), (v(PL, 128, 136), v("Ib"))])
+        mm(b, [(v(PL, 136, 144), v("Ib")), (v(PL, 144, 152), v("I256")), (v(PL, 152, 160), v("I256"))])
+        act(v("Og" + hs, p=8), v("msc" + hs, 0, 256, p=8), AF.Copy)
+        c = 256 * t + 128 * h
+        dma(lambda: T.yr[:, c:c + 128], lambda: ap(v("Og" + hs, 0, 128, p=8)), [v("Og" + hs)], [], 2000)
+        dma(lambda: T.yb[:, c:c + 128], lambda: ap(v("Og" + hs, 128, 256, p=8)), [v("Og" + hs)], [], 2000)
+
+    def places(h):
+        hs = str(h)
+        o = v("msc" + hs, 0, 8)
         parts = [(v("TriD"), v("FAR", 8 * h, 8 * h + 8))]
         if h == 1:
             parts.append((v("onesb"), v("FAR", 0, 8)))
         mm(o, parts)
-        tt(v("slt" + hs), o, v("trs", 8 * h, 8 * h + 8), OP.min)
-        tolist(h, v("slt" + hs), lst(0), v("sl16" + hs), 1024)
-        nm, qo = qv(t, h)
-        cp((v("hq%d" % (t + 1)), v("sl16" + hs)), v(nm, qo, qo + 128))
+        ts(v("slt" + hs), o, 1024.0, OP.add)
+        for gg in range(8):
+            ts(v("PM" + hs, 128 * gg, 128 * gg + 128), v("iob"), v("slt" + hs, gg, gg + 1), OP.is_equal)
 
-    def radii(t, h):
-        hs = str(h)
-        m = v("msc" + hs, 0, 128)
-        mm(m, [(v("sel", p=16), v("Og" + hs, p=16))])
-        act(v("rbs" + hs), m, AF.Copy)
-        cp((v("hr%d" % (t + 1)), v("sl16" + hs)), v("rbs" + hs))
-
-    def grow1(t, h):
-        hs = str(h)
-        tolist(h, v("nsc" + hs), lst(7), v("nb16" + hs))
-        act(v("Kb" + hs), (v("ctab", TR, TR + M0 + 256 * t), v("nb16" + hs)), AF.Copy)
-        ts(v("bI" + hs), v("tI" + hs), 20, OP.arith_shift_right)
-        oh = v("oh" + hs)
-        tt(oh, (v("bI" + hs), lst(7)), v("iT"), OP.is_equal)
-        m = v("msc" + hs, 0, 128)
-        mm(m, [(v("Kb" + hs), v("If"))])
-        tt(v("pr" + hs), m, oh, OP.mult)
-        scan(v("osc" + hs), v("mulR"), v("pr" + hs), 0.0, OP.mult, OP.add)
-        tt(v("nF" + hs), node(h), v("FAR", 8 * h, 8 * h + 8), OP.mult)
-        ts(v("dgi" + hs, 0, 8), v("nF" + hs), 4032, OP.bitwise_and)
-        ts(v("dgi" + hs, 8, 16), v("nF" + hs), 63, OP.bitwise_and)
-        ts(v("z" + hs), v("osc" + hs, 15, 128, 16), 0.0, OP.is_equal)
-        tt(v("DG" + hs, 0, 8), v("z" + hs), v("dgi" + hs, 0, 8), OP.mult)
-        tt(v("DG" + hs, 8, 16), v("z" + hs), v("dgi" + hs, 8, 16), OP.mult)
-        tt(v("nc" + hs), v("z" + hs), v("nF" + hs), OP.mult)
-        mm(v("lst" + hs, 0, 128, p=16), [(v("DG" + hs), v("Ib"))])
-        act(v("Ud", 128 * h, 128 * h + 128, p=16), v("lst" + hs, 0, 128, p=16), AF.Copy)
-        ts(v("z2" + hs), v("nc" + hs), 0.0, OP.is_gt, float(TR), OP.mult)
-        tt(v("ncs" + hs), v("z2" + hs), v("nc" + hs), OP.add)
-        d = v("msc" + hs, 0, 128)
-        mm(d, [(oh, v("dgl")), (oh, v("Ik%d%d" % (t, h))), (v("If"), v("Kb" + hs))])
-        act(v("vals" + hs), d, AF.Copy)
-
-    def grow2(t, h):
-        hs = str(h)
-        w = 128 * (h + 1)
-        per = 512 // w
-        for b in range(8 // per):
-            vec = 2 * b < 8 // per
-            bank = ("dif0", "dif1", "key0", "key1")[b if h == 1 else 2 * b]
-            gs = range(per * b, per * b + per)
-            for k, gg in enumerate(gs):
-                x = v(bank, w * k, w * k + w)
-                y = v(bank, w * k + w - 128, w * k + w)
-                neg = (v("nsel", 128 * gg, 128 * gg + 128, p=16), v("Ud", 0, w, p=16))
-                own = (v("Ud", 128 * h, 128 * h + 128, p=16), v("selg", 256 * gg, 256 * gg + w, p=16))
-                if vec:
-                    mm(x, [own, neg, (v("Ib"), v("tri8"))], True, True, [x, x, y])
-                else:
-                    mm(x, [neg, (v("Ib"), v("tri8"))], True, True, [x, y])
-            for k, gg in enumerate(gs):
-                x = v(bank, w * k, w * k + w)
-                if vec:
-                    red(v("dm" + hs, gg, gg + 1), x)
-                else:
-                    act(v("sq%d" % (gg % 4) + hs, 0, w), x, AF.Square, bias=v("nc" + hs, gg, gg + 1))
-            for gg in gs:
-                if not vec:
-                    act(v("sr" + hs, 0, w), v("sq%d" % (gg % 4) + hs, 0, w), AF.Relu, bias=1.0, scale=-1.0, accum=v("dm" + hs, gg, gg + 1))
-        ts(v("nd" + hs, 0, 4), v("dm" + hs, 0, 4), 0.5, OP.is_gt)
-        ts(v("nd" + hs, 4, 8), v("dm" + hs, 4, 8), 0.5, OP.is_lt)
-        tt(v("z3" + hs), v("nd" + hs), v("ncs" + hs), OP.mult)
-        tt(v("off" + hs), v("z3" + hs), v("trw", 8 * h, 8 * h + 8), OP.max)
-        tolist(h, v("off" + hs), lst(0), v("of16" + hs))
-        cp((v("ctab"), v("of16" + hs)), v("vals" + hs))
-        tt(v("wn" + hs), v("nd" + hs), v("nc" + hs), OP.mult)
-        mm(v("lst" + hs, 0, 128, p=8), [(v("wn" + hs), v("If"))])
-        act(v("wg" + hs, p=8), v("lst" + hs, 0, 128, p=8), AF.Copy)
-        c = 256 * t + 128 * h
-        dma(lambda: T.yp[:, c:c + 128], lambda: ap(v("wg" + hs, p=8)), [v("wg" + hs)], [], 2000)
+    def hand_on(t):
+        o = v("msc1", 0, PW)
+        mm(o, [(v("onesb", p=1), v("fr", p=1))], True, False)
+        for h in (0, 1):
+            for g0 in (0, 4):
+                parts, outs = [], []
+                for gg in range(g0, g0 + 4):
+                    pm = v("PM%d" % h, 128 * gg, 128 * gg + 128)
+                    parts += [(pm, v("PL%d" % h, 16 * gg, 16 * gg + 16)), (pm, v("PL%d" % h, 128 + gg, PW, 8))]
+                    outs += [v("msc1", 16 * gg, 16 * gg + 16), v("msc1", 128 + gg, PW, 8)]
+                mm(o, parts, False, h == 1 and g0 == 4, outs)
+        act(v("SB%d" % (t + 1)), o, AF.Copy)
+        j = send(v("RV%d" % (t + 1)), v("SB%d" % (t + 1)), right, "a%d" % (t + 1), "l%d" % (t + 1))
+        arrive(v("RV%d" % (t + 1)), left, "a%d" % (t + 1), j, 3000.0)
 
     for h in range(2):
-        spread(0, h, "VS")
+        roots([(0, h)], "lst%d" % h)
+        spread(0, h, "VVS")
+        begin(0, h)
+    bonus[0] = -30000.0
+    late_constants()
+    roots([(1, 1), (2, 1), (3, 1)], "msc1")
     for t in range(1, 4):
         spread(t, 1, "G")
-    begin(0, 0)
-    begin(0, 1)
     for t in range(VI):
         order = (0, 1) if t == 0 else (1, 0)
         for s in range(4):
             for h in order:
-                bonus[0] = LEAD * (1 - h)
+                bonus[0] = CFG["lead"] * h
                 push(t, h, s)
+                if s == 1 and t < 3:
+                    bonus[0] = -5000.0
+                    lanes_of(t, h)
         bonus[0] = 0.0
-        for h in order:
-            finish(t, h)
-        if t < 3:
-            for h in (0, 1):
-                slots(t, h)
-            jq = send(v("lq%d" % (t + 1)), v("hq%d" % (t + 1), 0, 128), right, "aq%d" % (t + 1))
-            arrive(v("lq%d" % (t + 1)), left, "aq%d" % (t + 1), jq, 3000.0)
-        for h in order:
-            codes(t, h)
-        if t < 3:
+        if t == 3:
             for h in order:
-                grow1(t, h)
-            for h in (0, 1):
-                radii(t, h)
-            jr = send(v("lr%d" % (t + 1)), v("hr%d" % (t + 1), 0, 128), right, "ar%d" % (t + 1))
-            arrive(v("lr%d" % (t + 1)), left, "ar%d" % (t + 1), jr, 3000.0)
-            for h in order:
-                grow2(t, h)
-            begin(t + 1, 1)
-            spread(t + 1, 0, A_SPREAD)
-            begin(t + 1, 0)
+                digits(t, h)
+                if h == 0:
+                    carried(t)
+                outputs(t, h)
+            break
+        digits(t, 1)
+        wishes(t, 1)
+        equal(1, 1, CFG["eq"][2])
+        count(1, 1, True, False)
+        outputs(t, 1)
+        digits(t, 0)
+        wishes(t, 0)
+        if t > 0:
+            carried(t)
+        places(0)
+        places(1)
+        hand_on(t)
+        equal(0, 0, CFG["eq"][0])
+        equal(0, 1, CFG["eq"][1])
+        count(0, 0, True, True)
+        count(0, 1, False, True)
+        grow(t, 0)
+        grow(t, 1)
+        outputs(t, 0)
+        parents(t, 0)
+        parents(t, 1)
+        begin(t + 1, 1)
+        receive(t + 1)
+        roots([(t + 1, 0)], "lst0")
+        spread(t + 1, 0, CFG["spread0"])
+        begin(t + 1, 0)
 
     n = len(ops)
     succ = [[] for _ in range(n)]
@@ -684,15 +767,17 @@ def rank_program(g, core, T, topo):
         if be != "R":
             free[be] = end
         for k in succ[i]:
-            need = ops[k]["deps"].get(i, True)
-            a = (end + o["lat"] + HOP) if need else end
+            if i in ops[k]["deps"]:
+                a = (end + o["lat"] + HOP) if ops[k]["deps"][i] else end
+            else:
+                a = end
             est[k] = max(est[k], a)
             cnt[k] -= 1
             if cnt[k] == 0:
                 ready[ops[k]["eng"]].append(k)
 
     queue = {"V": g.vector, "S": g.scalar, "P": g.tensor, "G": g, "Y": g.sync}
-    count = {"V": 0, "S": 0, "P": 0, "G": 0}
+    count_of = {"V": 0, "S": 0, "P": 0, "G": 0}
     known = {e: {} for e in queue}
     done = [None] * n
     clock = [None] * n
@@ -723,8 +808,8 @@ def rank_program(g, core, T, topo):
                     kn[s2] = v2
         ins = o["emit"]()
         if o["sem"] is None:
-            count[e] += 1
-            s, val = "s" + e, count[e]
+            count_of[e] += 1
+            s, val = "s" + e, count_of[e]
             ins.then_inc(T.sem[s], 1)
         else:
             s, val = o["sem"][0], o["sem"][1]

@@ -12,17 +12,18 @@ STRIP = ~(31 << 12)
 BASE = 1.75
 PW = 168
 CFG = {
-    "chunks": (((32, "S"), (32, "V"), (32, "V"), (32, "V")), ((32, "S"), (32, "S"), (32, "V"), (32, "V"))),
+    "chunks": (((32, "S"), (48, (24, 24)), (48, (24, 24))),) * 2,
+    "labs": 500.0, "conv": "G", "margin": 500.0, "tol": 400.0, "gap": 100.0, "iscan": True, "sign": (1, 0), "dr": "G", "ksplit": 4, "lS": 0.0, "spreadA": "VS", "rounds": 3,
     "kgroups": ((0, 128),),
     "p16": "V",
     "pen": "S",
-    "spread0": "VSGVSGVSGVSGVSGV",
-    "eq": ("VVVVVVSS", "VVVVVVSS", "VVVVSSSS"),
+    "spread0": "VG",
+    "eq": ("VVVVVVVV", "VVVVSSSS", "VVVVSSSS"),
     "engines": 8,
-    "look": 70.0, "later": 2500.0, "hop": 90.0, "lead": 0.0,
+    "look": 40.0, "later": 2000.0, "hop": 90.0, "lead": -2000.0,
 }
 
-AR = {"af": ("float32", 14000), "ab": ("bfloat16", 44000), "ai": ("int32", 2600), "au": ("uint16", 1200)}
+AR = {"af": ("float32", 14000), "ab": ("bfloat16", 44000), "ai": ("int32", 3600), "au": ("uint16", 1200)}
 SCRATCH = {k: ("sbuf", [128, n], d) for k, (d, n) in AR.items()}
 SCRATCH["ptab"] = ("sbuf", [128, W], "bfloat16")
 SCRATCH["ctab"] = ("sbuf", [128, W], "float32")
@@ -135,7 +136,7 @@ def rank_program(g, core, T, topo):
         for x in wr:
             acc[x[0]] = [e for e in acc.get(x[0], []) if e[0] == i or not covers(x, e[1])]
             acc[x[0]].append((i, x, True))
-        ops.append({"eng": eng, "emit": emit, "deps": deps, "busy": busy, "lat": lat, "sem": sem, "tdeps": list(extra), "bonus": bonus[0]})
+        ops.append({"eng": eng, "emit": emit, "deps": deps, "busy": busy, "lat": lat, "sem": sem, "tdeps": list(extra), "bonus": bonus[0], "tag": CFG["tagf"]() if "tagf" in CFG else 0})
         return i
 
     def vdur(out, ins, two=False):
@@ -250,7 +251,7 @@ def rank_program(g, core, T, topo):
     for nm, n, k in [("onesb", 128, B), ("onesf", 128, F), ("Ib", 128, B), ("If", 128, F), ("nI", 128, B), ("Ipen", 128, B), ("IU", 128, B), ("I128", 128, B),
                      ("I256", 128, B), ("n8k", 128, B), ("r8k", 128, B), ("tri", 128, B), ("TriD", 128, B), ("dgl", 128, B), ("Blk", 128, B), ("maskL", 128, F),
                      ("maskP", 128, F), ("mask3", 384, F), ("rhsC", 8, F), ("BS", 8, B), ("iT", 128, F), ("iT8", 128, F), ("maxR", 128, F), ("zk", 128, B),
-                     ("zk0", 128, F), ("zk1", 128, F), ("rowc", 1, F), ("i9", 1, I), ("XC", 384, B), ("xa", 128, I), ("e0", 128, F), ("e8", 128, F), ("xr", 128, F),
+                     ("zk0", 128, F), ("zk1", 128, F), ("kc0", 128, F), ("KC", 128, B), ("XC", 384, B), ("xa", 128, I), ("e0", 128, F), ("e8", 128, F), ("xr", 128, F),
                      ("xs", 384, F), ("c16", 1, F), ("c17", 1, F), ("c18", 1, F), ("k1", 1, F), ("k2", 1, F), ("k3", 1, F), ("n16", 1, F),
                      ("RTb", 8, B), ("pf", 1, F), ("wf", 1, F), ("thf", 1, F), ("thr", 128, B), ("thv", 8, F), ("WS", 8, B), ("r0b", 1024, B), ("N0", 64, F), ("N0o", 64, F),
                      ("i1", 128, I), ("i2", 128, I), ("i3", 8, I), ("i4", 8, I), ("i5", 128, I), ("i6", 128, I), ("i8", 1, I), ("il", 80, I), ("lists", 80, S16),
@@ -298,27 +299,17 @@ def rank_program(g, core, T, topo):
     ts(v("zk0"), v("iT"), -16.0, OP.mult)
     asel(v("zk1", p=2), v("zk0", p=2), [[0, 128]], OP.is_ge, -7.5, 0, -1)
     cp(v("zk", p=2), v("zk1", p=2))
-    ts(v("i9"), v("i8"), 15, OP.bitwise_and)
-    ts(v("rowc"), v("i9"), 4096.0, OP.mult, 4096.0 - NONE, OP.add)
-    iota(v("xa", p=32), [[-1, 8], [0, 16]], 0, 1)
-    ts(v("e0", p=32), v("xa", p=32), 0.0, OP.is_equal)
-    ts(v("e8", p=32), v("xa", p=32), 8.0, OP.is_equal)
-    ts(v("c16", p=32), v("pf", p=32), 16.0, OP.is_equal, 16.0, OP.mult)
-    ts(v("n16", p=32), v("c16", p=32), -1.0, OP.mult)
-    ts(v("k1", p=32), v("pf", p=32), 17.0, OP.is_equal, 120.5, OP.mult)
-    ts(v("k2", p=32), v("pf", p=32), 17.0, OP.is_equal, -15.5, OP.mult)
-    ts(v("c17", p=32), v("pf", p=32), 17.0, OP.is_equal, -256.0, OP.mult)
-    ts(v("c18", p=32), v("pf", p=32), 18.0, OP.is_equal, -0.5, OP.mult)
-    tt(v("k3", p=32), v("c17", p=32), v("c18", p=32), OP.add)
-    ts(v("xs", 0, 128, p=32), v("iT", p=32), v("n16", p=32), OP.mult, v("k1", p=32), OP.add)
-    ts(v("xs", 128, 256, p=32), v("iT", p=32), v("n16", p=32), OP.mult, v("k2", p=32), OP.add)
-    ts(v("xs", 256, 384, p=32), v("iT", p=32), v("c16", p=32), OP.mult, v("k3", p=32), OP.add)
-    tt(v("XC", 0, 128, p=32), v("xs", 0, 128, p=32), v("e0", p=32), OP.add)
-    tt(v("xr", p=32), v("e0", p=32), v("e8", p=32), OP.subtract)
-    tt(v("XC", 128, 256, p=32), v("xs", 128, 256, p=32), v("xr", p=32), OP.add)
-    tt(v("xr", p=32), v("e0", p=32), v("e8", p=32), OP.add)
-    tt(v("XC", 256, 384, p=32), v("xs", 256, 384, p=32), v("xr", p=32), OP.subtract)
-    cp(v("r0b", p=8), v("r0i", p=8))
+    iota(v("kc0", p=2), [[0, 8], [4096, 16]], 4096, 0, True)
+    asel(v("KC", p=2), v("kc0", p=2), [[0, 128]], OP.is_gt, -NONE, 0, 1)
+    for k, (step, rows) in enumerate(((-16, ((17, 120.5, 0), (0, 1.0, -1))), (-16, ((17, -15.5, 0), (0, 1.0, -1), (8, -1.0, -1))),
+                                      (16, ((17, -256.0, 0), (18, -0.5, 0), (0, -1.0, -1), (8, -1.0, -1))))):
+        x = v("XC", 128 * k, 128 * k + 128, p=32)
+        iota(x, [[0, 8], [step, 16]], 0, 0, True)
+        asel(x, x, [[0, 128]], OP.is_equal, 0.0, -16, 1)
+        for (r, c, d) in rows:
+            asel(x, x, [[d, 8], [0, 16]], OP.not_equal, c, -r, 1)
+    cp(v("r0b", 0, 256, p=8), v("r0i", 0, 256, p=8))
+    asel(v("r0b", 256, 1024, p=8), v("r0i", 256, 1024, p=8), [[0, 768]], OP.is_ge, 0.0, 1, 0)
     mm(v("lst0", 0, 64), [(v("r0b", 128 * j, 128 * j + 128, p=8), v("Ib", 0, 8, p=8)) for j in range(1)], True, True, [v("lst0", 0, 8)])
     mm(v("lst1", 0, 64), [(v("r0b", 128, 256, p=8), v("Ib", 0, 8, p=8))], True, True, [v("lst1", 0, 8)])
     for h in range(2):
@@ -327,20 +318,26 @@ def rank_program(g, core, T, topo):
     ms(v("ptab", 0, 1), 31.0)
     cp(v("ctab", 0, RT), v("cint", 0, RT))
     for k in range(3):
-        cp(v("ctab", cuts[k], cuts[k + 1]), v("cint", cuts[k], cuts[k + 1]))
-    ms(v("ctab", M0, W), 0.0)
+        if CFG["conv"] == "V":
+            cp(v("ctab", cuts[k], cuts[k + 1]), v("cint", cuts[k], cuts[k + 1]))
+        else:
+            asel(v("ctab", cuts[k], cuts[k + 1]), v("cint", cuts[k], cuts[k + 1]), [[0, cuts[k + 1] - cuts[k]]], OP.is_ge, 0.0, 1, 0)
+    iota(v("ctab", M0, W), [[0, W - M0]], 0, 0, True)
 
     for h in range(2):
         for nm, n, k in [("P16", 128, S16), ("mo", 8, S16), ("kS", 128, F), ("gm", 128, B), ("adm", 128, B), ("pen", 256, B), ("df", 2048, B), ("ad", 2048, B),
                          ("sc1", 128, F), ("sc2", 128, F), ("ins", 128, B), ("v20", 128, F), ("v21", 128, F), ("op", 8, F), ("s20", 128, F), ("TN", 16, I), ("ST", 16, I), ("DR", 16, B), ("DT", 128, B), ("mI", 8, I), ("E", 128, F),
                          ("of", 8, F), ("kd", 8, F), ("As0", 128, F), ("As1", 128, F), ("a3", 128, B), ("b3", 128, B), ("s3", 128, F), ("np2", 8, F), ("sl0", 8, F),
-                         ("DI", 32, I), ("PL", PW, B), ("z", 8, F), ("wi3", 32, B), ("ndf", 8, F), ("fl", 8, F), ("dl", 8, F), ("bI", 8, I), ("oh", 128, B), ("nb16", 8, S16),
-                         ("Kb", 128, F), ("osc", 128, F), ("cand", 8, B), ("vals", 128, F), ("Ud", 128, B), ("EQ0", 1024, B), ("EQ1", 1024, B), ("ea", 1024, B),
-                         ("win", 8, F), ("wd", 8, F), ("wn", 8, F), ("of16", 8, S16), ("Og", 256, F), ("wg", 128, F), ("slt", 8, B), ("PM", 1024, B)]:
+                         ("DI", 32, I), ("PL", PW, B), ("z", 8, F), ("wi3", 32, B), ("fl", 8, F), ("bI", 8, I), ("oh", 128, B), ("nb16", 8, S16), ("S20", 256, I), ("S21", 256, I),
+                         ("Kb", 128, F), ("Ks", 128, B), ("osc", 128, F), ("Ud", 128, B), ("EQ0", 1024, B), ("EQ1", 1024, B), ("ea", 1024, B),
+                         ("Og", 256, F), ("PM", 1024, B)]:
             if not (nm == "EQ0" and h == 1):
                 al(nm + str(h), n, k)
         ms(v("DT%d" % h, p=32), 1.0)
         ms(v("PL%d" % h, PW - 8, PW), -1.0)
+    for nm, n, k in [("ndf", 16, F), ("dl", 16, F), ("cand", 16, B), ("vals", 256, F), ("win", 16, F), ("wd", 16, F), ("wn", 16, F), ("of16", 16, S16), ("wg", 256, F),
+                     ("slt", 16, B), ("ownl", 128, B), ("ownc", 16, B), ("own0", 128, B), ("own1", 16, B)]:
+        al(nm, n, k)
     al("q16a", 2048, B)
     for t in range(4):
         al("q16b%d" % t, 2048, B)
@@ -367,6 +364,10 @@ def rank_program(g, core, T, topo):
         asel(v("sg1", p=16), v("zs", p=16), [[-1, 8], [0, 128]], OP.not_equal, 1.0, 0, 1)
         asel(v("SW", p=16), v("sg1", p=16), [[-1, 8], [0, 128]], OP.not_equal, 256.0, -8, 1)
         iota(v("iob"), [[1, 128]], 0, 0, True)
+        iota(v("own0", p=2), [[0, 8], [1, 16]], 0, 0, True)
+        asel(v("ownl", p=2), v("own0", p=2), [[0, 128]], OP.is_ge, 1.0, 0, -1)
+        iota(v("own1", p=2), [[16, 16]], 0, 0, True)
+        asel(v("ownc", p=2), v("own1", p=2), [[0, 16]], OP.is_gt, 1.0, 0, 1)
         ms(v("fr", 0, PW - 8, p=1), 0.0)
         ms(v("fr", PW - 8, PW, p=1), 1.0)
         ms(v("wb", p=1), 1.0 / BASE)
@@ -453,13 +454,30 @@ def rank_program(g, core, T, topo):
         nm, o = qv(t, h)
         hs = str(h)
         if t < 3:
-            act(v("ptab", M0 + 256 * t + 128 * h, M0 + 256 * t + 128 * h + 128), v(nm, o, o + 128), AF.Copy)
+            asel(v("ptab", M0 + 256 * t + 128 * h, M0 + 256 * t + 128 * h + 128), v(nm, o, o + 128), [[0, 128]], OP.is_ge, 0.0, 1, 0)
 
     def lanes_of(t, h):
         nm, o = qv(t, h)
         m = v("msc%d" % h, 0, 128)
         mm(m, [(v(nm, o, o + 128), v("Ib"))])
         act(v("PL%d" % h, 0, 128), m, AF.Copy)
+
+    def root(t, h):
+        hs = str(h)
+        nm, o = qv(t, h)
+        j, n0 = RS[(t, h)], 16 * t + 8 * h
+        As = v("As0" + hs)
+        act(v("gm" + hs), (v("ptab", 0, RT), v("mor", 8 * j, 8 * j + 8)), AF.Copy)
+        mz = v("msc" + hs, 0, 128)
+        mm(mz, [(v("nI"), v(nm, o, o + 128)), (v("Ib"), v("gm" + hs))])
+        act(v("adm" + hs), mz, AF.Abs)
+        m3, m2 = v("msc" + hs, 128, 256), v("msc" + hs, 256, 264)
+        mm(m3, [(v("onesb", p=2), v("zk", p=2)), (v("adm" + hs), v("Blk"))])
+        mm(m2, [(v("adm" + hs), v("BS"))])
+        act(As, m3, AF.Abs, scale=U * KK)
+        tt(v("kd" + hs), m2, v("rm3", 8 * j, 8 * j + 8), OP.add)
+        tt(v("ST" + hs, 8, 16), v("kd" + hs), v("N0", n0, n0 + 8), OP.min)
+        tt(v("pen" + hs, 0, 128), (v("N0o", n0, n0 + 8), L0), As, OP.is_lt)
 
     def push(t, h, s):
         hs = str(h)
@@ -473,27 +491,23 @@ def rank_program(g, core, T, topo):
         TN, ST = "TN" + hs, "ST" + hs
         As = v("As%d" % min(s, 1) + hs)
         kS, P16 = v("kS" + hs), v("P16" + hs)
-        act(kS, (ch, mo), AF.Identity, bias=v("rowc"))
-        if CFG["p16"] == "V":
+        how = CFG["p16"][s % len(CFG["p16"])]
+        if how != "K":
+            act(kS, (ch, mo), AF.Copy)
+        if how == "K":
             cp(P16, (ch, mo))
+            asel(kS, P16, [[0, 128]], OP.is_ge, 0.0, 1, 0)
+        elif how == "V":
+            cp(P16, (ch, mo))
+        elif how == "S":
+            cp(P16, kS)
+        elif how == "G":
+            asel(P16, kS, [[0, 128]], OP.is_ge, 0.0, 1, 0)
         else:
-            ts(P16, kS, v("rowc"), OP.subtract)
-        n0 = 16 * t + 8 * h
+            for c in (0, 64):
+                asel(v("P16" + hs, c, c + 64), v("kS" + hs, c, c + 64), [[0, 64]], OP.is_ge, 0.0, 1, 0)
         pens = [v("pen" + hs, 0, 128)]
-        if s == 0:
-            act(v("gm" + hs), (pt, mo), AF.Copy)
-            mz = v("msc" + hs, 0, 128)
-            mm(mz, [(v("Ib"), v("gm" + hs)), (v("nI"), v(nm, o, o + 128))])
-            act(v("adm" + hs), mz, AF.Abs)
-            m3 = v("msc" + hs, 128, 256)
-            mm(m3, [(v("adm" + hs), v("Blk")), (v("onesb", p=2), v("zk", p=2))])
-            act(As, m3, AF.Abs, scale=U * KK)
-            m2 = v("lst" + hs, 0, 8)
-            mm(m2, [(v("adm" + hs), v("BS"))])
-            tt(v("kd" + hs), m2, v("rm3", 8 * j, 8 * j + 8), OP.add)
-            tt(v(ST, 8, 16), v("kd" + hs), v("N0", n0, n0 + 8), OP.min)
-            tt(pens[0], (v("N0o", n0, n0 + 8), L0), As, OP.is_lt)
-        else:
+        if s > 0:
             m = v("msc" + hs, 0, 128, p=16)
             mm(m, [(v("DR" + hs), v("Ib"))])
             act(v("DT" + hs, p=16), m, AF.Copy, scale=1.0 / U)
@@ -503,7 +517,9 @@ def rank_program(g, core, T, topo):
             if s < 3:
                 act(As, v("msc" + hs, 128, 256), AF.Abs, scale=U * KK)
             pens.append(v("pen" + hs, 128, 256))
-        mm(key, [(kS, v("If"))] + [(v("Ipen"), x) for x in pens], True, False)
+        mm(key, [(v("onesb", p=2), v("KC", p=2))], True, False)
+        mm(key, [(kS, v("If"))], False, False)
+        mm(key, [(v("Ipen"), x) for x in pens], False, False)
         l0 = 0
         save = bonus[0]
         for ci, (n_l, who) in enumerate(CFG["chunks"][h]):
@@ -513,47 +529,62 @@ def rank_program(g, core, T, topo):
             df, ad, qq = v("df" + hs, a, b), v("ad" + hs, a, b), v(q16(t, h), a, b)
             bonus[0] = save - LATER
             if who == "S":
+                bonus[0] = save - CFG["lS"]
                 act(df, (pt, P), AF.Copy)
-                d = v("dif" + hs, 0, b - a)
-                mm(d, [(v("nI"), qq), (v("Ib"), df)])
+                d = v(("dif", "lst")[ci] + hs, 0, b - a)
+                mm(d, [(v("nI"), qq)], True, False)
+                mm(d, [(v("Ib"), df)], False, True)
                 act(ad, d, AF.Abs)
             else:
-                tt(df, (pt, P), qq, OP.subtract)
+                c0 = l0 - n_l
+                for w in who:
+                    tt(v("df" + hs, 16 * c0, 16 * (c0 + w)), (pt, v("P16" + hs, c0, c0 + w)), v(q16(t, h), 16 * c0, 16 * (c0 + w)), OP.subtract)
+                    c0 += w
+                bonus[0] = save - CFG["labs"]
                 act(ad, df, AF.Abs)
         bonus[0] = save
         for (a, b) in CFG["kgroups"]:
-            mm(key, [(v("ad" + hs, 16 * a + i, 16 * b, 16), v("BS")) for i in range(16)], False, b == 128, [v(kb, k0 + i, k0 + 128, 16, (a, b)) for i in range(16)])
+            for i0 in range(0, 16, CFG["ksplit"]):
+                rows = range(i0, i0 + CFG["ksplit"])
+                mm(key, [(v("ad" + hs, 16 * a + i, 16 * b, 16), v("BS")) for i in rows], False, b == 128 and 15 in rows, [v(kb, k0 + i, k0 + 128, 16, (a, b)) for i in rows])
         sc1, sc2, v2 = "sc1" + hs, ("sc2" if s else "s20") + hs, v("v2%d" % min(s, 1) + hs)
         scan(v(sc1), v("maxR"), key, NONE, OP.max, OP.min)
         k15 = v(sc1, 15, 128, 16)
         of = v("of" + hs)
+        t1, nn, both, so = v(TN, 0, 8), v(TN, 8, 16), v(TN), v(sc2)
+        if CFG["iscan"] and s < 3:
+            S2 = "S2%d" % min(s, 1) + hs
+            t1, nn, both, so = v(S2, 15, 128, 16), v(S2, 143, 256, 16), v(S2, 15, 256, 16), v(S2, 0, 128)
         if s == 0:
-            tt(v(TN, 8, 16), v(ST, 8, 16), k15, OP.min)
-            ts(of, v(TN, 8, 16), OFF, OP.add, -KK, OP.mult)
+            tt(nn, v(ST, 8, 16), k15, OP.min)
+            ts(of, nn, OFF, OP.add, -KK, OP.mult)
         elif s < 3:
             ts(of, k15, OFF, OP.add, -KK, OP.mult)
         if s < 3:
             tt(v("ins" + hs), (of, L0), As, OP.add)
             tt(v2, key, v("ins" + hs), OP.max)
-            scan(v(sc2), v("maxR"), v2, NONE, OP.max, OP.min)
-            src = v(sc2, 15, 128, 16)
+            scan(so, v("maxR"), v2, NONE, OP.max, OP.min)
+            src = (so[0], so[1] + 15, so[2], 16, 128)
             if s == 2:
-                tt(v(TN, 0, 8), src, v("sl0" + hs), OP.min)
-            else:
-                cp(v(TN, 0, 8), src)
-            ts(v("mI" + hs), v(TN, 0, 8), 4095, OP.bitwise_and)
+                tt(t1, src, v("sl0" + hs), OP.min)
+            elif not CFG["iscan"]:
+                cp(t1, src)
+            ts(v("mI" + hs), t1, 4095, OP.bitwise_and)
             tolist(h, v("mI" + hs), v("mo" + hs))
         if s > 0:
-            tt(v(TN, 8, 16), v(ST, 8, 16), k15, OP.min)
+            tt(nn, v(ST, 8, 16), k15, OP.min)
         if s < 3:
-            ts(v(ST), v(TN), STRIP, OP.bitwise_and)
-            cp(v("DR" + hs), v(ST))
+            ts(v(ST), both, STRIP, OP.bitwise_and)
+            if CFG["dr"] == "V":
+                cp(v("DR" + hs), v(ST))
+            else:
+                asel(v("DR" + hs), v(ST), [[0, 16]], OP.is_ge, 0.0, 1, 0)
         if s == 0:
-            tt(v("a3" + hs), (v(sc2), L15), v2, OP.is_ge)
+            tt(v("a3" + hs), (so, L15), v2, OP.is_ge)
         if s == 1:
             ts(v("op" + hs), of, -1.0, OP.mult)
             tt(v("b3" + hs), (v("op" + hs), L0), v("As0" + hs), OP.is_lt)
-            ts(v("np2" + hs), v(TN, 0, 8), NONE, OP.is_lt, 4 * NONE, OP.mult)
+            ts(v("np2" + hs), t1, NONE, OP.is_lt, 4 * NONE, OP.mult)
             k00 = v("lst" + hs, 128, 256)
             mm(k00, [(v("If"), v("v20" + hs)), (v("Ipen"), v("a3" + hs)), (v("Ipen"), v("b3" + hs))])
             scan(v("s3" + hs), v("maxR"), k00, NONE, OP.max, OP.min)
@@ -575,34 +606,38 @@ def rank_program(g, core, T, topo):
     def wishes(t, h):
         hs = str(h)
         DI, PL = "DI" + hs, "PL" + hs
-        act(v("Kb" + hs), (v("ctab", 0, M0 + 256 * t), v("nb16" + hs)), AF.Copy)
+        col = (v("ctab", 0, M0 + 256 * t), v("nb16" + hs))
+        if CFG["sign"][h]:
+            act(v("Ks" + hs), col, AF.Sign)
+        act(v("Kb" + hs), col, AF.Copy)
         m = v("msc" + hs, 0, 128, p=16)
         mm(m, [(v(PL, 136, 152), v("Ib"))])
         act(v("Ud" + hs, p=16), m, AF.Copy)
-        cp(v("ndf" + hs), v(DI, 24, 32))
+        ndf = v("ndf", 8 * h, 8 * h + 8)
+        cp(ndf, v(DI, 24, 32))
         ts(v("bI" + hs), v("TN" + hs, 8, 16), 21, OP.arith_shift_right)
         oh = v("oh" + hs)
         tt(oh, (v("bI" + hs), L0), v("iT8"), OP.is_equal)
-        tt(v("fl" + hs), v("FAR", 8 * h, 8 * h + 8), v("ndf" + hs), OP.min)
-        ts(v("dl" + hs), v("ndf" + hs), v("pf"), OP.subtract, float(M0 + 256 * t + 128 * h), OP.subtract)
-        x = v("msc" + hs, 128, 256)
-        mm(x, [(v("onesb", p=1), v("r8k", p=1)), (v("n8k"), oh), (v("Kb" + hs), v("If"))])
-        scan(v("osc" + hs), v("maxR"), x, NONE, OP.max, OP.min)
-        tt(v("cand" + hs), v("osc" + hs, 15, 128, 16), v("fl" + hs), OP.is_lt)
+        tt(v("fl" + hs), v("FAR", 8 * h, 8 * h + 8), ndf, OP.min)
+        ts(v("dl", 8 * h, 8 * h + 8), ndf, v("pf"), OP.subtract, float(M0 + 256 * t + 128 * h), OP.subtract)
         for k, bank in enumerate(("key" + hs, "dif" + hs)):
             for gg in range(4 * k, 4 * k + 4):
                 c = 128 * (gg % 4)
                 mm(v(bank, c, c + 128), [(v("SW", 128 * gg, 128 * gg + 128, p=16), v("Ud" + hs, p=16))])
+        x = v("msc" + hs, 128, 256)
+        mm(x, [(v("onesb", p=1), v("r8k", p=1)), (v("n8k"), oh), (v("Ks" + hs), v("Ib")) if CFG["sign"][h] else (v("Kb" + hs), v("If"))])
+        scan(v("osc" + hs), v("maxR"), x, NONE, OP.max, OP.min)
+        tt(v("cand", 8 * h, 8 * h + 8), v("osc" + hs, 15, 128, 16), v("fl" + hs), OP.is_lt)
         d = v("msc" + hs, 256, 384)
         mm(d, [(oh, v("dgl")), (oh, v("Ik%d%d" % (t, h))), (v("If"), v("Kb" + hs))])
-        act(v("vals" + hs), d, AF.Copy)
+        act(v("vals", 128 * h, 128 * h + 128), d, AF.Copy)
 
     def equal(a, b, how):
         dst = "EQ%d%d" % (0 if a == b == 0 else 1, a)
         run = [gg for gg in range(8) if how[gg] == "S"]
         for gg in range(8):
             src = v(("key", "dif")[gg // 4] + str(b), 128 * (gg % 4), 128 * (gg % 4) + 128)
-            col = v("ndf%d" % a, gg, gg + 1)
+            col = v("ndf", 8 * a + gg, 8 * a + gg + 1)
             if how[gg] == "V":
                 ts(v(dst, 128 * gg, 128 * gg + 128), src, col, OP.is_equal, v("wc", a, a + 1), OP.mult)
             else:
@@ -611,28 +646,32 @@ def rank_program(g, core, T, topo):
             lo, hi = 128 * run[0], 128 * run[-1] + 128
             act(v(dst, lo, hi), v("ea%d" % b, lo, hi), AF.Relu, bias=v("wc", a, a + 1), scale=v("nw", a, a + 1))
 
-    def count(a, b, first, last):
+    def count(a, b, first, last, graphs=range(8)):
         dst = "EQ%d%d" % (0 if a == b == 0 else 1, a)
-        o = v("lst%d" % b, 0, 8)
-        head = [(v("Dw%d" % b), v("cand%d" % b))] if first else []
-        mm(o, head + [(v(dst, 128 * gg, 128 * gg + 128), v("cand%d" % a, gg, gg + 1)) for gg in range(8)], first, last,
-           [o] * len(head) + [v("lst%d" % b, gg, gg + 1) for gg in range(8)])
+        o = v("lst1", 0, 16)
+        parts, outs = [], []
+        if first:
+            parts, outs = [(v("onesb", p=1), v("zs", 0, 16, p=1))], [o]
+        if a == b and 0 in graphs:
+            parts, outs = parts + [(v("Dw%d" % b), v("cand", 8 * b, 8 * b + 8))], outs + [v("lst1", 8 * b, 8 * b + 8)]
+        mm(o, parts + [(v(dst, 128 * gg, 128 * gg + 128), v("cand", 8 * a + gg, 8 * a + gg + 1)) for gg in graphs], first, last,
+           outs + [v("lst1", 8 * b + gg, 8 * b + gg + 1) for gg in graphs])
 
-    def grow(t, h):
-        hs = str(h)
-        ts(v("win" + hs), v("lst" + hs, 0, 8), 0.0, OP.is_lt)
-        tt(v("wd" + hs), v("win" + hs), v("dl" + hs), OP.mult)
-        tolist(h, v("wd" + hs), v("of16" + hs), M0 + 256 * t + 128 * h)
-        cp((v("ctab", 0, M0 + 256 * t + 256), v("of16" + hs)), v("vals" + hs))
+    def grow(t):
+        ts(v("win"), v("lst1", 0, 16), 0.0, OP.is_lt)
+        tt(v("wd"), v("win"), v("dl"), OP.mult)
+        tt(v("Er", 0, 256), (v("wd"), v("lists", 0, 16)), v("mask3", 0, 256), OP.mult)
+        o = v("lst0", 0, 16)
+        mm(o, [(v("ownl", p=2), v("ownc", p=2)), (v("Er", 0, 128), v("rhsC")), (v("Er", 128, 256), v("rhsC"))], True, True, [o, v("lst0", 0, 8), v("lst0", 8, 16)])
+        ts(v("of16"), o, float(M0 + 256 * t), OP.add)
+        cp((v("ctab", 0, M0 + 256 * t + 256), v("of16")), v("vals"))
 
-    def parents(t, h):
-        hs = str(h)
-        tt(v("wn" + hs), v("win" + hs), v("ndf" + hs), OP.mult)
-        m = v("msc" + hs, 0, 128, p=8)
-        mm(m, [(v("wn" + hs), v("If"))])
-        act(v("wg" + hs, p=8), m, AF.Copy)
-        c = 256 * t + 128 * h
-        dma(lambda: T.yp[:, c:c + 128], lambda: ap(v("wg" + hs, p=8)), [v("wg" + hs)], [], 2000)
+    def parents(t):
+        tt(v("wn"), v("win"), v("ndf"), OP.mult)
+        for h in range(2):
+            mm(v("msc1", 128 * h, 128 * h + 128, p=8), [(v("wn", 8 * h, 8 * h + 8), v("If"))])
+        act(v("wg", p=8), v("msc1", 0, 256, p=8), AF.Copy)
+        dma(lambda: T.yp[:, 256 * t:256 * t + 256], lambda: ap(v("wg", p=8)), [v("wg")], [], 2000)
 
     def carried(t):
         ts(v("z0"), v("DI0", 24, 32), 0.0, OP.is_equal)
@@ -650,39 +689,34 @@ def rank_program(g, core, T, topo):
         dma(lambda: T.yr[:, c:c + 128], lambda: ap(v("Og" + hs, 0, 128, p=8)), [v("Og" + hs)], [], 2000)
         dma(lambda: T.yb[:, c:c + 128], lambda: ap(v("Og" + hs, 128, 256, p=8)), [v("Og" + hs)], [], 2000)
 
-    def places(h):
-        hs = str(h)
-        o = v("msc" + hs, 0, 8)
-        parts = [(v("TriD"), v("FAR", 8 * h, 8 * h + 8))]
-        if h == 1:
-            parts.append((v("onesb"), v("FAR", 0, 8)))
-        mm(o, parts)
-        ts(v("slt" + hs), o, 1024.0, OP.add)
-        for gg in range(8):
-            ts(v("PM" + hs, 128 * gg, 128 * gg + 128), v("iob"), v("slt" + hs, gg, gg + 1), OP.is_equal)
+    def places():
+        o = v("msc0", 0, 16)
+        mm(o, [(v("TriD"), v("FAR")), (v("onesb"), v("FAR", 0, 8))], True, True, [o, v("msc0", 8, 16)])
+        ts(v("slt"), o, 1024.0, OP.add)
+        for h in (1, 0):
+            for gg in range(8):
+                ts(v("PM%d" % h, 128 * gg, 128 * gg + 128), v("iob"), v("slt", 8 * h + gg, 8 * h + gg + 1), OP.is_equal)
 
     def hand_on(t):
         o = v("msc1", 0, PW)
         mm(o, [(v("onesb", p=1), v("fr", p=1))], True, False)
-        for h in (0, 1):
-            for g0 in (0, 4):
+        for h in (1, 0):
+            for g0 in range(0, 8, 2):
                 parts, outs = [], []
-                for gg in range(g0, g0 + 4):
+                for gg in range(g0, g0 + 2):
                     pm = v("PM%d" % h, 128 * gg, 128 * gg + 128)
                     parts += [(pm, v("PL%d" % h, 16 * gg, 16 * gg + 16)), (pm, v("PL%d" % h, 128 + gg, PW, 8))]
                     outs += [v("msc1", 16 * gg, 16 * gg + 16), v("msc1", 128 + gg, PW, 8)]
-                mm(o, parts, False, h == 1 and g0 == 4, outs)
+                mm(o, parts, False, h == 0 and g0 == 6, outs)
         act(v("SB%d" % (t + 1)), o, AF.Copy)
         j = send(v("RV%d" % (t + 1)), v("SB%d" % (t + 1)), right, "a%d" % (t + 1), "l%d" % (t + 1))
         arrive(v("RV%d" % (t + 1)), left, "a%d" % (t + 1), j, 3000.0)
 
     for h in range(2):
         roots([(0, h)], "lst%d" % h)
-        spread(0, h, "VVS")
+        spread(0, h, CFG["spreadA"])
         begin(0, h)
-    bonus[0] = -30000.0
-    late_constants()
-    roots([(1, 1), (2, 1), (3, 1)], "msc1")
+        root(0, h)
     for t in range(1, 4):
         spread(t, 1, "G")
     for t in range(VI):
@@ -692,9 +726,18 @@ def rank_program(g, core, T, topo):
                 bonus[0] = CFG["lead"] * h
                 push(t, h, s)
                 if s == 1 and t < 3:
-                    bonus[0] = -5000.0
+                    bonus[0] = 0.0
                     lanes_of(t, h)
-        bonus[0] = 0.0
+            bonus[0] = 0.0
+            if (t, s) == (0, 0):
+                late_constants()
+            if s == 0 and t > 0:
+                outputs(t - 1, 0)
+                parents(t - 1)
+            if (t, s) == (0, 2) and CFG.get("boom"):
+                mm(v("msc0", 0, 8), [(v("Ib"), v("DR0", 0, 8))], False, True)
+            if (t, s) == (0, 1):
+                roots([(1, 1), (2, 1), (3, 1)], "msc1")
         if t == 3:
             for h in order:
                 digits(t, h)
@@ -706,26 +749,25 @@ def rank_program(g, core, T, topo):
         wishes(t, 1)
         equal(1, 1, CFG["eq"][2])
         count(1, 1, True, False)
-        outputs(t, 1)
         digits(t, 0)
+        places()
         wishes(t, 0)
         if t > 0:
             carried(t)
-        places(0)
-        places(1)
         hand_on(t)
-        equal(0, 0, CFG["eq"][0])
+        root(t + 1, 1)
+        outputs(t, 1)
         equal(0, 1, CFG["eq"][1])
-        count(0, 0, True, True)
-        count(0, 1, False, True)
-        grow(t, 0)
-        grow(t, 1)
-        outputs(t, 0)
-        parents(t, 0)
-        parents(t, 1)
+        equal(0, 0, CFG["eq"][0])
+        count(0, 1, False, False, range(4))
+        count(0, 0, False, False, range(4))
+        count(0, 1, False, False, range(4, 8))
+        count(0, 0, False, True, range(4, 8))
+        grow(t)
         begin(t + 1, 1)
         receive(t + 1)
         roots([(t + 1, 0)], "lst0")
+        root(t + 1, 0)
         spread(t + 1, 0, CFG["spread0"])
         begin(t + 1, 0)
 
@@ -748,6 +790,7 @@ def rank_program(g, core, T, topo):
         if cnt[i] == 0:
             ready[ops[i]["eng"]].append(i)
     sched = []
+    first = [0.0] * n
     left_n = n
     while left_n:
         bt, be = None, None
@@ -757,13 +800,23 @@ def rank_program(g, core, T, topo):
                 if bt is None or t0 < bt:
                     bt, be = t0, e
         cand = [i for i in ready[be] if est[i] <= bt + LOOK]
-        i = max(cand, key=lambda k: (pri[k] + ops[k]["bonus"], -k))
+        rate = lambda k: (pri[k] + ops[k]["bonus"], -k)
+        i = max(cand, key=rate)
+        soon = [k for k in ready[be] if rate(k)[0] > rate(i)[0] + CFG["margin"] and est[k] + CFG["tol"] < bt + ops[i]["busy"]]
+        if soon:
+            due = min(soon, key=lambda k: est[k])
+            fit = [k for k in cand if bt + ops[k]["busy"] <= est[due] + CFG["tol"]]
+            if fit:
+                i = max(fit, key=rate)
+            elif est[due] - bt <= CFG["gap"]:
+                i = due
         ready[be].remove(i)
         o = ops[i]
         sched.append(i)
         left_n -= 1
         bt = max(bt, est[i])
         end = bt + o["busy"]
+        first[i] = bt
         if be != "R":
             free[be] = end
         for k in succ[i]:
@@ -775,6 +828,53 @@ def rank_program(g, core, T, topo):
             cnt[k] -= 1
             if cnt[k] == 0:
                 ready[ops[k]["eng"]].append(k)
+
+    before = [[] for _ in range(n)]
+    after = [[] for _ in range(n)]
+    for i, o in enumerate(ops):
+        for j in set(o["deps"]) | set(o["tdeps"]):
+            w = ops[j]["lat"] + HOP if o["deps"].get(j, False) else 0.0
+            before[i].append((j, w))
+            after[j].append((i, w))
+    tail = [o["lat"] for o in ops]
+
+    def place(order, edges, back):
+        at = [0.0] * n
+        lines = {e: ([], []) for e in free}
+        for i in order:
+            d = ops[i]["busy"]
+            t0 = max([at[j] + ops[j]["busy"] + w for (j, w) in edges[i]] + [tail[i] if back else 0.0])
+            if d > 0:
+                lo, hi = lines[ops[i]["eng"]]
+                a, b = 0, len(hi)
+                while a < b:
+                    m = (a + b) // 2
+                    if hi[m] <= t0:
+                        a = m + 1
+                    else:
+                        b = m
+                while a < len(lo) and lo[a] < t0 + d:
+                    t0 = max(t0, hi[a])
+                    a += 1
+                lo.insert(a, t0)
+                hi.insert(a, t0 + d)
+            at[i] = t0
+        return at
+
+    def span(at):
+        return max(at[i] + ops[i]["busy"] + tail[i] for i in range(n))
+    best = first
+    at = first
+    for _ in range(CFG["rounds"]):
+        back = place(sorted(range(n), key=lambda i: (-(at[i] + ops[i]["busy"]), -i)), after, True)
+        at = place(sorted(range(n), key=lambda i: (-(back[i] + ops[i]["busy"]), i)), before, False)
+        if span(at) < span(best):
+            best = at
+    sched = sorted(range(n), key=lambda i: (best[i], i))
+    if "ops" in CFG:
+        CFG["ops"].append((ops, before, after, best, pri))
+    if "dbg" in CFG and rank == 1:
+        CFG["dbg"] += [(ops[i]["tag"], ops[i]["eng"], best[i], best[i] + ops[i]["busy"], i) for i in sched]
 
     queue = {"V": g.vector, "S": g.scalar, "P": g.tensor, "G": g, "Y": g.sync}
     count_of = {"V": 0, "S": 0, "P": 0, "G": 0}

@@ -12,18 +12,21 @@ STRIP = ~(31 << 12)
 BASE = 1.75
 PW = 168
 CFG = {
-    "chunks": (((32, "S"), (48, (24, 24)), (48, (24, 24))),) * 2,
-    "labs": 500.0, "conv": "G", "margin": 500.0, "tol": 400.0, "gap": 100.0, "iscan": True, "sign": (1, 0), "dr": "G", "ksplit": 4, "lS": 0.0, "spreadA": "VS", "rounds": 3,
+    "chunks": (((32, "S"), (44, (44,)), (36, (10, 8, 8, 10)), (16, (16,))),) * 2, "pms": (0, 0), "cv": "GGGG",
+    "labs": 500.0, "conv": "GGVV", "cuts": (128, 1280, 2176, 2816, 3072), "bw": 180.0, "margin": 500.0, "tol": 400.0, "gap": 100.0, "iscan": True, "sign": (1, 0), "dr": "VGGG", "gs": 1, "sf": 110.0, "weave": "ggcgccgcgcgccggc", "late": 0, "ed": 1, "psplit": 0, "tied": (1, 1), "pc": 0.72, "pf": 5.0, "rl": 4000.0, "ksplit": 8, "lS": 0.0, "spreadA": "VS", "rounds": 3,
     "kgroups": ((0, 128),),
-    "p16": "V",
+    "p16": "K",
     "pen": "S",
-    "spread0": "VG",
+    "spread0": "VVG",
     "eq": ("VVVVVVVV", "VVVVSSSS", "VVVVSSSS"),
     "engines": 8,
-    "look": 40.0, "later": 2000.0, "hop": 90.0, "lead": -2000.0,
+    "look": 40.0, "later": 0.0, "hop": 90.0, "lead": -2000.0,
 }
+CFG.update({"sf": 65.0, "p16": "K", "later": 0.0, "cv": "VGVG", "spread0": "VVSG", "hop": 170.0, "bw": 350.0, "dr": "GGGG", "sign": (0, 0), "tol": 400.0, "look": 10.0,
+            "margin": 1e9, "tied": (1, 1), "psplit": 2, "pms": (2, 2), "spreadA": "VS", "rounds": 2, "weave": "ggcgccgcgcgcgcggc", "late": 1, "rl": 2500.0,
+            "conv": "GGGV", "ksplit": 16, "chunks": (((32, "S"), (44, (44,)), (32, (8, 6, 6, 6, 6)), (20, (20,))),) * 2})
 
-AR = {"af": ("float32", 14000), "ab": ("bfloat16", 44000), "ai": ("int32", 3600), "au": ("uint16", 1200)}
+AR = {"af": ("float32", 12000), "ab": ("bfloat16", 48000), "ai": ("int32", 3600), "au": ("uint16", 1200)}
 SCRATCH = {k: ("sbuf", [128, n], d) for k, (d, n) in AR.items()}
 SCRATCH["ptab"] = ("sbuf", [128, W], "bfloat16")
 SCRATCH["ctab"] = ("sbuf", [128, W], "float32")
@@ -49,6 +52,8 @@ def rank_program(g, core, T, topo):
     fill = {k: 0 for k in AR}
     names = {}
     bonus = [0.0]
+    line = [None]
+    gate = []
     psum = {k for k in SCRATCH if SCRATCH[k][0] == "psum"}
 
     def al(name, n, kind):
@@ -136,7 +141,10 @@ def rank_program(g, core, T, topo):
         for x in wr:
             acc[x[0]] = [e for e in acc.get(x[0], []) if e[0] == i or not covers(x, e[1])]
             acc[x[0]].append((i, x, True))
-        ops.append({"eng": eng, "emit": emit, "deps": deps, "busy": busy, "lat": lat, "sem": sem, "tdeps": list(extra), "bonus": bonus[0], "tag": CFG["tagf"]() if "tagf" in CFG else 0})
+        if eng == "V" and line[0] is not None:
+            extra = list(extra) + line[0]
+            line[0] = [i]
+        ops.append({"eng": eng, "emit": emit, "deps": deps, "busy": busy, "lat": lat, "sem": sem, "tdeps": list(extra) + gate, "bonus": bonus[0], "tag": CFG["tagf"]() if "tagf" in CFG else 0})
         return i
 
     def vdur(out, ins, two=False):
@@ -185,7 +193,7 @@ def rank_program(g, core, T, topo):
             if scale is not None:
                 kw["scale"] = ap(scale) if isinstance(scale, tuple) else scale
             return g.scalar.activation(ap(out), ap(a), func, **kw)
-        add("S", emit, rd, [out], 65 + CYC * width(out) * (GX if len(a) == 2 else 1))
+        add("S", emit, rd, [out], CFG["sf"] + CYC * width(out) * (GX if len(a) == 2 else 1))
 
     def mm(out, parts, start=True, stop=True, outs=None):
         n = len(parts)
@@ -194,7 +202,7 @@ def rank_program(g, core, T, topo):
         for (a, b) in parts:
             rd += [a, b]
             f = 4 if a[0] == "af" else 1
-            dur += 0.72 * f * max(min(64, width(a)), width(b)) + 5
+            dur += CFG["pc"] * f * max(min(64, width(a)), width(b)) + CFG["pf"]
 
         def emit():
             ins = None
@@ -209,6 +217,12 @@ def rank_program(g, core, T, topo):
 
     def asel(out, a, pat, cop, fillv, base, cm):
         add("G", lambda: g.affine_select(ap(out), ap(a), pat, cop, fillv, base, cm), [a], [out], 170 + 2 * CYC * width(out))
+
+    def conv(who, out, a):
+        if who == "V":
+            cp(out, a)
+        else:
+            asel(out, a, [[0, width(out)]], OP.is_ge, 0.0, 1, 0)
 
     ysem = [0]
     ylast = []
@@ -239,30 +253,36 @@ def rank_program(g, core, T, topo):
     al("thi", 1, I)
     al("r0i", 1024, I)
     RT = 128
-    cuts = (RT, 1024, 2048, M0)
-    loads = [(v("wi"), lambda: T.w[:], 2000), (v("qsb"), lambda: T.q[:], 3000), (v("cint", 0, RT), lambda: T.ch[:, 0:RT], 3300),
-             (v("r0i", p=8), lambda: T.r0[:], 3400), (v("ptab", 0, M0), lambda: T.pt[:], 7000), (v("thi"), lambda: T.th[:], 7000)]
-    for k in range(3):
-        loads.append((v("cint", cuts[k], cuts[k + 1]), lambda k=k: T.ch[:, cuts[k]:cuts[k + 1]], 9500 + 2500 * k))
-    for (o, src, lat) in loads:
+    cuts = CFG["cuts"]
+    loads = [(v("wi"), lambda: T.w[:], 512), (v("qsb", 0, LN), lambda: T.q[:, 0:LN], 256 * LN), (v("cint", 0, RT), lambda: T.ch[:, 0:RT], 512 * RT),
+             (v("r0i", p=8), lambda: T.r0[:], 32768), (v("ptab", 0, M0), lambda: T.pt[:], 256 * M0)]
+    if CFG.get("extra"):
+        al("xtra", M0, B)
+        loads.append((v("xtra"), lambda: T.pt[:], 0))
+    for k in range(len(cuts) - 1):
+        loads.append((v("cint", cuts[k], cuts[k + 1]), lambda k=k: T.ch[:, cuts[k]:cuts[k + 1]], 512 * (cuts[k + 1] - cuts[k])))
+    loads += [(v("qsb", LN, VI * LN), lambda: T.q[:, LN:VI * LN], 768 * LN), (v("thi"), lambda: T.th[:], 512)]
+    lat = 2000.0
+    for (o, src, size) in loads:
+        lat += size / CFG["bw"]
         ylast.append(dma(lambda o=o: ap(o), src, [], [o], lat))
     del ylast[:]
 
     for nm, n, k in [("onesb", 128, B), ("onesf", 128, F), ("Ib", 128, B), ("If", 128, F), ("nI", 128, B), ("Ipen", 128, B), ("IU", 128, B), ("I128", 128, B),
-                     ("I256", 128, B), ("n8k", 128, B), ("r8k", 128, B), ("tri", 128, B), ("TriD", 128, B), ("dgl", 128, B), ("Blk", 128, B), ("maskL", 128, F),
-                     ("maskP", 128, F), ("mask3", 384, F), ("rhsC", 8, F), ("BS", 8, B), ("iT", 128, F), ("iT8", 128, F), ("maxR", 128, F), ("zk", 128, B),
-                     ("zk0", 128, F), ("zk1", 128, F), ("kc0", 128, F), ("KC", 128, B), ("XC", 384, B), ("xa", 128, I), ("e0", 128, F), ("e8", 128, F), ("xr", 128, F),
+                     ("I256", 128, B), ("n8k", 128, B), ("r8k", 128, B), ("tri", 128, B), ("TriD", 128, B), ("dgl", 128, B), ("Blk", 256, B), ("maskL", 128, F),
+                     ("zb", 128, B), ("mask3", 384, F), ("rhsC", 8, F), ("BS", 8, B), ("iT", 128, F), ("iT8", 128, F), ("maxR", 128, F), ("zk", 128, B),
+                     ("zk0", 128, F), ("zk1", 128, F), ("kc0", 128, F), ("KC", 128, B), ("XC", 768, B), ("xa", 128, I), ("e0", 128, F), ("e8", 128, F), ("xr", 128, F),
                      ("xs", 384, F), ("c16", 1, F), ("c17", 1, F), ("c18", 1, F), ("k1", 1, F), ("k2", 1, F), ("k3", 1, F), ("n16", 1, F),
                      ("RTb", 8, B), ("pf", 1, F), ("wf", 1, F), ("thf", 1, F), ("thr", 128, B), ("thv", 8, F), ("WS", 8, B), ("r0b", 1024, B), ("N0", 64, F), ("N0o", 64, F),
                      ("i1", 128, I), ("i2", 128, I), ("i3", 8, I), ("i4", 8, I), ("i5", 128, I), ("i6", 128, I), ("i8", 1, I), ("il", 80, I), ("lists", 80, S16),
-                     ("zs", 1024, B), ("sg1", 1024, B), ("SW", 1024, B), ("iob", 128, B), ("fr", PW, B), ("wb", 256, F), ("wr", 256, F), ("wc", 2, F), ("nw", 2, F),
+                     ("zs", 48, B), ("sg1", 8, F), ("SW", 1024, B), ("iob", 128, B), ("fr", PW, B), ("wb", 256, F), ("wr", 256, F), ("wc", 2, F), ("nw", 2, F),
                      ("Dw0", 128, B), ("Dw1", 128, B), ("FAR", 16, B), ("rm", 24, I), ("rm2", 64, I), ("rm3", 64, F), ("Er", 384, F), ("mor", 64, S16), ("u", 144, B)]:
         al(nm, n, k)
     ms(v("onesb"), 1.0)
     ms(v("onesf"), 1.0)
     asel(v("If"), v("onesf"), [[-1, 128]], OP.is_equal, 0.0, 0, 1)
     cp(v("Ib"), v("If"))
-    for nm, c in (("nI", -1.0), ("Ipen", PEN), ("IU", U), ("I128", 128.0), ("I256", 256.0), ("n8k", -8192.0)):
+    for nm, c in (("nI", -1.0), ("Ipen", PEN)):
         ts(v(nm), v("Ib"), c, OP.mult)
     ms(v("r8k", p=1), 8192.0)
     cp(v("wf"), v("wi"))
@@ -285,13 +305,11 @@ def rank_program(g, core, T, topo):
     iota(v("i1"), [[-1, 128]], 256, 1)
     ts(v("i2"), v("i1"), 15, OP.bitwise_and)
     ts(v("maskL"), v("i2"), 0.0, OP.is_equal)
-    for k in range(3):
-        cp(v("mask3", 128 * k, 128 * k + 128), v("maskL"))
     cp(v("pf"), v("i8"))
-    ts(v("maskP"), v("maskL"), v("pf"), OP.mult)
     iota(v("i5"), [[-16, 8], [0, 16]], 0, 1)
     ts(v("i6"), v("i5"), 4, OP.arith_shift_right)
-    ts(v("Blk"), v("i6"), 0.0, OP.is_equal)
+    ts(v("Blk", 0, 128), v("i6"), 0.0, OP.is_equal)
+    ts(v("Blk", 128, 256), v("Blk", 0, 128), -1.0, OP.mult)
     iota(v("iT"), [[0, 8], [1, 16]], 0, 0, True)
     ts(v("iT8"), v("iT"), -8.0, OP.add)
     ts(v("maxR"), v("iT"), 0.0, OP.is_equal, 3 * NONE, OP.mult)
@@ -302,10 +320,13 @@ def rank_program(g, core, T, topo):
     iota(v("kc0", p=2), [[0, 8], [4096, 16]], 4096, 0, True)
     asel(v("KC", p=2), v("kc0", p=2), [[0, 128]], OP.is_gt, -NONE, 0, 1)
     for k, (step, rows) in enumerate(((-16, ((17, 120.5, 0), (0, 1.0, -1))), (-16, ((17, -15.5, 0), (0, 1.0, -1), (8, -1.0, -1))),
-                                      (16, ((17, -256.0, 0), (18, -0.5, 0), (0, -1.0, -1), (8, -1.0, -1))))):
+                                      (16, ((17, -256.0, 0), (18, -0.5, 0), (0, -1.0, -1), (8, -1.0, -1))),
+                                      (-16, ((17, -128.0, 0), (18, -15.5, 0), (8, -1.0, -1))), (16, ((17, -128.0, 0), (18, -0.5, 0), (8, -1.0, -1))),
+                                      (0, ((17, 128 * PEN, 0), (0, -PEN, -1))))):
         x = v("XC", 128 * k, 128 * k + 128, p=32)
         iota(x, [[0, 8], [step, 16]], 0, 0, True)
-        asel(x, x, [[0, 128]], OP.is_equal, 0.0, -16, 1)
+        if step:
+            asel(x, x, [[0, 128]], OP.is_equal, 0.0, -16, 1)
         for (r, c, d) in rows:
             asel(x, x, [[d, 8], [0, 16]], OP.not_equal, c, -r, 1)
     cp(v("r0b", 0, 256, p=8), v("r0i", 0, 256, p=8))
@@ -317,8 +338,8 @@ def rank_program(g, core, T, topo):
         ts(v("N0o", 8 * h, 8 * h + 8), v("N0", 8 * h, 8 * h + 8), OFF, OP.add, KK, OP.mult)
     ms(v("ptab", 0, 1), 31.0)
     cp(v("ctab", 0, RT), v("cint", 0, RT))
-    for k in range(3):
-        if CFG["conv"] == "V":
+    for k in range(len(cuts) - 1):
+        if CFG["conv"][k] == "V":
             cp(v("ctab", cuts[k], cuts[k + 1]), v("cint", cuts[k], cuts[k + 1]))
         else:
             asel(v("ctab", cuts[k], cuts[k + 1]), v("cint", cuts[k], cuts[k + 1]), [[0, cuts[k + 1] - cuts[k]]], OP.is_ge, 0.0, 1, 0)
@@ -327,7 +348,7 @@ def rank_program(g, core, T, topo):
     for h in range(2):
         for nm, n, k in [("P16", 128, S16), ("mo", 8, S16), ("kS", 128, F), ("gm", 128, B), ("adm", 128, B), ("pen", 256, B), ("df", 2048, B), ("ad", 2048, B),
                          ("sc1", 128, F), ("sc2", 128, F), ("ins", 128, B), ("v20", 128, F), ("v21", 128, F), ("op", 8, F), ("s20", 128, F), ("TN", 16, I), ("ST", 16, I), ("DR", 16, B), ("DT", 128, B), ("mI", 8, I), ("E", 128, F),
-                         ("of", 8, F), ("kd", 8, F), ("As0", 128, F), ("As1", 128, F), ("a3", 128, B), ("b3", 128, B), ("s3", 128, F), ("np2", 8, F), ("sl0", 8, F),
+                         ("of", 8, F), ("kd", 8, F), ("As0", 128, F), ("As1", 128, F), ("a3", 128, B), ("b3", 256, B), ("s3", 128, F), ("np2", 8, F), ("sl0", 8, F),
                          ("DI", 32, I), ("PL", PW, B), ("z", 8, F), ("wi3", 32, B), ("fl", 8, F), ("bI", 8, I), ("oh", 128, B), ("nb16", 8, S16), ("S20", 256, I), ("S21", 256, I),
                          ("Kb", 128, F), ("Ks", 128, B), ("osc", 128, F), ("Ud", 128, B), ("EQ0", 1024, B), ("EQ1", 1024, B), ("ea", 1024, B),
                          ("Og", 256, F), ("PM", 1024, B)]:
@@ -336,7 +357,7 @@ def rank_program(g, core, T, topo):
         ms(v("DT%d" % h, p=32), 1.0)
         ms(v("PL%d" % h, PW - 8, PW), -1.0)
     for nm, n, k in [("ndf", 16, F), ("dl", 16, F), ("cand", 16, B), ("vals", 256, F), ("win", 16, F), ("wd", 16, F), ("wn", 16, F), ("of16", 16, S16), ("wg", 256, F),
-                     ("slt", 16, B), ("ownl", 128, B), ("ownc", 16, B), ("own0", 128, B), ("own1", 16, B)]:
+                     ("slt", 16, B), ("ED", 256, F), ("Pm", 128, B), ("rq", 128, B), ("pa", 1024, B), ("ownl", 128, B), ("ownc", 16, B), ("own0", 128, B), ("own1", 16, B)]:
         al(nm, n, k)
     al("q16a", 2048, B)
     for t in range(4):
@@ -350,20 +371,31 @@ def rank_program(g, core, T, topo):
 
     def late_constants():
         asel(v("tri"), v("onesb"), [[1, 128]], OP.is_gt, 0.0, 0, -1)
-        ts(v("TriD"), v("Ib"), -1024.0, OP.mult)
-        tt(v("TriD"), v("TriD"), v("tri"), OP.add)
-        ts(v("dgl"), v("Ib"), v("pf"), OP.mult)
+        asel(v("TriD"), v("tri"), [[-1, 128]], OP.not_equal, -1024.0, 0, 1)
+        iota(v("zb"), [[0, 128]], 0, 0, True)
+        iota(v("dgl"), [[0, 128]], 0, 1, True)
+        asel(v("dgl"), v("dgl"), [[-1, 128]], OP.is_equal, 0.0, 0, 1)
+        for nm, c in (("IU", U), ("I128", 128.0), ("I256", 256.0), ("n8k", -8192.0)):
+            asel(v(nm), v("zb"), [[-1, 128]], OP.not_equal, c, 0, 1)
+        for k in range(3):
+            asel(v("mask3", 128 * k, 128 * k + 128), v("maskL"), [[0, 128]], OP.is_ge, 0.0, 1, 0)
         for t in range(3):
             for h in range(2):
-                ts(v("Ik%d%d" % (t, h)), v("Ib"), float(M0 + 256 * t + 128 * h), OP.mult)
+                asel(v("Ik%d%d" % (t, h)), v("zb"), [[-1, 128]], OP.not_equal, float(M0 + 256 * t + 128 * h), 0, 1)
         cp(v("thf"), v("thi"))
         ts(v("thr"), v("onesf"), v("thf"), OP.mult)
         mm(v("msc0", 0, 8), [(v("thr"), v("RTb"))])
         ts(v("thv"), v("msc0", 0, 8), -128.0, OP.add, U, OP.mult)
-        iota(v("zs", p=16), [[0, 1024]], 0, 0, True)
-        asel(v("sg1", p=16), v("zs", p=16), [[-1, 8], [0, 128]], OP.not_equal, 1.0, 0, 1)
-        asel(v("SW", p=16), v("sg1", p=16), [[-1, 8], [0, 128]], OP.not_equal, 256.0, -8, 1)
+        iota(v("zs", p=16), [[0, 48]], 0, 0, True)
+        asel(v("sg1", p=16), v("zs", 0, 8, p=16), [[-1, 8]], OP.not_equal, 1.0, 0, 1)
+        asel(v("sg1", p=16), v("sg1", p=16), [[-1, 8]], OP.not_equal, 256.0, -8, 1)
+        for gg in range(8):
+            act(v("SW", 128 * gg, 128 * gg + 128, p=16), v("onesb", p=16), AF.Identity, scale=v("sg1", gg, gg + 1, p=16))
         iota(v("iob"), [[1, 128]], 0, 0, True)
+        asel(v("Pm"), v("onesb"), [[-1, 16], [-16, 8]], OP.is_equal, 0.0, 0, 1)
+        ts(v("il", 56, 57), v("i8"), 15, OP.bitwise_and)
+        ts(v("c16"), v("il", 56, 57), 8.0, OP.mult)
+        ts(v("lists", 48, 56), v("il", 0, 8), v("c16"), OP.add)
         iota(v("own0", p=2), [[0, 8], [1, 16]], 0, 0, True)
         asel(v("ownl", p=2), v("own0", p=2), [[0, 128]], OP.is_ge, 1.0, 0, -1)
         iota(v("own1", p=2), [[16, 16]], 0, 0, True)
@@ -434,7 +466,7 @@ def rank_program(g, core, T, topo):
         cp(v("rm", 0, 8 * n), o)
         r2 = v("rm2", 8 * j, 8 * j + 8 * n)
         ts(r2, v("rm", 0, 8 * n), 63, OP.bitwise_and)
-        tt(v("Er", 0, 128 * n), (r2, v("lists", 0, 8 * n)), v("mask3", 0, 128 * n), OP.mult)
+        tt(v("Er", 0, 128 * n), (r2, v("lists", 0, 8 * n)), v("mask3", 0, 128 * n) if n > 1 else v("maskL"), OP.mult)
         mm(o, zero + [(v("Er", 128 * k, 128 * k + 128), v("rhsC")) for k in range(n)], True, True, [o] * len(zero) + outs)
         ts(v("mor", 8 * j, 8 * j + 8 * n), o, 1.0, OP.add)
         ts(v("rm3", 8 * j, 8 * j + 8 * n), r2, 1.0 - NONE, OP.add)
@@ -442,8 +474,9 @@ def rank_program(g, core, T, topo):
     def receive(t):
         RV, u = "RV%d" % t, v("u")
         tt(u, (v(RV), LNF), v("FT%d" % t), OP.mult)
+        act(v("rq"), (v(RV), v("lists", 48, 56)), AF.Copy)
         m = v("msc0", 0, 128)
-        mm(m, [(v(RV, 0, 128), v("Ib")), (v("u", 0, 128), v("Ib"))])
+        mm(m, [(v("rq"), v("Ib")), (v("u", 0, 128), v("Ib"))])
         act(v("lq%d" % t), m, AF.Copy)
         o = v("lst0", 0, 8)
         mm(o, [(v("IU"), v(RV, 128, 136)), (v("IU"), v("u", 128, 136))])
@@ -459,7 +492,7 @@ def rank_program(g, core, T, topo):
     def lanes_of(t, h):
         nm, o = qv(t, h)
         m = v("msc%d" % h, 0, 128)
-        mm(m, [(v(nm, o, o + 128), v("Ib"))])
+        mm(m, [(v(nm, o, o + 128), v("Pm"))])
         act(v("PL%d" % h, 0, 128), m, AF.Copy)
 
     def root(t, h):
@@ -472,11 +505,10 @@ def rank_program(g, core, T, topo):
         mm(mz, [(v("nI"), v(nm, o, o + 128)), (v("Ib"), v("gm" + hs))])
         act(v("adm" + hs), mz, AF.Abs)
         m3, m2 = v("msc" + hs, 128, 256), v("msc" + hs, 256, 264)
-        mm(m3, [(v("onesb", p=2), v("zk", p=2)), (v("adm" + hs), v("Blk"))])
-        mm(m2, [(v("adm" + hs), v("BS"))])
+        mm(m3, [(v("onesb", p=2), v("zk", p=2)), (v("adm" + hs), v("Blk", 0, 128))])
+        mm(m2, [(v("If"), v("rm3", 8 * j, 8 * j + 8)), (v("adm" + hs), v("BS"))])
         act(As, m3, AF.Abs, scale=U * KK)
-        tt(v("kd" + hs), m2, v("rm3", 8 * j, 8 * j + 8), OP.add)
-        tt(v("ST" + hs, 8, 16), v("kd" + hs), v("N0", n0, n0 + 8), OP.min)
+        tt(v("ST" + hs, 8, 16), m2, v("N0", n0, n0 + 8), OP.min)
         tt(v("pen" + hs, 0, 128), (v("N0o", n0, n0 + 8), L0), As, OP.is_lt)
 
     def push(t, h, s):
@@ -495,10 +527,15 @@ def rank_program(g, core, T, topo):
         if how != "K":
             act(kS, (ch, mo), AF.Copy)
         if how == "K":
-            cp(P16, (ch, mo))
+            src, c = v("cint") if (t, s) == (0, 1) else ch, CFG["psplit"]
+            if c:
+                cp(v("P16" + hs, 16 * c, 128), (src, (mo[0], mo[1] + c, mo[2], 1, 128)))
+                cp(v("P16" + hs, 0, 16 * c), (src, (mo[0], mo[1], mo[1] + c, 1, 128)))
+            else:
+                cp(P16, (src, mo))
             asel(kS, P16, [[0, 128]], OP.is_ge, 0.0, 1, 0)
         elif how == "V":
-            cp(P16, (ch, mo))
+            cp(P16, (v("cint") if (t, s) == (0, 1) else ch, mo))
         elif how == "S":
             cp(P16, kS)
         elif how == "G":
@@ -506,6 +543,7 @@ def rank_program(g, core, T, topo):
         else:
             for c in (0, 64):
                 asel(v("P16" + hs, c, c + 64), v("kS" + hs, c, c + 64), [[0, 64]], OP.is_ge, 0.0, 1, 0)
+        yield
         pens = [v("pen" + hs, 0, 128)]
         if s > 0:
             m = v("msc" + hs, 0, 128, p=16)
@@ -517,6 +555,17 @@ def rank_program(g, core, T, topo):
             if s < 3:
                 act(As, v("msc" + hs, 128, 256), AF.Abs, scale=U * KK)
             pens.append(v("pen" + hs, 128, 256))
+        if s == 2:
+            x, DT = v("msc" + hs, 256, 512), v("DT" + hs, p=19)
+            mm(x, [(v("adm" + hs), v("Blk")), (DT, v("XC", 384, 640, p=19))])
+            act(v("b3" + hs), x, AF.Relu)
+            k00 = v("lst" + hs, 128, 256)
+            mm(k00, [(v("If"), v("v20" + hs))], True, False)
+            mm(k00, [(v("Ipen"), v("a3" + hs)), (DT, v("XC", 640, 768, p=19))], False, False)
+            mm(k00, [(v("Ipen"), v("b3" + hs, 0, 128)), (v("Ipen"), v("b3" + hs, 128, 256))], False, True)
+            keep, line[0] = line[0], None
+            scan(v("s3" + hs), v("maxR"), k00, NONE, OP.max, OP.min)
+            line[0] = keep
         mm(key, [(v("onesb", p=2), v("KC", p=2))], True, False)
         mm(key, [(kS, v("If"))], False, False)
         mm(key, [(v("Ipen"), x) for x in pens], False, False)
@@ -540,6 +589,7 @@ def rank_program(g, core, T, topo):
                 for w in who:
                     tt(v("df" + hs, 16 * c0, 16 * (c0 + w)), (pt, v("P16" + hs, c0, c0 + w)), v(q16(t, h), 16 * c0, 16 * (c0 + w)), OP.subtract)
                     c0 += w
+                    yield
                 bonus[0] = save - CFG["labs"]
                 act(ad, df, AF.Abs)
         bonus[0] = save
@@ -547,8 +597,10 @@ def rank_program(g, core, T, topo):
             for i0 in range(0, 16, CFG["ksplit"]):
                 rows = range(i0, i0 + CFG["ksplit"])
                 mm(key, [(v("ad" + hs, 16 * a + i, 16 * b, 16), v("BS")) for i in rows], False, b == 128 and 15 in rows, [v(kb, k0 + i, k0 + 128, 16, (a, b)) for i in rows])
+        yield
         sc1, sc2, v2 = "sc1" + hs, ("sc2" if s else "s20") + hs, v("v2%d" % min(s, 1) + hs)
         scan(v(sc1), v("maxR"), key, NONE, OP.max, OP.min)
+        yield
         k15 = v(sc1, 15, 128, 16)
         of = v("of" + hs)
         t1, nn, both, so = v(TN, 0, 8), v(TN, 8, 16), v(TN), v(sc2)
@@ -560,35 +612,38 @@ def rank_program(g, core, T, topo):
             ts(of, nn, OFF, OP.add, -KK, OP.mult)
         elif s < 3:
             ts(of, k15, OFF, OP.add, -KK, OP.mult)
-        if s < 3:
-            tt(v("ins" + hs), (of, L0), As, OP.add)
-            tt(v2, key, v("ins" + hs), OP.max)
-            scan(so, v("maxR"), v2, NONE, OP.max, OP.min)
-            src = (so[0], so[1] + 15, so[2], 16, 128)
-            if s == 2:
-                tt(t1, src, v("sl0" + hs), OP.min)
-            elif not CFG["iscan"]:
-                cp(t1, src)
-            ts(v("mI" + hs), t1, 4095, OP.bitwise_and)
-            tolist(h, v("mI" + hs), v("mo" + hs))
-        if s > 0:
+        if s == 3 or (s > 0 and CFG["late"] < 2):
             tt(nn, v(ST, 8, 16), k15, OP.min)
-        if s < 3:
+        if s == 3:
+            return
+        yield
+        tt(v("ins" + hs), (of, L0), As, OP.add)
+        yield
+        tt(v2, key, v("ins" + hs), OP.max)
+        yield
+        scan(so, v("maxR"), v2, NONE, OP.max, OP.min)
+        yield
+        if s == 2:
+            tt(t1, t1, v("s3" + hs, 15, 128, 16), OP.min)
+        ts(v("mI" + hs), t1, 4095, OP.bitwise_and)
+        if CFG["late"] < 1:
             ts(v(ST), both, STRIP, OP.bitwise_and)
-            if CFG["dr"] == "V":
-                cp(v("DR" + hs), v(ST))
-            else:
-                asel(v("DR" + hs), v(ST), [[0, 16]], OP.is_ge, 0.0, 1, 0)
+        yield
+        E, o8 = v("E" + hs), v("lst" + hs, 0, 8)
+        tt(E, (v("mI" + hs), L0), v("maskL"), OP.mult)
+        mm(o8, [(E, v("rhsC"))])
+        yield
+        cp(v("mo" + hs), o8)
+        if CFG["late"] > 0:
+            if s > 0 and CFG["late"] == 2:
+                tt(nn, v(ST, 8, 16), k15, OP.min)
+            ts(v(ST), both, STRIP, OP.bitwise_and)
+        conv(CFG["dr"][t], v("DR" + hs), v(ST))
+        keep, line[0] = line[0], None
         if s == 0:
             tt(v("a3" + hs), (so, L15), v2, OP.is_ge)
-        if s == 1:
-            ts(v("op" + hs), of, -1.0, OP.mult)
-            tt(v("b3" + hs), (v("op" + hs), L0), v("As0" + hs), OP.is_lt)
-            ts(v("np2" + hs), t1, NONE, OP.is_lt, 4 * NONE, OP.mult)
-            k00 = v("lst" + hs, 128, 256)
-            mm(k00, [(v("If"), v("v20" + hs)), (v("Ipen"), v("a3" + hs)), (v("Ipen"), v("b3" + hs))])
-            scan(v("s3" + hs), v("maxR"), k00, NONE, OP.max, OP.min)
-            tt(v("sl0" + hs), v("np2" + hs), v("s3" + hs, 15, 128, 16), OP.add)
+        line[0] = keep
+
 
     def digits(t, h):
         hs = str(h)
@@ -600,7 +655,7 @@ def rank_program(g, core, T, topo):
         ts(v(DI, 8, 16), Nn, 255, OP.bitwise_and)
         ts(v(DI, 16, 24), Nn, 4095, OP.bitwise_and, 8, OP.arith_shift_right)
         ts(v(DI, 0, 8), Nn, 17, OP.arith_shift_right)
-        cp(v(PL, 128, 152), v(DI, 0, 24))
+        conv(CFG["cv"][h], v(PL, 128, 152), v(DI, 0, 24))
         ts(v(PL, 152, 160), v(DI, 24, 32), 0.0, OP.is_gt, float(16 * rank), OP.mult)
 
     def wishes(t, h):
@@ -614,22 +669,28 @@ def rank_program(g, core, T, topo):
         mm(m, [(v(PL, 136, 152), v("Ib"))])
         act(v("Ud" + hs, p=16), m, AF.Copy)
         ndf = v("ndf", 8 * h, 8 * h + 8)
-        cp(ndf, v(DI, 24, 32))
+        conv(CFG["cv"][2 + h], ndf, v(DI, 24, 32))
         ts(v("bI" + hs), v("TN" + hs, 8, 16), 21, OP.arith_shift_right)
         oh = v("oh" + hs)
         tt(oh, (v("bI" + hs), L0), v("iT8"), OP.is_equal)
         tt(v("fl" + hs), v("FAR", 8 * h, 8 * h + 8), ndf, OP.min)
         ts(v("dl", 8 * h, 8 * h + 8), ndf, v("pf"), OP.subtract, float(M0 + 256 * t + 128 * h), OP.subtract)
+        if CFG["ed"]:
+            tt(v("ED", 128 * h, 128 * h + 128), (v("dl", 8 * h, 8 * h + 8), L0), v("maskL"), OP.mult)
         for k, bank in enumerate(("key" + hs, "dif" + hs)):
             for gg in range(4 * k, 4 * k + 4):
                 c = 128 * (gg % 4)
                 mm(v(bank, c, c + 128), [(v("SW", 128 * gg, 128 * gg + 128, p=16), v("Ud" + hs, p=16))])
+        last = len(ops) - 1
         x = v("msc" + hs, 128, 256)
         mm(x, [(v("onesb", p=1), v("r8k", p=1)), (v("n8k"), oh), (v("Ks" + hs), v("Ib")) if CFG["sign"][h] else (v("Kb" + hs), v("If"))])
         scan(v("osc" + hs), v("maxR"), x, NONE, OP.max, OP.min)
         tt(v("cand", 8 * h, 8 * h + 8), v("osc" + hs, 15, 128, 16), v("fl" + hs), OP.is_lt)
         d = v("msc" + hs, 256, 384)
-        mm(d, [(oh, v("dgl")), (oh, v("Ik%d%d" % (t, h))), (v("If"), v("Kb" + hs))])
+        gate.append(last)
+        mm(d, [(oh, v("dgl")), (oh, v("Ik%d%d" % (t, h)))], True, False)
+        mm(d, [(v("If"), v("Kb" + hs))], False, True)
+        del gate[:]
         act(v("vals", 128 * h, 128 * h + 128), d, AF.Copy)
 
     def equal(a, b, how):
@@ -659,8 +720,11 @@ def rank_program(g, core, T, topo):
 
     def grow(t):
         ts(v("win"), v("lst1", 0, 16), 0.0, OP.is_lt)
-        tt(v("wd"), v("win"), v("dl"), OP.mult)
-        tt(v("Er", 0, 256), (v("wd"), v("lists", 0, 16)), v("mask3", 0, 256), OP.mult)
+        if CFG["ed"]:
+            tt(v("Er", 0, 256), (v("win"), v("lists", 0, 16)), v("ED"), OP.mult)
+        else:
+            tt(v("wd"), v("win"), v("dl"), OP.mult)
+            tt(v("Er", 0, 256), (v("wd"), v("lists", 0, 16)), v("mask3", 0, 256), OP.mult)
         o = v("lst0", 0, 16)
         mm(o, [(v("ownl", p=2), v("ownc", p=2)), (v("Er", 0, 128), v("rhsC")), (v("Er", 128, 256), v("rhsC"))], True, True, [o, v("lst0", 0, 8), v("lst0", 8, 16)])
         ts(v("of16"), o, float(M0 + 256 * t), OP.add)
@@ -694,43 +758,64 @@ def rank_program(g, core, T, topo):
         mm(o, [(v("TriD"), v("FAR")), (v("onesb"), v("FAR", 0, 8))], True, True, [o, v("msc0", 8, 16)])
         ts(v("slt"), o, 1024.0, OP.add)
         for h in (1, 0):
+            ns = CFG["pms"][h]
             for gg in range(8):
-                ts(v("PM%d" % h, 128 * gg, 128 * gg + 128), v("iob"), v("slt", 8 * h + gg, 8 * h + gg + 1), OP.is_equal)
+                col = v("slt", 8 * h + gg, 8 * h + gg + 1)
+                if gg < 8 - ns:
+                    ts(v("PM%d" % h, 128 * gg, 128 * gg + 128), v("iob"), col, OP.is_equal)
+                else:
+                    act(v("pa", 128 * gg, 128 * gg + 128), v("iob"), AF.Abs, bias=col, scale=-1.0)
+            if ns:
+                act(v("PM%d" % h, 1024 - 128 * ns, 1024), v("pa", 1024 - 128 * ns, 1024), AF.Relu, bias=1.0, scale=-1.0)
 
     def hand_on(t):
         o = v("msc1", 0, PW)
         mm(o, [(v("onesb", p=1), v("fr", p=1))], True, False)
         for h in (1, 0):
             for g0 in range(0, 8, 2):
-                parts, outs = [], []
-                for gg in range(g0, g0 + 2):
-                    pm = v("PM%d" % h, 128 * gg, 128 * gg + 128)
-                    parts += [(pm, v("PL%d" % h, 16 * gg, 16 * gg + 16)), (pm, v("PL%d" % h, 128 + gg, PW, 8))]
-                    outs += [v("msc1", 16 * gg, 16 * gg + 16), v("msc1", 128 + gg, PW, 8)]
-                mm(o, parts, False, h == 0 and g0 == 6, outs)
+                gs = range(g0, g0 + 2)
+                mm(o, [(v("PM%d" % h, 128 * gg, 128 * gg + 128), v("PL%d" % h, gg, PW, 8)) for gg in gs], False, h == 0 and g0 == 6, [v("msc1", gg, PW, 8) for gg in gs])
         act(v("SB%d" % (t + 1)), o, AF.Copy)
         j = send(v("RV%d" % (t + 1)), v("SB%d" % (t + 1)), right, "a%d" % (t + 1), "l%d" % (t + 1))
-        arrive(v("RV%d" % (t + 1)), left, "a%d" % (t + 1), j, 3000.0)
+        arrive(v("RV%d" % (t + 1)), left, "a%d" % (t + 1), j, CFG["rl"])
 
-    for h in range(2):
+    if CFG.get("early"):
+        al("wn0", 16, I)
+        arrive(v("wn0", 0, 1), right, "a0", send(v("wn0", 0, 1), v("wi"), left, "a0", "l0"), 3000.0)
+    for h in (1, 0):
         roots([(0, h)], "lst%d" % h)
         spread(0, h, CFG["spreadA"])
         begin(0, h)
         root(0, h)
-    for t in range(1, 4):
-        spread(t, 1, "G")
     for t in range(VI):
-        order = (0, 1) if t == 0 else (1, 0)
+        order = (1, 0)
+        ha, hb = order
+        run = {(h, s): push(t, h, s) for h in order for s in range(4)}
+        n_pieces = sum(len(who) for (n_l, who) in CFG["chunks"][0] if who != "S")
+
+        def weave(gathers, choice, tied):
+            line[0] = (line[0] or []) if tied else None
+            for x in CFG["weave"]:
+                which = gathers if x == "g" else choice
+                if which is not None:
+                    next(run[which], None)
+            line[0] = line[0] if tied else None
         for s in range(4):
-            for h in order:
-                bonus[0] = CFG["lead"] * h
-                push(t, h, s)
-                if s == 1 and t < 3:
-                    bonus[0] = 0.0
+            if s == 0:
+                weave((ha, 0), None, False)
+            weave((hb, s), (ha, s), CFG["tied"][0 if (s == 0 and t > 0) else 1])
+            weave((ha, s + 1) if s < 3 else None, (hb, s), s < 3 and CFG["tied"][1])
+            keep, line[0] = line[0], None
+            if s == 1 and t < 3:
+                for h in order:
                     lanes_of(t, h)
-            bonus[0] = 0.0
             if (t, s) == (0, 0):
                 late_constants()
+            if s == CFG["gs"] and t < 3:
+                gate.append(len(ops) - 1)
+                spread(t + 1, 1, "G")
+                begin(t + 1, 1)
+                del gate[:]
             if s == 0 and t > 0:
                 outputs(t - 1, 0)
                 parents(t - 1)
@@ -738,6 +823,7 @@ def rank_program(g, core, T, topo):
                 mm(v("msc0", 0, 8), [(v("Ib"), v("DR0", 0, 8))], False, True)
             if (t, s) == (0, 1):
                 roots([(1, 1), (2, 1), (3, 1)], "msc1")
+            line[0] = keep if s < 3 else None
         if t == 3:
             for h in order:
                 digits(t, h)
@@ -749,13 +835,13 @@ def rank_program(g, core, T, topo):
         wishes(t, 1)
         equal(1, 1, CFG["eq"][2])
         count(1, 1, True, False)
+        root(t + 1, 1)
         digits(t, 0)
         places()
         wishes(t, 0)
         if t > 0:
             carried(t)
         hand_on(t)
-        root(t + 1, 1)
         outputs(t, 1)
         equal(0, 1, CFG["eq"][1])
         equal(0, 0, CFG["eq"][0])
@@ -764,7 +850,6 @@ def rank_program(g, core, T, topo):
         count(0, 1, False, False, range(4, 8))
         count(0, 0, False, True, range(4, 8))
         grow(t)
-        begin(t + 1, 1)
         receive(t + 1)
         roots([(t + 1, 0)], "lst0")
         root(t + 1, 0)

from concourse.mybir import AluOpType, AxisListType, ActivationFunctionType

OP = AluOpType
AF = ActivationFunctionType
M0, LN, VI, W = 3072, 256, 4, 3840
U = 131072.0
NONE = 16777216.0
PEN = 268435456.0
OFF = 135.7 * U
KK = 4096.0
STRIP = ~(31 << 12)
BASE = 1.75
PW = 168
CFG = {
    "chunks": (((32, "S"), (44, (44,)), (36, (10, 8, 8, 10)), (16, (16,))),) * 2, "pms": (0, 0), "cv": "GGGG",
    "labs": 500.0, "conv": "GGVV", "cuts": (128, 1280, 2176, 2816, 3072), "bw": 180.0, "margin": 500.0, "tol": 400.0, "gap": 100.0, "iscan": True, "sign": (1, 0), "dr": "VGGG", "gs": 1, "sf": 110.0, "weave": "ggcgccgcgcgccggc", "late": 0, "ed": 1, "psplit": 0, "tied": (1, 1), "pc": 0.72, "pf": 5.0, "rl": 4000.0, "ksplit": 8, "lS": 0.0, "spreadA": "VS", "rounds": 3,
    "kgroups": ((0, 128),),
    "p16": "K",
    "pen": "S",
    "spread0": "VVG",
    "eq": ("VVVVVVVV", "VVVVSSSS", "VVVVSSSS"),
    "engines": 8,
    "look": 40.0, "later": 0.0, "hop": 90.0, "lead": -2000.0,
}
CFG.update({"sf": 65.0, "p16": "K", "later": 0.0, "cv": "VGVG", "spread0": "VVSG", "hop": 170.0, "bw": 350.0, "dr": "GGGG", "sign": (0, 0), "tol": 400.0, "look": 10.0,
            "margin": 1e9, "tied": (1, 1), "psplit": 2, "pms": (2, 2), "spreadA": "VS", "rounds": 2, "weave": "ggcgccgcgcgcgcggc", "late": 1, "rl": 2500.0,
            "conv": "GGGV", "ksplit": 16, "chunks": (((32, "S"), (44, (44,)), (32, (8, 6, 6, 6, 6)), (20, (20,))),) * 2})

AR = {"af": ("float32", 12000), "ab": ("bfloat16", 48000), "ai": ("int32", 3600), "au": ("uint16", 1200)}
SCRATCH = {k: ("sbuf", [128, n], d) for k, (d, n) in AR.items()}
SCRATCH["ptab"] = ("sbuf", [128, W], "bfloat16")
SCRATCH["ctab"] = ("sbuf", [128, W], "float32")
SCRATCH["cint"] = ("sbuf", [128, M0], "int32")
SCRATCH["qsb"] = ("sbuf", [128, VI * LN], "bfloat16")
for _h in range(2):
    for _b in ("key", "dif", "msc", "lst"):
        SCRATCH["%s%d" % (_b, _h)] = ("psum", [128, 512], "float32")
NY = 40
SEMAPHORES = ["sV", "sS", "sP", "sG"] + ["y%d" % k for k in range(NY)] + ["a1", "a2", "a3", "l1", "l2", "l3"]
CYC = 0.83
GX = 1.55


def rank_program(g, core, T, topo):
    rank = T.rank_of(core)
    if rank is None:
        return
    N = len(T.cores)
    HOP, LOOK, LATER = CFG["hop"], CFG["look"], CFG["later"]
    ops = []
    acc = {}
    fill = {k: 0 for k in AR}
    names = {}
    bonus = [0.0]
    line = [None]
    gate = []
    psum = {k for k in SCRATCH if SCRATCH[k][0] == "psum"}

    def al(name, n, kind):
        n2 = (n + 15) // 16 * 16
        b = fill[kind]
        fill[kind] = b + n2
        if fill[kind] > AR[kind][1]:
            raise ValueError("arena %s" % kind)
        names[name] = (kind, b, n)
        return name

    def v(name, lo=0, hi=None, st=1, p=128):
        if name in names:
            k, b, n = names[name]
        else:
            k, b, n = name, 0, SCRATCH[name][1][1]
        if hi is None:
            hi = n
        return (k, b + lo, b + hi, st, p)

    def ap(x):
        if len(x) == 2:
            return ap(x[0]).indirect(ap(x[1]))
        k, lo, hi, st, p = x
        p0, p1 = p if isinstance(p, tuple) else (0, p)
        t = T[k]
        if st == 1:
            return t[p0:p1, lo:hi]
        return t[p0:p1, lo:hi:st]

    def width(x):
        if len(x) == 2:
            return 16 * (x[1][2] - x[1][1])
        return len(range(x[1], x[2], x[3]))

    def is2(x):
        return len(x) == 5 and (x[0] in ("ab", "au", "ptab", "qsb"))

    def overlap(a, b):
        if a[1] >= b[2] or b[1] >= a[2]:
            return False
        if a[3] == b[3] and a[3] > 1 and (a[1] - b[1]) % a[3]:
            return False
        return True

    def covers(a, b):
        return (a[3] == 1 and a[1] <= b[1] and a[2] >= b[2]) or a[1:4] == b[1:4]

    def add(eng, emit, reads, writes, busy, lat=0.0, sem=None, extra=()):
        i = len(ops)
        deps = {}

        def dep(j):
            if j == i:
                return
            need = not (eng == "P" and ops[j]["eng"] == "P")
            deps[j] = deps.get(j, False) or need
        flat = []
        for x in reads:
            flat += list(x) if len(x) == 2 else [x]
        wr = []
        for x in writes:
            if len(x) == 2:
                wr.append(x[0])
                flat.append(x[1])
            else:
                wr.append(x)

        def norm(x):
            return (x[0], 0, 512, 1, 128) if x[0] in psum else x
        flat = [norm(x) for x in flat]
        wr = [norm(x) for x in wr]
        for x in flat:
            for (j, y, w) in acc.get(x[0], []):
                if w and overlap(x, y):
                    dep(j)
                elif not w and x[0] in psum and ops[j]["eng"] != eng:
                    dep(j)
        for x in wr:
            for (j, y, w) in acc.get(x[0], []):
                if overlap(x, y):
                    dep(j)
        for x in flat:
            acc.setdefault(x[0], []).append((i, x, False))
        for x in wr:
            acc[x[0]] = [e for e in acc.get(x[0], []) if e[0] == i or not covers(x, e[1])]
            acc[x[0]].append((i, x, True))
        if eng == "V" and line[0] is not None:
            extra = list(extra) + line[0]
            line[0] = [i]
        ops.append({"eng": eng, "emit": emit, "deps": deps, "busy": busy, "lat": lat, "sem": sem, "tdeps": list(extra) + gate, "bonus": bonus[0], "tag": CFG["tagf"]() if "tagf" in CFG else 0})
        return i

    def vdur(out, ins, two=False):
        n = width(out)
        for x in ins:
            if len(x) == 2:
                return 50 + GX * CYC * n
        if len(out) == 2:
            return 50 + 3.5 * CYC * width(out)
        c = 1.0
        if two and all(x[0] not in psum for x in ins):
            c = 2.0
        elif not two and is2(out) and all(is2(x) for x in ins):
            c = 0.5
        return 25 + CYC * max(64, c * n)

    def cp(out, a):
        add("V", lambda: g.vector.tensor_copy(ap(out), ap(a)), [a], [out], vdur(out, [a]))

    def tt(out, a, b, op):
        add("V", lambda: g.vector.tensor_tensor(ap(out), ap(a), ap(b), op), [a, b], [out], vdur(out, [a, b], True))

    def ts(out, a, s1, op0, s2=None, op1=None):
        rd = [a] + [s for s in (s1, s2) if isinstance(s, tuple)]

        def emit():
            s = ap(s1) if isinstance(s1, tuple) else s1
            if op1 is None:
                return g.vector.tensor_scalar(ap(out), ap(a), s, None, op0)
            return g.vector.tensor_scalar(ap(out), ap(a), s, ap(s2) if isinstance(s2, tuple) else s2, op0, op1)
        add("V", emit, rd, [out], vdur(out, [a]))

    def scan(out, d0, d1, init, op0, op1):
        add("V", lambda: g.vector.tensor_tensor_scan(ap(out), ap(d0), ap(d1), init, op0, op1), [d0, d1], [out], 25 + CYC * width(out))

    def ms(out, c):
        add("V", lambda: g.vector.memset(ap(out), c), [], [out], 25 + CYC * max(64, width(out) * (0.5 if is2(out) else 1)))

    def act(out, a, func, bias=None, scale=None):
        rd = [a] + [s for s in (bias, scale) if isinstance(s, tuple)]

        def emit():
            kw = {}
            if bias is not None:
                kw["bias"] = ap(bias) if isinstance(bias, tuple) else bias
            if scale is not None:
                kw["scale"] = ap(scale) if isinstance(scale, tuple) else scale
            return g.scalar.activation(ap(out), ap(a), func, **kw)
        add("S", emit, rd, [out], CFG["sf"] + CYC * width(out) * (GX if len(a) == 2 else 1))

    def mm(out, parts, start=True, stop=True, outs=None):
        n = len(parts)
        dur = 0.0
        rd = []
        for (a, b) in parts:
            rd += [a, b]
            f = 4 if a[0] == "af" else 1
            dur += CFG["pc"] * f * max(min(64, width(a)), width(b)) + CFG["pf"]

        def emit():
            ins = None
            for k, (a, b) in enumerate(parts):
                o = out if outs is None else outs[k]
                ins = g.tensor.matmul(ap(o), ap(a), ap(b), start and k == 0, stop and k == n - 1)
            return ins
        add("P", emit, rd, [out], dur, 30.0)

    def iota(out, pat, base, cm, fl=False):
        add("G", lambda: g.iota(ap(out), pat, base, cm, allow_small_or_imprecise_dtypes=True) if fl else g.iota(ap(out), pat, base, cm), [], [out], 130 + 2 * CYC * width(out))

    def asel(out, a, pat, cop, fillv, base, cm):
        add("G", lambda: g.affine_select(ap(out), ap(a), pat, cop, fillv, base, cm), [a], [out], 170 + 2 * CYC * width(out))

    def conv(who, out, a):
        if who == "V":
            cp(out, a)
        else:
            asel(out, a, [[0, width(out)]], OP.is_ge, 0.0, 1, 0)

    ysem = [0]
    ylast = []

    def dma(out_fn, in_fn, reads, writes, lat):
        s = "y%d" % ysem[0]
        ysem[0] += 1
        i = add("Y", lambda: g.sync.dma_start(out_fn(), in_fn()), reads, writes, 60.0, lat, (s, 16), ylast[-1:])
        return i

    right, left = T.cores[(rank + 1) % N], T.cores[(rank - 1) % N]

    def engs(a, b):
        return topo.engines(a, b)[:CFG["engines"]]

    def send(out, a, dst, rsem, lsem):
        es = engs(core, dst)
        mk = sum(1 << e for e in es)
        rid, pid = topo.addr(dst)[:2]
        return add("G", lambda: (g.remote_dma(ap(out), ap(a), T.sem[rsem], T.sem[lsem], pid, rid, mk), None)[1], [a], [], 900.0, 0.0, (lsem, len(es)))

    def arrive(out, src, rsem, after, lat):
        n = len(engs(src, core))
        return add("R", None, [], [out], 0.0, lat, (rsem, n), [after])

    F, B, I, S16 = "af", "ab", "ai", "au"
    al("wi", 1, I)
    al("thi", 1, I)
    al("r0i", 1024, I)
    RT = 128
    cuts = CFG["cuts"]
    loads = [(v("wi"), lambda: T.w[:], 512), (v("qsb", 0, LN), lambda: T.q[:, 0:LN], 256 * LN), (v("cint", 0, RT), lambda: T.ch[:, 0:RT], 512 * RT),
             (v("r0i", p=8), lambda: T.r0[:], 32768), (v("ptab", 0, M0), lambda: T.pt[:], 256 * M0)]
    if CFG.get("extra"):
        al("xtra", M0, B)
        loads.append((v("xtra"), lambda: T.pt[:], 0))
    for k in range(len(cuts) - 1):
        loads.append((v("cint", cuts[k], cuts[k + 1]), lambda k=k: T.ch[:, cuts[k]:cuts[k + 1]], 512 * (cuts[k + 1] - cuts[k])))
    loads += [(v("qsb", LN, VI * LN), lambda: T.q[:, LN:VI * LN], 768 * LN), (v("thi"), lambda: T.th[:], 512)]
    lat = 2000.0
    for (o, src, size) in loads:
        lat += size / CFG["bw"]
        ylast.append(dma(lambda o=o: ap(o), src, [], [o], lat))
    del ylast[:]

    for nm, n, k in [("onesb", 128, B), ("onesf", 128, F), ("Ib", 128, B), ("If", 128, F), ("nI", 128, B), ("Ipen", 128, B), ("IU", 128, B), ("I128", 128, B),
                     ("I256", 128, B), ("n8k", 128, B), ("r8k", 128, B), ("tri", 128, B), ("TriD", 128, B), ("dgl", 128, B), ("Blk", 256, B), ("maskL", 128, F),
                     ("zb", 128, B), ("mask3", 384, F), ("rhsC", 8, F), ("BS", 8, B), ("iT", 128, F), ("iT8", 128, F), ("maxR", 128, F), ("zk", 128, B),
                     ("zk0", 128, F), ("zk1", 128, F), ("kc0", 128, F), ("KC", 128, B), ("XC", 768, B), ("xa", 128, I), ("e0", 128, F), ("e8", 128, F), ("xr", 128, F),
                     ("xs", 384, F), ("c16", 1, F), ("c17", 1, F), ("c18", 1, F), ("k1", 1, F), ("k2", 1, F), ("k3", 1, F), ("n16", 1, F),
                     ("RTb", 8, B), ("pf", 1, F), ("wf", 1, F), ("thf", 1, F), ("thr", 128, B), ("thv", 8, F), ("WS", 8, B), ("r0b", 1024, B), ("N0", 64, F), ("N0o", 64, F),
                     ("i1", 128, I), ("i2", 128, I), ("i3", 8, I), ("i4", 8, I), ("i5", 128, I), ("i6", 128, I), ("i8", 1, I), ("il", 80, I), ("lists", 80, S16),
                     ("zs", 48, B), ("sg1", 8, F), ("SW", 1024, B), ("iob", 128, B), ("fr", PW, B), ("wb", 256, F), ("wr", 256, F), ("wc", 2, F), ("nw", 2, F),
                     ("Dw0", 128, B), ("Dw1", 128, B), ("FAR", 16, B), ("rm", 24, I), ("rm2", 64, I), ("rm3", 64, F), ("Er", 384, F), ("mor", 64, S16), ("u", 144, B)]:
        al(nm, n, k)
    ms(v("onesb"), 1.0)
    ms(v("onesf"), 1.0)
    asel(v("If"), v("onesf"), [[-1, 128]], OP.is_equal, 0.0, 0, 1)
    cp(v("Ib"), v("If"))
    for nm, c in (("nI", -1.0), ("Ipen", PEN)):
        ts(v(nm), v("Ib"), c, OP.mult)
    ms(v("r8k", p=1), 8192.0)
    cp(v("wf"), v("wi"))
    iota(v("i3"), [[-16, 8]], 0, 1)
    ts(v("i4"), v("i3"), 4, OP.arith_shift_right)
    ts(v("rhsC"), v("i4"), 0.0, OP.is_equal)
    ts(v("WS"), v("rhsC"), v("wf"), OP.mult)
    ts(v("BS"), v("rhsC"), U, OP.mult)
    ts(v("RTb"), v("i3"), 0.0, OP.is_equal)
    iota(v("il", 0, 24), [[1, 24]], 0, 0)
    iota(v("il", 24, 32), [[16, 8]], 15, 0)
    iota(v("il", 32, 40), [[1, 8]], PW - 8, 0)
    iota(v("i8"), [[0, 1]], 0, 1)
    ts(v("il", 42, 43), v("i8"), 7, OP.bitwise_and)
    cp(v("il", 43, 44), v("il", 42, 43))
    ts(v("il", 40, 41), v("il", 42, 43), float(PW - 8), OP.add)
    cp(v("il", 41, 42), v("il", 42, 43))
    cp(v("lists", 0, 44), v("il", 0, 44))
    L0, L15, LNF, LZ = v("lists", 0, 8), v("lists", 24, 32), v("lists", 32, 41), v("lists", 42, 44)
    iota(v("i1"), [[-1, 128]], 256, 1)
    ts(v("i2"), v("i1"), 15, OP.bitwise_and)
    ts(v("maskL"), v("i2"), 0.0, OP.is_equal)
    cp(v("pf"), v("i8"))
    iota(v("i5"), [[-16, 8], [0, 16]], 0, 1)
    ts(v("i6"), v("i5"), 4, OP.arith_shift_right)
    ts(v("Blk", 0, 128), v("i6"), 0.0, OP.is_equal)
    ts(v("Blk", 128, 256), v("Blk", 0, 128), -1.0, OP.mult)
    iota(v("iT"), [[0, 8], [1, 16]], 0, 0, True)
    ts(v("iT8"), v("iT"), -8.0, OP.add)
    ts(v("maxR"), v("iT"), 0.0, OP.is_equal, 3 * NONE, OP.mult)
    ts(v("maxR"), v("maxR"), -2 * NONE, OP.add)
    ts(v("zk0"), v("iT"), -16.0, OP.mult)
    asel(v("zk1", p=2), v("zk0", p=2), [[0, 128]], OP.is_ge, -7.5, 0, -1)
    cp(v("zk", p=2), v("zk1", p=2))
    iota(v("kc0", p=2), [[0, 8], [4096, 16]], 4096, 0, True)
    asel(v("KC", p=2), v("kc0", p=2), [[0, 128]], OP.is_gt, -NONE, 0, 1)
    for k, (step, rows) in enumerate(((-16, ((17, 120.5, 0), (0, 1.0, -1))), (-16, ((17, -15.5, 0), (0, 1.0, -1), (8, -1.0, -1))),
                                      (16, ((17, -256.0, 0), (18, -0.5, 0), (0, -1.0, -1), (8, -1.0, -1))),
                                      (-16, ((17, -128.0, 0), (18, -15.5, 0), (8, -1.0, -1))), (16, ((17, -128.0, 0), (18, -0.5, 0), (8, -1.0, -1))),
                                      (0, ((17, 128 * PEN, 0), (0, -PEN, -1))))):
        x = v("XC", 128 * k, 128 * k + 128, p=32)
        iota(x, [[0, 8], [step, 16]], 0, 0, True)
        if step:
            asel(x, x, [[0, 128]], OP.is_equal, 0.0, -16, 1)
        for (r, c, d) in rows:
            asel(x, x, [[d, 8], [0, 16]], OP.not_equal, c, -r, 1)
    cp(v("r0b", 0, 256, p=8), v("r0i", 0, 256, p=8))
    asel(v("r0b", 256, 1024, p=8), v("r0i", 256, 1024, p=8), [[0, 768]], OP.is_ge, 0.0, 1, 0)
    mm(v("lst0", 0, 64), [(v("r0b", 128 * j, 128 * j + 128, p=8), v("Ib", 0, 8, p=8)) for j in range(1)], True, True, [v("lst0", 0, 8)])
    mm(v("lst1", 0, 64), [(v("r0b", 128, 256, p=8), v("Ib", 0, 8, p=8))], True, True, [v("lst1", 0, 8)])
    for h in range(2):
        ts(v("N0", 8 * h, 8 * h + 8), v("lst%d" % h, 0, 8), -128.0, OP.add, U, OP.mult)
        ts(v("N0o", 8 * h, 8 * h + 8), v("N0", 8 * h, 8 * h + 8), OFF, OP.add, KK, OP.mult)
    ms(v("ptab", 0, 1), 31.0)
    cp(v("ctab", 0, RT), v("cint", 0, RT))
    for k in range(len(cuts) - 1):
        if CFG["conv"][k] == "V":
            cp(v("ctab", cuts[k], cuts[k + 1]), v("cint", cuts[k], cuts[k + 1]))
        else:
            asel(v("ctab", cuts[k], cuts[k + 1]), v("cint", cuts[k], cuts[k + 1]), [[0, cuts[k + 1] - cuts[k]]], OP.is_ge, 0.0, 1, 0)
    iota(v("ctab", M0, W), [[0, W - M0]], 0, 0, True)

    for h in range(2):
        for nm, n, k in [("P16", 128, S16), ("mo", 8, S16), ("kS", 128, F), ("gm", 128, B), ("adm", 128, B), ("pen", 256, B), ("df", 2048, B), ("ad", 2048, B),
                         ("sc1", 128, F), ("sc2", 128, F), ("ins", 128, B), ("v20", 128, F), ("v21", 128, F), ("op", 8, F), ("s20", 128, F), ("TN", 16, I), ("ST", 16, I), ("DR", 16, B), ("DT", 128, B), ("mI", 8, I), ("E", 128, F),
                         ("of", 8, F), ("kd", 8, F), ("As0", 128, F), ("As1", 128, F), ("a3", 128, B), ("b3", 256, B), ("s3", 128, F), ("np2", 8, F), ("sl0", 8, F),
                         ("DI", 32, I), ("PL", PW, B), ("z", 8, F), ("wi3", 32, B), ("fl", 8, F), ("bI", 8, I), ("oh", 128, B), ("nb16", 8, S16), ("S20", 256, I), ("S21", 256, I),
                         ("Kb", 128, F), ("Ks", 128, B), ("osc", 128, F), ("Ud", 128, B), ("EQ0", 1024, B), ("EQ1", 1024, B), ("ea", 1024, B),
                         ("Og", 256, F), ("PM", 1024, B)]:
            if not (nm == "EQ0" and h == 1):
                al(nm + str(h), n, k)
        ms(v("DT%d" % h, p=32), 1.0)
        ms(v("PL%d" % h, PW - 8, PW), -1.0)
    for nm, n, k in [("ndf", 16, F), ("dl", 16, F), ("cand", 16, B), ("vals", 256, F), ("win", 16, F), ("wd", 16, F), ("wn", 16, F), ("of16", 16, S16), ("wg", 256, F),
                     ("slt", 16, B), ("ED", 256, F), ("Pm", 128, B), ("rq", 128, B), ("pa", 1024, B), ("ownl", 128, B), ("ownc", 16, B), ("own0", 128, B), ("own1", 16, B)]:
        al(nm, n, k)
    al("q16a", 2048, B)
    for t in range(4):
        al("q16b%d" % t, 2048, B)
        if t > 0:
            for nm, n in (("FT", 144), ("RV", PW), ("SB", PW), ("lq", 128)):
                al("%s%d" % (nm, t), n, B)
        if t < 3:
            for h in range(2):
                al("Ik%d%d" % (t, h), 128, B)

    def late_constants():
        asel(v("tri"), v("onesb"), [[1, 128]], OP.is_gt, 0.0, 0, -1)
        asel(v("TriD"), v("tri"), [[-1, 128]], OP.not_equal, -1024.0, 0, 1)
        iota(v("zb"), [[0, 128]], 0, 0, True)
        iota(v("dgl"), [[0, 128]], 0, 1, True)
        asel(v("dgl"), v("dgl"), [[-1, 128]], OP.is_equal, 0.0, 0, 1)
        for nm, c in (("IU", U), ("I128", 128.0), ("I256", 256.0), ("n8k", -8192.0)):
            asel(v(nm), v("zb"), [[-1, 128]], OP.not_equal, c, 0, 1)
        for k in range(3):
            asel(v("mask3", 128 * k, 128 * k + 128), v("maskL"), [[0, 128]], OP.is_ge, 0.0, 1, 0)
        for t in range(3):
            for h in range(2):
                asel(v("Ik%d%d" % (t, h)), v("zb"), [[-1, 128]], OP.not_equal, float(M0 + 256 * t + 128 * h), 0, 1)
        cp(v("thf"), v("thi"))
        ts(v("thr"), v("onesf"), v("thf"), OP.mult)
        mm(v("msc0", 0, 8), [(v("thr"), v("RTb"))])
        ts(v("thv"), v("msc0", 0, 8), -128.0, OP.add, U, OP.mult)
        iota(v("zs", p=16), [[0, 48]], 0, 0, True)
        asel(v("sg1", p=16), v("zs", 0, 8, p=16), [[-1, 8]], OP.not_equal, 1.0, 0, 1)
        asel(v("sg1", p=16), v("sg1", p=16), [[-1, 8]], OP.not_equal, 256.0, -8, 1)
        for gg in range(8):
            act(v("SW", 128 * gg, 128 * gg + 128, p=16), v("onesb", p=16), AF.Identity, scale=v("sg1", gg, gg + 1, p=16))
        iota(v("iob"), [[1, 128]], 0, 0, True)
        asel(v("Pm"), v("onesb"), [[-1, 16], [-16, 8]], OP.is_equal, 0.0, 0, 1)
        ts(v("il", 56, 57), v("i8"), 15, OP.bitwise_and)
        ts(v("c16"), v("il", 56, 57), 8.0, OP.mult)
        ts(v("lists", 48, 56), v("il", 0, 8), v("c16"), OP.add)
        iota(v("own0", p=2), [[0, 8], [1, 16]], 0, 0, True)
        asel(v("ownl", p=2), v("own0", p=2), [[0, 128]], OP.is_ge, 1.0, 0, -1)
        iota(v("own1", p=2), [[16, 16]], 0, 0, True)
        asel(v("ownc", p=2), v("own1", p=2), [[0, 16]], OP.is_gt, 1.0, 0, 1)
        ms(v("fr", 0, PW - 8, p=1), 0.0)
        ms(v("fr", PW - 8, PW, p=1), 1.0)
        ms(v("wb", p=1), 1.0 / BASE)
        ms(v("wr", p=1), 0.0)
        scan(v("wr", p=1), v("wb", p=1), v("wr", p=1), BASE ** 120, OP.mult, OP.add)
        mm(v("msc1", 0, 2), [(v("wr", 0, 128, p=1), v("onesf", 0, 1, p=1))], True, True, [v("msc1", 0, 1)])
        ts(v("wc", 0, 1), v("msc1", 0, 1), BASE ** 8, OP.mult)
        mm(v("msc1", 0, 2), [(v("wr", 128, 256, p=1), v("onesf", 0, 1, p=1))], True, True, [v("msc1", 0, 1)])
        ts(v("wc", 1, 2), v("msc1", 0, 1), BASE ** 8, OP.mult)
        ts(v("nw"), v("wc"), -1.0, OP.mult)
        for h in range(2):
            ts(v("Dw%d" % h), v("Ib"), v("wc", h, h + 1), OP.mult, -2.55, OP.mult)
        o = v("msc0", 0, 48)
        mm(o, [(v("onesb", p=1), v("zs", 0, 48, p=1))] + [(v("r0b", 128 * j, 128 * j + 128, p=8), v("Ib", 0, 8, p=8)) for j in range(2, 8)], True, True,
           [o] + [v("msc0", 8 * j - 16, 8 * j - 8) for j in range(2, 8)])
        ts(v("N0", 16, 64), o, -128.0, OP.add, U, OP.mult)
        ts(v("N0o", 16, 64), v("N0", 16, 64), OFF, OP.add, KK, OP.mult)
        for t in range(1, 4):
            ms(v("FT%d" % t, 128, 144), 0.0)
            ts(v("FT%d" % t, 128, 136), v("N0", 16 * t, 16 * t + 8), 1.0 / U, OP.mult)
            mm(v("msc1", 0, 128), [(v("qsb", 256 * t, 256 * t + 128), v("Ib"))])
            act(v("FT%d" % t, 0, 128), v("msc1", 0, 128), AF.Copy)

    def qv(t, h):
        if h == 0 and t > 0:
            return ("lq%d" % t, 0)
        return ("qsb", 256 * t + 128 * h)

    def q16(t, h):
        return "q16a" if h == 0 else "q16b%d" % t

    def spread(t, h, how):
        nm, o = qv(t, h)
        for i in range(16):
            out, a = v(q16(t, h), i, 2048, 16), v(nm, o, o + 128)
            e = how[i % len(how)]
            if e == "G":
                asel(out, a, [[0, 128]], OP.is_ge, 0.0, 1, 0)
            elif e == "V":
                cp(out, a)
            else:
                act(out, a, AF.Copy)

    def tolist(h, win, dst, own=None):
        E = v("E%d" % h)
        o = v("lst%d" % h, 0, 8)
        tt(E, (win, L0), v("maskL"), OP.mult)
        if own is None:
            mm(o, [(E, v("rhsC"))])
            cp(dst, o)
        else:
            mm(o, [(v("maskP"), v("rhsC")), (E, v("rhsC"))])
            ts(dst, o, float(own), OP.add)

    RS = {(0, 0): 0, (0, 1): 1, (1, 1): 2, (2, 1): 3, (3, 1): 4, (1, 0): 5, (2, 0): 6, (3, 0): 7}

    def roots(which, bank):
        n, j = len(which), RS[which[0]]
        o = v(bank, 0, 8 * n)
        outs = [v(bank, 8 * k, 8 * k + 8) for k in range(n)]
        zero = [(v("onesb", p=1), v("zs", 0, 8 * n, p=1))] if n > 1 else []
        qs = [qv(t, h) for (t, h) in which]
        mm(o, zero + [(v(nm, c, c + 128), v("WS")) for (nm, c) in qs], True, True, [o] * len(zero) + outs)
        cp(v("rm", 0, 8 * n), o)
        r2 = v("rm2", 8 * j, 8 * j + 8 * n)
        ts(r2, v("rm", 0, 8 * n), 63, OP.bitwise_and)
        tt(v("Er", 0, 128 * n), (r2, v("lists", 0, 8 * n)), v("mask3", 0, 128 * n) if n > 1 else v("maskL"), OP.mult)
        mm(o, zero + [(v("Er", 128 * k, 128 * k + 128), v("rhsC")) for k in range(n)], True, True, [o] * len(zero) + outs)
        ts(v("mor", 8 * j, 8 * j + 8 * n), o, 1.0, OP.add)
        ts(v("rm3", 8 * j, 8 * j + 8 * n), r2, 1.0 - NONE, OP.add)

    def receive(t):
        RV, u = "RV%d" % t, v("u")
        tt(u, (v(RV), LNF), v("FT%d" % t), OP.mult)
        act(v("rq"), (v(RV), v("lists", 48, 56)), AF.Copy)
        m = v("msc0", 0, 128)
        mm(m, [(v("rq"), v("Ib")), (v("u", 0, 128), v("Ib"))])
        act(v("lq%d" % t), m, AF.Copy)
        o = v("lst0", 0, 8)
        mm(o, [(v("IU"), v(RV, 128, 136)), (v("IU"), v("u", 128, 136))])
        cp(v("N0", 16 * t, 16 * t + 8), o)
        ts(v("N0o", 16 * t, 16 * t + 8), o, OFF, OP.add, KK, OP.mult)

    def begin(t, h):
        nm, o = qv(t, h)
        hs = str(h)
        if t < 3:
            asel(v("ptab", M0 + 256 * t + 128 * h, M0 + 256 * t + 128 * h + 128), v(nm, o, o + 128), [[0, 128]], OP.is_ge, 0.0, 1, 0)

    def lanes_of(t, h):
        nm, o = qv(t, h)
        m = v("msc%d" % h, 0, 128)
        mm(m, [(v(nm, o, o + 128), v("Pm"))])
        act(v("PL%d" % h, 0, 128), m, AF.Copy)

    def root(t, h):
        hs = str(h)
        nm, o = qv(t, h)
        j, n0 = RS[(t, h)], 16 * t + 8 * h
        As = v("As0" + hs)
        act(v("gm" + hs), (v("ptab", 0, RT), v("mor", 8 * j, 8 * j + 8)), AF.Copy)
        mz = v("msc" + hs, 0, 128)
        mm(mz, [(v("nI"), v(nm, o, o + 128)), (v("Ib"), v("gm" + hs))])
        act(v("adm" + hs), mz, AF.Abs)
        m3, m2 = v("msc" + hs, 128, 256), v("msc" + hs, 256, 264)
        mm(m3, [(v("onesb", p=2), v("zk", p=2)), (v("adm" + hs), v("Blk", 0, 128))])
        mm(m2, [(v("If"), v("rm3", 8 * j, 8 * j + 8)), (v("adm" + hs), v("BS"))])
        act(As, m3, AF.Abs, scale=U * KK)
        tt(v("ST" + hs, 8, 16), m2, v("N0", n0, n0 + 8), OP.min)
        tt(v("pen" + hs, 0, 128), (v("N0o", n0, n0 + 8), L0), As, OP.is_lt)

    def push(t, h, s):
        hs = str(h)
        nm, o = qv(t, h)
        W1 = M0 + 256 * t
        j = RS[(t, h)]
        mo = v("mor", 8 * j, 8 * j + 8) if s == 0 else v("mo" + hs)
        ch, pt = v("ctab", 0, RT if s == 0 else W1), v("ptab", 0, W1)
        kb, k0 = "key" + hs, 0
        key = v(kb, k0, k0 + 128)
        TN, ST = "TN" + hs, "ST" + hs
        As = v("As%d" % min(s, 1) + hs)
        kS, P16 = v("kS" + hs), v("P16" + hs)
        how = CFG["p16"][s % len(CFG["p16"])]
        if how != "K":
            act(kS, (ch, mo), AF.Copy)
        if how == "K":
            src, c = v("cint") if (t, s) == (0, 1) else ch, CFG["psplit"]
            if c:
                cp(v("P16" + hs, 16 * c, 128), (src, (mo[0], mo[1] + c, mo[2], 1, 128)))
                cp(v("P16" + hs, 0, 16 * c), (src, (mo[0], mo[1], mo[1] + c, 1, 128)))
            else:
                cp(P16, (src, mo))
            asel(kS, P16, [[0, 128]], OP.is_ge, 0.0, 1, 0)
        elif how == "V":
            cp(P16, (v("cint") if (t, s) == (0, 1) else ch, mo))
        elif how == "S":
            cp(P16, kS)
        elif how == "G":
            asel(P16, kS, [[0, 128]], OP.is_ge, 0.0, 1, 0)
        else:
            for c in (0, 64):
                asel(v("P16" + hs, c, c + 64), v("kS" + hs, c, c + 64), [[0, 64]], OP.is_ge, 0.0, 1, 0)
        yield
        pens = [v("pen" + hs, 0, 128)]
        if s > 0:
            m = v("msc" + hs, 0, 128, p=16)
            mm(m, [(v("DR" + hs), v("Ib"))])
            act(v("DT" + hs, p=16), m, AF.Copy, scale=1.0 / U)
            lo = 0 if s < 3 else 128
            mm(v("msc" + hs, 128 + lo, 512), [(v("DT" + hs, p=19), v("XC", lo, 384, p=19))])
            act(v("pen" + hs), v("msc" + hs, 256, 512), AF.Relu)
            if s < 3:
                act(As, v("msc" + hs, 128, 256), AF.Abs, scale=U * KK)
            pens.append(v("pen" + hs, 128, 256))
        if s == 2:
            x, DT = v("msc" + hs, 256, 512), v("DT" + hs, p=19)
            mm(x, [(v("adm" + hs), v("Blk")), (DT, v("XC", 384, 640, p=19))])
            act(v("b3" + hs), x, AF.Relu)
            k00 = v("lst" + hs, 128, 256)
            mm(k00, [(v("If"), v("v20" + hs))], True, False)
            mm(k00, [(v("Ipen"), v("a3" + hs)), (DT, v("XC", 640, 768, p=19))], False, False)
            mm(k00, [(v("Ipen"), v("b3" + hs, 0, 128)), (v("Ipen"), v("b3" + hs, 128, 256))], False, True)
            keep, line[0] = line[0], None
            scan(v("s3" + hs), v("maxR"), k00, NONE, OP.max, OP.min)
            line[0] = keep
        mm(key, [(v("onesb", p=2), v("KC", p=2))], True, False)
        mm(key, [(kS, v("If"))], False, False)
        mm(key, [(v("Ipen"), x) for x in pens], False, False)
        l0 = 0
        save = bonus[0]
        for ci, (n_l, who) in enumerate(CFG["chunks"][h]):
            P = v("P16" + hs, l0, l0 + n_l)
            a, b = 16 * l0, 16 * (l0 + n_l)
            l0 += n_l
            df, ad, qq = v("df" + hs, a, b), v("ad" + hs, a, b), v(q16(t, h), a, b)
            bonus[0] = save - LATER
            if who == "S":
                bonus[0] = save - CFG["lS"]
                act(df, (pt, P), AF.Copy)
                d = v(("dif", "lst")[ci] + hs, 0, b - a)
                mm(d, [(v("nI"), qq)], True, False)
                mm(d, [(v("Ib"), df)], False, True)
                act(ad, d, AF.Abs)
            else:
                c0 = l0 - n_l
                for w in who:
                    tt(v("df" + hs, 16 * c0, 16 * (c0 + w)), (pt, v("P16" + hs, c0, c0 + w)), v(q16(t, h), 16 * c0, 16 * (c0 + w)), OP.subtract)
                    c0 += w
                    yield
                bonus[0] = save - CFG["labs"]
                act(ad, df, AF.Abs)
        bonus[0] = save
        for (a, b) in CFG["kgroups"]:
            for i0 in range(0, 16, CFG["ksplit"]):
                rows = range(i0, i0 + CFG["ksplit"])
                mm(key, [(v("ad" + hs, 16 * a + i, 16 * b, 16), v("BS")) for i in rows], False, b == 128 and 15 in rows, [v(kb, k0 + i, k0 + 128, 16, (a, b)) for i in rows])
        yield
        sc1, sc2, v2 = "sc1" + hs, ("sc2" if s else "s20") + hs, v("v2%d" % min(s, 1) + hs)
        scan(v(sc1), v("maxR"), key, NONE, OP.max, OP.min)
        yield
        k15 = v(sc1, 15, 128, 16)
        of = v("of" + hs)
        t1, nn, both, so = v(TN, 0, 8), v(TN, 8, 16), v(TN), v(sc2)
        if CFG["iscan"] and s < 3:
            S2 = "S2%d" % min(s, 1) + hs
            t1, nn, both, so = v(S2, 15, 128, 16), v(S2, 143, 256, 16), v(S2, 15, 256, 16), v(S2, 0, 128)
        if s == 0:
            tt(nn, v(ST, 8, 16), k15, OP.min)
            ts(of, nn, OFF, OP.add, -KK, OP.mult)
        elif s < 3:
            ts(of, k15, OFF, OP.add, -KK, OP.mult)
        if s == 3 or (s > 0 and CFG["late"] < 2):
            tt(nn, v(ST, 8, 16), k15, OP.min)
        if s == 3:
            return
        yield
        tt(v("ins" + hs), (of, L0), As, OP.add)
        yield
        tt(v2, key, v("ins" + hs), OP.max)
        yield
        scan(so, v("maxR"), v2, NONE, OP.max, OP.min)
        yield
        if s == 2:
            tt(t1, t1, v("s3" + hs, 15, 128, 16), OP.min)
        ts(v("mI" + hs), t1, 4095, OP.bitwise_and)
        if CFG["late"] < 1:
            ts(v(ST), both, STRIP, OP.bitwise_and)
        yield
        E, o8 = v("E" + hs), v("lst" + hs, 0, 8)
        tt(E, (v("mI" + hs), L0), v("maskL"), OP.mult)
        mm(o8, [(E, v("rhsC"))])
        yield
        cp(v("mo" + hs), o8)
        if CFG["late"] > 0:
            if s > 0 and CFG["late"] == 2:
                tt(nn, v(ST, 8, 16), k15, OP.min)
            ts(v(ST), both, STRIP, OP.bitwise_and)
        conv(CFG["dr"][t], v("DR" + hs), v(ST))
        keep, line[0] = line[0], None
        if s == 0:
            tt(v("a3" + hs), (so, L15), v2, OP.is_ge)
        line[0] = keep


    def digits(t, h):
        hs = str(h)
        Nn, DI, PL = v("TN" + hs, 8, 16), "DI" + hs, "PL" + hs
        ts(v(DI, 24, 32), Nn, 4095, OP.bitwise_and)
        if t < 3:
            tolist(h, v(DI, 24, 32), v("nb16" + hs))
            tt(v("FAR", 8 * h, 8 * h + 8), Nn, v("thv"), OP.is_ge)
        ts(v(DI, 8, 16), Nn, 255, OP.bitwise_and)
        ts(v(DI, 16, 24), Nn, 4095, OP.bitwise_and, 8, OP.arith_shift_right)
        ts(v(DI, 0, 8), Nn, 17, OP.arith_shift_right)
        conv(CFG["cv"][h], v(PL, 128, 152), v(DI, 0, 24))
        ts(v(PL, 152, 160), v(DI, 24, 32), 0.0, OP.is_gt, float(16 * rank), OP.mult)

    def wishes(t, h):
        hs = str(h)
        DI, PL = "DI" + hs, "PL" + hs
        col = (v("ctab", 0, M0 + 256 * t), v("nb16" + hs))
        if CFG["sign"][h]:
            act(v("Ks" + hs), col, AF.Sign)
        act(v("Kb" + hs), col, AF.Copy)
        m = v("msc" + hs, 0, 128, p=16)
        mm(m, [(v(PL, 136, 152), v("Ib"))])
        act(v("Ud" + hs, p=16), m, AF.Copy)
        ndf = v("ndf", 8 * h, 8 * h + 8)
        conv(CFG["cv"][2 + h], ndf, v(DI, 24, 32))
        ts(v("bI" + hs), v("TN" + hs, 8, 16), 21, OP.arith_shift_right)
        oh = v("oh" + hs)
        tt(oh, (v("bI" + hs), L0), v("iT8"), OP.is_equal)
        tt(v("fl" + hs), v("FAR", 8 * h, 8 * h + 8), ndf, OP.min)
        ts(v("dl", 8 * h, 8 * h + 8), ndf, v("pf"), OP.subtract, float(M0 + 256 * t + 128 * h), OP.subtract)
        if CFG["ed"]:
            tt(v("ED", 128 * h, 128 * h + 128), (v("dl", 8 * h, 8 * h + 8), L0), v("maskL"), OP.mult)
        for k, bank in enumerate(("key" + hs, "dif" + hs)):
            for gg in range(4 * k, 4 * k + 4):
                c = 128 * (gg % 4)
                mm(v(bank, c, c + 128), [(v("SW", 128 * gg, 128 * gg + 128, p=16), v("Ud" + hs, p=16))])
        last = len(ops) - 1
        x = v("msc" + hs, 128, 256)
        mm(x, [(v("onesb", p=1), v("r8k", p=1)), (v("n8k"), oh), (v("Ks" + hs), v("Ib")) if CFG["sign"][h] else (v("Kb" + hs), v("If"))])
        scan(v("osc" + hs), v("maxR"), x, NONE, OP.max, OP.min)
        tt(v("cand", 8 * h, 8 * h + 8), v("osc" + hs, 15, 128, 16), v("fl" + hs), OP.is_lt)
        d = v("msc" + hs, 256, 384)
        gate.append(last)
        mm(d, [(oh, v("dgl")), (oh, v("Ik%d%d" % (t, h)))], True, False)
        mm(d, [(v("If"), v("Kb" + hs))], False, True)
        del gate[:]
        act(v("vals", 128 * h, 128 * h + 128), d, AF.Copy)

    def equal(a, b, how):
        dst = "EQ%d%d" % (0 if a == b == 0 else 1, a)
        run = [gg for gg in range(8) if how[gg] == "S"]
        for gg in range(8):
            src = v(("key", "dif")[gg // 4] + str(b), 128 * (gg % 4), 128 * (gg % 4) + 128)
            col = v("ndf", 8 * a + gg, 8 * a + gg + 1)
            if how[gg] == "V":
                ts(v(dst, 128 * gg, 128 * gg + 128), src, col, OP.is_equal, v("wc", a, a + 1), OP.mult)
            else:
                act(v("ea%d" % b, 128 * gg, 128 * gg + 128), src, AF.Abs, bias=col, scale=-1.0)
        if run:
            lo, hi = 128 * run[0], 128 * run[-1] + 128
            act(v(dst, lo, hi), v("ea%d" % b, lo, hi), AF.Relu, bias=v("wc", a, a + 1), scale=v("nw", a, a + 1))

    def count(a, b, first, last, graphs=range(8)):
        dst = "EQ%d%d" % (0 if a == b == 0 else 1, a)
        o = v("lst1", 0, 16)
        parts, outs = [], []
        if first:
            parts, outs = [(v("onesb", p=1), v("zs", 0, 16, p=1))], [o]
        if a == b and 0 in graphs:
            parts, outs = parts + [(v("Dw%d" % b), v("cand", 8 * b, 8 * b + 8))], outs + [v("lst1", 8 * b, 8 * b + 8)]
        mm(o, parts + [(v(dst, 128 * gg, 128 * gg + 128), v("cand", 8 * a + gg, 8 * a + gg + 1)) for gg in graphs], first, last,
           outs + [v("lst1", 8 * b + gg, 8 * b + gg + 1) for gg in graphs])

    def grow(t):
        ts(v("win"), v("lst1", 0, 16), 0.0, OP.is_lt)
        if CFG["ed"]:
            tt(v("Er", 0, 256), (v("win"), v("lists", 0, 16)), v("ED"), OP.mult)
        else:
            tt(v("wd"), v("win"), v("dl"), OP.mult)
            tt(v("Er", 0, 256), (v("wd"), v("lists", 0, 16)), v("mask3", 0, 256), OP.mult)
        o = v("lst0", 0, 16)
        mm(o, [(v("ownl", p=2), v("ownc", p=2)), (v("Er", 0, 128), v("rhsC")), (v("Er", 128, 256), v("rhsC"))], True, True, [o, v("lst0", 0, 8), v("lst0", 8, 16)])
        ts(v("of16"), o, float(M0 + 256 * t), OP.add)
        cp((v("ctab", 0, M0 + 256 * t + 256), v("of16")), v("vals"))

    def parents(t):
        tt(v("wn"), v("win"), v("ndf"), OP.mult)
        for h in range(2):
            mm(v("msc1", 128 * h, 128 * h + 128, p=8), [(v("wn", 8 * h, 8 * h + 8), v("If"))])
        act(v("wg", p=8), v("msc1", 0, 256, p=8), AF.Copy)
        dma(lambda: T.yp[:, 256 * t:256 * t + 256], lambda: ap(v("wg", p=8)), [v("wg")], [], 2000)

    def carried(t):
        ts(v("z0"), v("DI0", 24, 32), 0.0, OP.is_equal)
        tt(v("wi30"), (v("z0"), LZ), v("RV%d" % t, 136, 168), OP.mult)
        tt(v("PL0", 136, 160), v("PL0", 136, 160), v("wi30", 0, 24), OP.add)

    def outputs(t, h):
        hs = str(h)
        PL = "PL" + hs
        a, b = v("msc" + hs, 0, 128, p=8), v("msc" + hs, 128, 256, p=8)
        mm(a, [(v("onesb", 0, 8), v("I128")), (v(PL, 128, 136), v("Ib"))])
        mm(b, [(v(PL, 136, 144), v("Ib")), (v(PL, 144, 152), v("I256")), (v(PL, 152, 160), v("I256"))])
        act(v("Og" + hs, p=8), v("msc" + hs, 0, 256, p=8), AF.Copy)
        c = 256 * t + 128 * h
        dma(lambda: T.yr[:, c:c + 128], lambda: ap(v("Og" + hs, 0, 128, p=8)), [v("Og" + hs)], [], 2000)
        dma(lambda: T.yb[:, c:c + 128], lambda: ap(v("Og" + hs, 128, 256, p=8)), [v("Og" + hs)], [], 2000)

    def places():
        o = v("msc0", 0, 16)
        mm(o, [(v("TriD"), v("FAR")), (v("onesb"), v("FAR", 0, 8))], True, True, [o, v("msc0", 8, 16)])
        ts(v("slt"), o, 1024.0, OP.add)
        for h in (1, 0):
            ns = CFG["pms"][h]
            for gg in range(8):
                col = v("slt", 8 * h + gg, 8 * h + gg + 1)
                if gg < 8 - ns:
                    ts(v("PM%d" % h, 128 * gg, 128 * gg + 128), v("iob"), col, OP.is_equal)
                else:
                    act(v("pa", 128 * gg, 128 * gg + 128), v("iob"), AF.Abs, bias=col, scale=-1.0)
            if ns:
                act(v("PM%d" % h, 1024 - 128 * ns, 1024), v("pa", 1024 - 128 * ns, 1024), AF.Relu, bias=1.0, scale=-1.0)

    def hand_on(t):
        o = v("msc1", 0, PW)
        mm(o, [(v("onesb", p=1), v("fr", p=1))], True, False)
        for h in (1, 0):
            for g0 in range(0, 8, 2):
                gs = range(g0, g0 + 2)
                mm(o, [(v("PM%d" % h, 128 * gg, 128 * gg + 128), v("PL%d" % h, gg, PW, 8)) for gg in gs], False, h == 0 and g0 == 6, [v("msc1", gg, PW, 8) for gg in gs])
        act(v("SB%d" % (t + 1)), o, AF.Copy)
        j = send(v("RV%d" % (t + 1)), v("SB%d" % (t + 1)), right, "a%d" % (t + 1), "l%d" % (t + 1))
        arrive(v("RV%d" % (t + 1)), left, "a%d" % (t + 1), j, CFG["rl"])

    if CFG.get("early"):
        al("wn0", 16, I)
        arrive(v("wn0", 0, 1), right, "a0", send(v("wn0", 0, 1), v("wi"), left, "a0", "l0"), 3000.0)
    for h in (1, 0):
        roots([(0, h)], "lst%d" % h)
        spread(0, h, CFG["spreadA"])
        begin(0, h)
        root(0, h)
    for t in range(VI):
        order = (1, 0)
        ha, hb = order
        run = {(h, s): push(t, h, s) for h in order for s in range(4)}
        n_pieces = sum(len(who) for (n_l, who) in CFG["chunks"][0] if who != "S")

        def weave(gathers, choice, tied):
            line[0] = (line[0] or []) if tied else None
            for x in CFG["weave"]:
                which = gathers if x == "g" else choice
                if which is not None:
                    next(run[which], None)
            line[0] = line[0] if tied else None
        for s in range(4):
            if s == 0:
                weave((ha, 0), None, False)
            weave((hb, s), (ha, s), CFG["tied"][0 if (s == 0 and t > 0) else 1])
            weave((ha, s + 1) if s < 3 else None, (hb, s), s < 3 and CFG["tied"][1])
            keep, line[0] = line[0], None
            if s == 1 and t < 3:
                for h in order:
                    lanes_of(t, h)
            if (t, s) == (0, 0):
                late_constants()
            if s == CFG["gs"] and t < 3:
                gate.append(len(ops) - 1)
                spread(t + 1, 1, "G")
                begin(t + 1, 1)
                del gate[:]
            if s == 0 and t > 0:
                outputs(t - 1, 0)
                parents(t - 1)
            if (t, s) == (0, 2) and CFG.get("boom"):
                mm(v("msc0", 0, 8), [(v("Ib"), v("DR0", 0, 8))], False, True)
            if (t, s) == (0, 1):
                roots([(1, 1), (2, 1), (3, 1)], "msc1")
            line[0] = keep if s < 3 else None
        if t == 3:
            for h in order:
                digits(t, h)
                if h == 0:
                    carried(t)
                outputs(t, h)
            break
        digits(t, 1)
        wishes(t, 1)
        equal(1, 1, CFG["eq"][2])
        count(1, 1, True, False)
        root(t + 1, 1)
        digits(t, 0)
        places()
        wishes(t, 0)
        if t > 0:
            carried(t)
        hand_on(t)
        outputs(t, 1)
        equal(0, 1, CFG["eq"][1])
        equal(0, 0, CFG["eq"][0])
        count(0, 1, False, False, range(4))
        count(0, 0, False, False, range(4))
        count(0, 1, False, False, range(4, 8))
        count(0, 0, False, True, range(4, 8))
        grow(t)
        receive(t + 1)
        roots([(t + 1, 0)], "lst0")
        root(t + 1, 0)
        spread(t + 1, 0, CFG["spread0"])
        begin(t + 1, 0)

    n = len(ops)
    succ = [[] for _ in range(n)]
    cnt = [0] * n
    for i, o in enumerate(ops):
        ps = set(o["deps"]) | set(o["tdeps"])
        cnt[i] = len(ps)
        for j in ps:
            succ[j].append(i)
    pri = [0.0] * n
    for i in range(n - 1, -1, -1):
        o = ops[i]
        pri[i] = o["busy"] + o["lat"] + max([pri[k] + HOP for k in succ[i]] + [0.0])
    free = {e: 0.0 for e in "VSPGYR"}
    ready = {e: [] for e in free}
    est = [0.0] * n
    for i in range(n):
        if cnt[i] == 0:
            ready[ops[i]["eng"]].append(i)
    sched = []
    first = [0.0] * n
    left_n = n
    while left_n:
        bt, be = None, None
        for e in free:
            if ready[e]:
                t0 = max(free[e], min(est[i] for i in ready[e]))
                if bt is None or t0 < bt:
                    bt, be = t0, e
        cand = [i for i in ready[be] if est[i] <= bt + LOOK]
        rate = lambda k: (pri[k] + ops[k]["bonus"], -k)
        i = max(cand, key=rate)
        soon = [k for k in ready[be] if rate(k)[0] > rate(i)[0] + CFG["margin"] and est[k] + CFG["tol"] < bt + ops[i]["busy"]]
        if soon:
            due = min(soon, key=lambda k: est[k])
            fit = [k for k in cand if bt + ops[k]["busy"] <= est[due] + CFG["tol"]]
            if fit:
                i = max(fit, key=rate)
            elif est[due] - bt <= CFG["gap"]:
                i = due
        ready[be].remove(i)
        o = ops[i]
        sched.append(i)
        left_n -= 1
        bt = max(bt, est[i])
        end = bt + o["busy"]
        first[i] = bt
        if be != "R":
            free[be] = end
        for k in succ[i]:
            if i in ops[k]["deps"]:
                a = (end + o["lat"] + HOP) if ops[k]["deps"][i] else end
            else:
                a = end
            est[k] = max(est[k], a)
            cnt[k] -= 1
            if cnt[k] == 0:
                ready[ops[k]["eng"]].append(k)

    before = [[] for _ in range(n)]
    after = [[] for _ in range(n)]
    for i, o in enumerate(ops):
        for j in set(o["deps"]) | set(o["tdeps"]):
            w = ops[j]["lat"] + HOP if o["deps"].get(j, False) else 0.0
            before[i].append((j, w))
            after[j].append((i, w))
    tail = [o["lat"] for o in ops]

    def place(order, edges, back):
        at = [0.0] * n
        lines = {e: ([], []) for e in free}
        for i in order:
            d = ops[i]["busy"]
            t0 = max([at[j] + ops[j]["busy"] + w for (j, w) in edges[i]] + [tail[i] if back else 0.0])
            if d > 0:
                lo, hi = lines[ops[i]["eng"]]
                a, b = 0, len(hi)
                while a < b:
                    m = (a + b) // 2
                    if hi[m] <= t0:
                        a = m + 1
                    else:
                        b = m
                while a < len(lo) and lo[a] < t0 + d:
                    t0 = max(t0, hi[a])
                    a += 1
                lo.insert(a, t0)
                hi.insert(a, t0 + d)
            at[i] = t0
        return at

    def span(at):
        return max(at[i] + ops[i]["busy"] + tail[i] for i in range(n))
    best = first
    at = first
    for _ in range(CFG["rounds"]):
        back = place(sorted(range(n), key=lambda i: (-(at[i] + ops[i]["busy"]), -i)), after, True)
        at = place(sorted(range(n), key=lambda i: (-(back[i] + ops[i]["busy"]), i)), before, False)
        if span(at) < span(best):
            best = at
    sched = sorted(range(n), key=lambda i: (best[i], i))
    if "ops" in CFG:
        CFG["ops"].append((ops, before, after, best, pri))
    if "dbg" in CFG and rank == 1:
        CFG["dbg"] += [(ops[i]["tag"], ops[i]["eng"], best[i], best[i] + ops[i]["busy"], i) for i in sched]

    queue = {"V": g.vector, "S": g.scalar, "P": g.tensor, "G": g, "Y": g.sync}
    count_of = {"V": 0, "S": 0, "P": 0, "G": 0}
    known = {e: {} for e in queue}
    done = [None] * n
    clock = [None] * n
    totals = {}
    for i in sched:
        o = ops[i]
        e = o["eng"]
        if e == "R":
            done[i] = (o["sem"][0], o["sem"][1])
            totals[done[i][0]] = done[i][1]
            clock[i] = {done[i][0]: done[i][1]}
            continue
        kn = known[e]
        want = {}
        for j, need in o["deps"].items():
            if need:
                s, val = done[j]
                if kn.get(s, 0) < val and want.get(s, (0, 0))[0] < val:
                    want[s] = (val, j)
        for s in list(want):
            val = want[s][0]
            if any(s2 != s and clock[want[s2][1]].get(s, 0) >= val for s2 in want):
                del want[s]
        for s, (val, j) in want.items():
            queue[e].wait_ge(T.sem[s], val)
            for s2, v2 in clock[j].items():
                if kn.get(s2, 0) < v2:
                    kn[s2] = v2
        ins = o["emit"]()
        if o["sem"] is None:
            count_of[e] += 1
            s, val = "s" + e, count_of[e]
            ins.then_inc(T.sem[s], 1)
        else:
            s, val = o["sem"][0], o["sem"][1]
            if e == "Y":
                ins.then_inc(T.sem[s], 16)
        done[i] = (s, val)
        totals[s] = max(totals.get(s, 0), val)
        c = dict(kn)
        c[s] = val
        clock[i] = c
    kn = known["G"]
    for s in totals:
        if kn.get(s, 0) < totals[s]:
            g.wait_ge(T.sem[s], totals[s])
